import numpy as np
import ml_dtypes


def mxq(x, axis, fmt="e4m3"):
    dtype, down = {"e4m3": (ml_dtypes.float8_e4m3fn, 7), "e5m2": (ml_dtypes.float8_e5m2, 14)}[fmt]
    v = np.moveaxis(np.asarray(x, np.float32).astype(ml_dtypes.bfloat16).astype(np.float64), axis, -1)
    blocks = v.reshape(v.shape[:-1] + (-1, 32))
    amax = np.abs(blocks).max(-1, keepdims=True)
    byte = np.maximum(np.where(amax > 0, np.frexp(amax)[1] - 1 + 127, 0) - down, 1)
    scale = np.exp2(byte - 127.0)
    codes = (blocks / scale).astype(np.float32).astype(dtype).astype(np.float64)
    return np.moveaxis((codes * scale).reshape(v.shape), -1, axis)


WIDE = False


def mx_kscale(k):
    if not WIDE:
        return np.ones(k)
    levels = np.array([24, -24, 12, -12, 0])
    if k % 512:
        return np.exp2(np.random.permutation(np.resize(levels, k // 32))).repeat(32)
    a = np.empty((k // 512, 16))
    for p in range(k // 512):
        a[p, :8] = np.random.permutation(np.resize(levels, 8))
        for g in range(8):
            far = levels[np.abs(levels - a[p, g]) >= 10]
            a[p, g + 8] = far[np.random.randint(len(far))]
    return np.exp2(a.ravel()).repeat(32)


def f64(x):
    return np.asarray(x).astype(np.float64)


def striped(idx):
    return np.tile(idx.reshape(-1, 16).T, (8, 1)).astype(np.uint16)


def unstriped(offs):
    return offs[:16].T.reshape(-1).astype(np.int64)


E2M1 = np.array([0.0, 0.5, 1.0, 1.5, 2.0, 3.0, 4.0, 6.0, -0.0, -0.5, -1.0, -1.5, -2.0, -3.0, -4.0, -6.0])


def pack_weight(w, fmt):
    k, n = w.shape
    w = f64(np.asarray(w, np.float32).astype(ml_dtypes.bfloat16)).reshape(k // 32, 32, n)
    amax = np.abs(w).max(1)
    if fmt == "e4m3":
        byte = np.frexp(amax)[1] - 1 + 127 - 7
    else:
        mant, ex = np.frexp(amax / 6.0)
        byte = np.where(mant > 0.5, ex, ex - 1) + 127
    byte = np.clip(np.where(amax > 0, byte, 1), 1, 254)
    scaled = (w * np.exp2(127.0 - byte)[:, None, :]).reshape(k, n).astype(np.float32)
    by_word = np.ascontiguousarray(scaled.reshape(k // 512, 128, 4, n).transpose(0, 1, 3, 2))
    if fmt == "e4m3":
        words = by_word.astype(ml_dtypes.float8_e4m3fn).view(np.uint8)
    else:
        c = by_word.astype(ml_dtypes.float4_e2m1fn).view(np.uint8) & 0xF
        words = (c[..., 0::2] | (c[..., 1::2] << 4)).reshape(k // 512, 128, 2 * n)
    return np.ascontiguousarray(words), np.ascontiguousarray(byte.astype(np.uint8).reshape(k // 512, 16, n))


def unpack_weight(words, scales, fmt):
    g, _, n = scales.shape
    words = np.ascontiguousarray(words).reshape(g, 128, n, -1)
    if fmt == "e4m3":
        vals = words.view(ml_dtypes.float8_e4m3fn).astype(np.float64)
    else:
        nib = np.empty((g, 128, n, 4), np.uint8)
        nib[..., 0::2] = words & 0xF
        nib[..., 1::2] = words >> 4
        vals = E2M1[nib]
    vals = vals * np.repeat(np.exp2(scales.astype(np.float64) - 127.0), 8, axis=1)[..., None]
    return vals.transpose(0, 1, 3, 2).reshape(g * 512, n)


def sigm(f):
    return 1.0 / (1.0 + np.exp(-np.maximum(f, -700.0)))


K, L, R, N, T, J = 512, 512, 1024, 256, 1024, 512


def setup_inputs():
    n = np.random.standard_normal
    s = mx_kscale(K)[:, None]
    s2 = mx_kscale(L)[:, None]
    u = mx_kscale(R)[:, None]
    en = n((R, N)) / np.sqrt(R) / u
    p_tab = pack_weight(n((K, T)) * s, "e4m3")
    p_tab2 = pack_weight(n((L, T)) * s2, "e4m3")
    p_wa = pack_weight(n((K, R)) / np.sqrt(K) / s * u.T, "e4m3")
    p_wb = pack_weight(n((L, R)) / np.sqrt(L) / s2, "e2m1")
    p_en8 = pack_weight(en[:512], "e4m3")
    p_en4 = pack_weight(en[512:], "e2m1")
    return {
        "tab_words": p_tab[0],
        "tab_scales": p_tab[1],
        "tab2_words": p_tab2[0],
        "tab2_scales": p_tab2[1],
        "wa_words": p_wa[0],
        "wa_scales": p_wa[1],
        "wb_words": p_wb[0],
        "wb_scales": p_wb[1],
        "en8_words": p_en8[0],
        "en8_scales": p_en8[1],
        "en4_words": p_en4[0],
        "en4_scales": p_en4[1],
        "offs": striped(np.random.permutation(T)[:J]),
        "offs2": striped(np.random.permutation(T)[:J]),
    }


def reference(tab_words, tab_scales, tab2_words, tab2_scales, wa_words, wa_scales, wb_words, wb_scales, en8_words, en8_scales, en4_words, en4_scales, offs, offs2):
    idx = unstriped(offs)
    idx2 = unstriped(offs2)
    tab_ = unpack_weight(tab_words, tab_scales, "e4m3")[:, idx]
    tab2_ = unpack_weight(tab2_words, tab2_scales, "e4m3")[:, idx2]
    wa_ = unpack_weight(wa_words, wa_scales, "e4m3")
    wb_ = unpack_weight(wb_words, wb_scales, "e2m1")
    ha = wa_.T @ tab_
    hb = wb_.T @ tab2_
    h = ha * sigm(hb)
    h_ = mxq(h, 0, "e4m3")
    en8_ = unpack_weight(en8_words, en8_scales, "e4m3")
    en4_ = unpack_weight(en4_words, en4_scales, "e2m1")
    y = en8_.T @ h_[:512] + en4_.T @ h_[512:]
    return y

@@ -1,0 +1,212 @@
+from contextlib import ExitStack
+
+import concourse.mybir as mybir
+from concourse.masks import make_identity
+
+K, L, R, N, T, J = 512, 512, 1024, 256, 1024, 512
+FLOPS = 2 * J * (K * R + L * R + R * N)
+
+F32 = mybir.dt.float32
+BF16 = mybir.dt.bfloat16
+I32 = mybir.dt.int32
+U32 = mybir.dt.uint32
+U16 = mybir.dt.uint16
+U8 = mybir.dt.uint8
+FP8X4 = mybir.dt.float8_e4m3fn_x4
+FP4X4 = mybir.dt.float4_e2m1fn_x4
+SIGMOID = mybir.ActivationFunctionType.Sigmoid
+MULT = mybir.AluOpType.mult
+
+P = 128
+PASS = 512
+CHUNKS = J // P
+HALVES = R // PASS
+LIST_COLS = P // 16
+WA_ROW, TAB_ROW, EN8_ROW = 4, 8, 12
+
+
+def load_scales(queue, plane, scales, first_row):
+    rows = scales[0].bitcast(I32).rearrange("(q r) w -> r q w", r=4)
+    for r in range(4):
+        queue.dma_start(out=plane[first_row + r : P : 32, :], in_=rows[r])
+
+
+def words8(w):
+    return w[0].rearrange("p n t -> p (n t)").bitcast(I32)
+
+
+def tile_list_kg_gate_mix_none_kernel(tc, tab_words, tab_scales, tab2_words, tab2_scales, wa_words, wa_scales, wb_words, wb_scales, en8_words, en8_scales, en4_words, en4_scales, offs, offs2, out):
+    nc = tc.nc
+    with ExitStack() as ctx:
+        keep = ctx.enter_context(tc.tile_pool(name="keep", bufs=1))
+        acc_pool = ctx.enter_context(tc.psum_pool(name="acc", bufs=4))
+        xt_pool = ctx.enter_context(tc.psum_pool(name="xt", bufs=2))
+        y_pool = ctx.enter_context(tc.psum_pool(name="y", bufs=2))
+
+        list1 = keep.tile([P, J // 16], U16, name="list1")
+        list2 = keep.tile([P, J // 16], U16, name="list2")
+        tab_w = keep.tile([P, T], I32, name="tab_w", align_bytes=64)
+        tab2_w = keep.tile([P, T], I32, name="tab2_w", align_bytes=64)
+        tab_s = keep.tile([P, T // 4], I32, name="tab_s", align_bytes=64)
+        tab2_s = keep.tile([P, T // 4], I32, name="tab2_s", align_bytes=64)
+        wa_w = keep.tile([P, R], I32, name="wa_w", align_bytes=64)
+        wb_w = keep.tile([P, R // 2], I32, name="wb_w", align_bytes=64)
+        en8_w = keep.tile([P, N], I32, name="en8_w", align_bytes=64)
+        en4_w = keep.tile([P, N // 2], I32, name="en4_w", align_bytes=64)
+        wb_s = keep.tile([P, R // 4], I32, name="wb_s", align_bytes=64)
+        wa_s = keep.tile([P, R // 4], I32, name="wa_s", align_bytes=64)
+        en_s = keep.tile([P, N // 4], I32, name="en_s", align_bytes=64)
+        ident = keep.tile([P, P], F32, name="ident", align_bytes=64)
+        warm = keep.tile([P, 8], F32, name="warm")
+
+        nc.vector.memset(tab2_s[:], 0)
+        nc.vector.memset(wb_s[:], 0)
+        nc.vector.memset(tab_s[:], 0)
+        nc.vector.memset(wa_s[:], 0)
+        nc.vector.memset(en_s[:], 0)
+        nc.vector.memset(warm[:, 0:1], 0.0)
+
+        make_identity(nc, ident[:])
+
+        nc.sync.dma_start(list2[:], offs2)
+        nc.sync.dma_start(out=tab2_w[:], in_=words8(tab2_words))
+        load_scales(nc.scalar, tab2_s, tab2_scales, 0)
+        nc.sync.dma_start(list1[:], offs)
+        nc.sync.dma_start(out=wb_w[:], in_=wb_words[0].bitcast(I32))
+        nc.scalar.activation(out=warm[:, 1:2], in_=warm[:, 0:1], func=SIGMOID)
+        load_scales(nc.sync, wb_s, wb_scales, 0)
+        nc.sync.dma_start(out=tab_w[:], in_=words8(tab_words))
+        load_scales(nc.sync, tab_s, tab_scales, TAB_ROW)
+        nc.sync.dma_start(out=wa_w[:], in_=words8(wa_words))
+        load_scales(nc.sync, wa_s, wa_scales, WA_ROW)
+        nc.sync.dma_start(out=en8_w[:], in_=words8(en8_words))
+        nc.sync.dma_start(out=en4_w[:], in_=en4_words[0].bitcast(I32))
+        load_scales(nc.sync, en_s, en8_scales, EN8_ROW)
+        load_scales(nc.sync, en_s, en4_scales, 0)
+
+        v_w = keep.tile([P, J], U32, name="v_w", align_bytes=64)
+        v_s = keep.tile([P, J], U8, name="v_s", align_bytes=64)
+        v2_w = keep.tile([P, J], U32, name="v2_w", align_bytes=64)
+        v2_s = keep.tile([P, J], U8, name="v2_s", align_bytes=64)
+        gate = keep.tile([P, CHUNKS, HALVES, PASS], F32, name="gate", align_bytes=64)
+        h = keep.tile([P, CHUNKS, HALVES, PASS], BF16, name="h", align_bytes=64)
+        ht = keep.tile([P, CHUNKS, HALVES, PASS], BF16, name="ht", align_bytes=64)
+        hq_w = keep.tile([P, CHUNKS, HALVES, P], U32, name="hq_w", align_bytes=64)
+        hq_s = keep.tile([P, CHUNKS, HALVES, P], U8, name="hq_s", align_bytes=64)
+        y_sb = keep.tile([P, CHUNKS, N // P, P], F32, name="y_sb", align_bytes=64)
+
+        def gather(c, dst_w, dst_s, src_w, src_s, lst):
+            cols = slice(c * P, (c + 1) * P)
+            piece = lst[:, c * LIST_COLS : (c + 1) * LIST_COLS]
+            nc.vector.tensor_copy(dst_s[:, cols], src_s[:].bitcast(U8).indirect(piece))
+            nc.vector.tensor_copy(dst_w[:, cols], src_w[:].bitcast(U32).indirect(piece))
+
+        def by_pair(bank):
+            return bank[:].rearrange("p (m u e) -> p u m e", u=2, e=2)
+
+        def gate_stage(c):
+            cols = slice(c * P, (c + 1) * P)
+            for b in range(HALVES):
+                hb = acc_pool.tile([P, PASS], F32, name="acc")
+                nc.tensor.matmul_mx(
+                    out=hb[:],
+                    lhsT=v2_w[:, cols].bitcast(FP8X4),
+                    lhsT_scale=v2_s[:, cols],
+                    rhs=wb_w[:].bitcast(U8)[:, 2 * b * PASS : 2 * (b + 1) * PASS].bitcast(FP4X4),
+                    rhs_scale=wb_s[:].bitcast(U8)[:, b * PASS : (b + 1) * PASS],
+                    start=True,
+                    stop=True,
+                )
+                nc.scalar.activation(out=gate[:, c, b, :].rearrange("p (u m e) -> p u m e", u=2, e=2), in_=by_pair(hb), func=SIGMOID)
+
+        def product_stage(c, b):
+            cols = slice(c * P, (c + 1) * P)
+            ha = acc_pool.tile([P, PASS], F32, name="acc")
+            nc.tensor.matmul_mx(
+                out=ha[:],
+                lhsT=v_w[:, cols].bitcast(FP8X4),
+                lhsT_scale=v_s[TAB_ROW:P, cols],
+                rhs=wa_w[:, b * PASS : (b + 1) * PASS].bitcast(FP8X4),
+                rhs_scale=wa_s[WA_ROW:P, :].bitcast(U8)[:, b * PASS : (b + 1) * PASS],
+                start=True,
+                stop=True,
+            )
+            nc.vector.tensor_tensor(
+                out=h[:, c, b, :].rearrange("p (u m e) -> p u m e", u=2, e=2),
+                in0=by_pair(ha),
+                in1=gate[:, c, b, :].rearrange("p (u m e) -> p u m e", u=2, e=2),
+                op=MULT,
+            )
+
+        def turn_stage(c, b0, b1):
+            nb = b1 - b0
+            xt = xt_pool.tile([P, HALVES, 2, P], F32, name="xt")
+            for b in range(b0, b1):
+                pairs = h[:, c, b, :].bitcast(F32)
+                for u in range(2):
+                    nc.tensor.transpose(xt[:, b, u, :], pairs[:, u * P : (u + 1) * P], ident[:])
+            nc.scalar.copy(
+                out=ht[:, c, b0:b1, :].rearrange("p b w -> p (b w)").bitcast(F32).rearrange("p (b j u) -> p b j u", b=nb, u=2),
+                in_=xt[:, b0:b1, :, :].rearrange("p b u j -> p b j u"),
+            )
+
+        def quant_stage(c, b0, b1):
+            nc.vector.quantize_mx(
+                out=hq_w[:, c, b0:b1, :].rearrange("p b w -> p (b w)").bitcast(FP8X4),
+                scales=hq_s[:, c, b0:b1, :].rearrange("p b w -> p (b w)"),
+                in_=ht[:, c, b0:b1, :].rearrange("p b w -> p (b w)"),
+            )
+
+        def score_stage(c):
+            banks = [y_pool.tile([P, P], F32, name="y") for nt in range(N // P)]
+            for nt in range(N // P):
+                nc.tensor.matmul_mx(
+                    out=banks[nt][:],
+                    lhsT=en8_w[:, nt * P : (nt + 1) * P].bitcast(FP8X4),
+                    lhsT_scale=en_s[EN8_ROW:P, :].bitcast(U8)[:, nt * P : (nt + 1) * P],
+                    rhs=hq_w[:, c, 0, :].bitcast(FP8X4),
+                    rhs_scale=hq_s[:, c, 0, :],
+                    start=True,
+                    stop=False,
+                )
+            for nt in range(N // P):
+                nc.tensor.matmul_mx(
+                    out=banks[nt][:],
+                    lhsT=en4_w[:].bitcast(U8)[:, 2 * nt * P : 2 * (nt + 1) * P].bitcast(FP4X4),
+                    lhsT_scale=en_s[:].bitcast(U8)[:, nt * P : (nt + 1) * P],
+                    rhs=hq_w[:, c, 1, :].bitcast(FP8X4),
+                    rhs_scale=hq_s[:, c, 1, :],
+                    start=False,
+                    stop=True,
+                )
+            cols = slice(c * P, (c + 1) * P)
+            if c < CHUNKS - 1:
+                for nt in range(N // P):
+                    nc.scalar.copy(out=y_sb[:, c, nt, :], in_=banks[nt][:])
+                nc.sync.dma_start(out=out.rearrange("(a p) j -> p a j", p=P)[:, :, cols], in_=y_sb[:, c, :, :])
+            else:
+                nc.vector.tensor_copy(out=y_sb[:, c, 0, :], in_=banks[0][:])
+                nc.sync.dma_start(out=out[0:P, cols], in_=y_sb[:, c, 0, :])
+                nc.scalar.copy(out=y_sb[:, c, 1, :], in_=banks[1][:])
+                nc.scalar.dma_start(out=out[P : 2 * P, cols], in_=y_sb[:, c, 1, :])
+
+        for c in range(CHUNKS):
+            gather(c, v2_w, v2_s, tab2_w, tab2_s, list2)
+            gate_stage(c)
+        for c in range(CHUNKS):
+            gather(c, v_w, v_s, tab_w, tab_s, list1)
+        last = CHUNKS - 1
+        for c in range(CHUNKS):
+            product_stage(c, 0)
+            if c == last:
+                turn_stage(c, 0, 1)
+            if c > 0:
+                quant_stage(c - 1, 0, 2)
+                score_stage(c - 1)
+            product_stage(c, 1)
+            if c < last:
+                turn_stage(c, 0, 2)
+        turn_stage(last, 1, 2)
+        quant_stage(last, 0, 1)
+        quant_stage(last, 1, 2)
+        score_stage(last)

@@ -26,9 +26,9 @@ WA_ROW, TAB_ROW, EN8_ROW = 4, 8, 12
 
 
 def load_scales(queue, plane, scales, first_row):
-    rows = scales[0].bitcast(I32).rearrange("(q r) w -> r q w", r=4)
-    for r in range(4):
-        queue.dma_start(out=plane[first_row + r : P : 32, :], in_=rows[r])
+    rows = scales[0].bitcast(I32)
+    for q in range(4):
+        queue.dma_start(out=plane[32 * q + first_row : 32 * q + first_row + 4, :], in_=rows[4 * q : 4 * q + 4, :])
 
 
 def words8(w):
@@ -39,20 +39,17 @@ def tile_list_kg_gate_mix_none_kernel(tc, tab_words, tab_scales, tab2_words, tab
     nc = tc.nc
     with ExitStack() as ctx:
         keep = ctx.enter_context(tc.tile_pool(name="keep", bufs=1))
-        acc_pool = ctx.enter_context(tc.psum_pool(name="acc", bufs=4))
-        xt_pool = ctx.enter_context(tc.psum_pool(name="xt", bufs=2))
-        y_pool = ctx.enter_context(tc.psum_pool(name="y", bufs=2))
+        psum = ctx.enter_context(tc.psum_pool(name="psum", bufs=8))
+        reuse = ctx.enter_context(tc.tile_pool(name="reuse", bufs=1))
 
         list1 = keep.tile([P, J // 16], U16, name="list1")
         list2 = keep.tile([P, J // 16], U16, name="list2")
         tab_w = keep.tile([P, T], I32, name="tab_w", align_bytes=64)
-        tab2_w = keep.tile([P, T], I32, name="tab2_w", align_bytes=64)
+        tab2_w = reuse.tile([P, T], I32, name="words", align_bytes=64)
         tab_s = keep.tile([P, T // 4], I32, name="tab_s", align_bytes=64)
         tab2_s = keep.tile([P, T // 4], I32, name="tab2_s", align_bytes=64)
         wa_w = keep.tile([P, R], I32, name="wa_w", align_bytes=64)
         wb_w = keep.tile([P, R // 2], I32, name="wb_w", align_bytes=64)
-        en8_w = keep.tile([P, N], I32, name="en8_w", align_bytes=64)
-        en4_w = keep.tile([P, N // 2], I32, name="en4_w", align_bytes=64)
         wb_s = keep.tile([P, R // 4], I32, name="wb_s", align_bytes=64)
         wa_s = keep.tile([P, R // 4], I32, name="wa_s", align_bytes=64)
         en_s = keep.tile([P, N // 4], I32, name="en_s", align_bytes=64)
@@ -66,21 +63,19 @@ def tile_list_kg_gate_mix_none_kernel(tc, tab_words, tab_scales, tab2_words, tab
         nc.vector.memset(en_s[:], 0)
         nc.vector.memset(warm[:, 0:1], 0.0)
 
+        nc.gpsimd.dma_start(out=tab_w[:], in_=words8(tab_words))
+        nc.gpsimd.dma_start(out=wa_w[:], in_=words8(wa_words))
         make_identity(nc, ident[:])
 
         nc.sync.dma_start(list2[:], offs2)
         nc.sync.dma_start(out=tab2_w[:], in_=words8(tab2_words))
-        load_scales(nc.scalar, tab2_s, tab2_scales, 0)
         nc.sync.dma_start(list1[:], offs)
         nc.sync.dma_start(out=wb_w[:], in_=wb_words[0].bitcast(I32))
+        load_scales(nc.scalar, tab2_s, tab2_scales, 0)
         nc.scalar.activation(out=warm[:, 1:2], in_=warm[:, 0:1], func=SIGMOID)
         load_scales(nc.sync, wb_s, wb_scales, 0)
-        nc.sync.dma_start(out=tab_w[:], in_=words8(tab_words))
         load_scales(nc.sync, tab_s, tab_scales, TAB_ROW)
-        nc.sync.dma_start(out=wa_w[:], in_=words8(wa_words))
         load_scales(nc.sync, wa_s, wa_scales, WA_ROW)
-        nc.sync.dma_start(out=en8_w[:], in_=words8(en8_words))
-        nc.sync.dma_start(out=en4_w[:], in_=en4_words[0].bitcast(I32))
         load_scales(nc.sync, en_s, en8_scales, EN8_ROW)
         load_scales(nc.sync, en_s, en4_scales, 0)
 
@@ -95,11 +90,8 @@ def tile_list_kg_gate_mix_none_kernel(tc, tab_words, tab_scales, tab2_words, tab
         hq_s = keep.tile([P, CHUNKS, HALVES, P], U8, name="hq_s", align_bytes=64)
         y_sb = keep.tile([P, CHUNKS, N // P, P], F32, name="y_sb", align_bytes=64)
 
-        def gather(c, dst_w, dst_s, src_w, src_s, lst):
-            cols = slice(c * P, (c + 1) * P)
-            piece = lst[:, c * LIST_COLS : (c + 1) * LIST_COLS]
-            nc.vector.tensor_copy(dst_s[:, cols], src_s[:].bitcast(U8).indirect(piece))
-            nc.vector.tensor_copy(dst_w[:, cols], src_w[:].bitcast(U32).indirect(piece))
+        def gather(dst, window, lst, c0, c1):
+            nc.vector.tensor_copy(dst[:, c0 * P : c1 * P], window.indirect(lst[:, c0 * LIST_COLS : c1 * LIST_COLS]))
 
         def by_pair(bank):
             return bank[:].rearrange("p (m u e) -> p u m e", u=2, e=2)
@@ -107,7 +99,7 @@ def tile_list_kg_gate_mix_none_kernel(tc, tab_words, tab_scales, tab2_words, tab
         def gate_stage(c):
             cols = slice(c * P, (c + 1) * P)
             for b in range(HALVES):
-                hb = acc_pool.tile([P, PASS], F32, name="acc")
+                hb = psum.tile([P, PASS], F32, name="bank")
                 nc.tensor.matmul_mx(
                     out=hb[:],
                     lhsT=v2_w[:, cols].bitcast(FP8X4),
@@ -119,9 +111,9 @@ def tile_list_kg_gate_mix_none_kernel(tc, tab_words, tab_scales, tab2_words, tab
                 )
                 nc.scalar.activation(out=gate[:, c, b, :].rearrange("p (u m e) -> p u m e", u=2, e=2), in_=by_pair(hb), func=SIGMOID)
 
-        def product_stage(c, b):
+        def project_stage(c, b):
             cols = slice(c * P, (c + 1) * P)
-            ha = acc_pool.tile([P, PASS], F32, name="acc")
+            ha = psum.tile([P, PASS], F32, name="bank")
             nc.tensor.matmul_mx(
                 out=ha[:],
                 lhsT=v_w[:, cols].bitcast(FP8X4),
@@ -131,6 +123,9 @@ def tile_list_kg_gate_mix_none_kernel(tc, tab_words, tab_scales, tab2_words, tab
                 start=True,
                 stop=True,
             )
+            return ha
+
+        def product_stage(c, b, ha):
             nc.vector.tensor_tensor(
                 out=h[:, c, b, :].rearrange("p (u m e) -> p u m e", u=2, e=2),
                 in0=by_pair(ha),
@@ -140,7 +135,7 @@ def tile_list_kg_gate_mix_none_kernel(tc, tab_words, tab_scales, tab2_words, tab
 
         def turn_stage(c, b0, b1):
             nb = b1 - b0
-            xt = xt_pool.tile([P, HALVES, 2, P], F32, name="xt")
+            xt = psum.tile([P, HALVES, 2, P], F32, name="bank")
             for b in range(b0, b1):
                 pairs = h[:, c, b, :].bitcast(F32)
                 for u in range(2):
@@ -158,7 +153,7 @@ def tile_list_kg_gate_mix_none_kernel(tc, tab_words, tab_scales, tab2_words, tab
             )
 
         def score_stage(c):
-            banks = [y_pool.tile([P, P], F32, name="y") for nt in range(N // P)]
+            banks = [psum.tile([P, P], F32, name="bank") for nt in range(N // P)]
             for nt in range(N // P):
                 nc.tensor.matmul_mx(
                     out=banks[nt][:],
@@ -172,7 +167,7 @@ def tile_list_kg_gate_mix_none_kernel(tc, tab_words, tab_scales, tab2_words, tab
             for nt in range(N // P):
                 nc.tensor.matmul_mx(
                     out=banks[nt][:],
-                    lhsT=en4_w[:].bitcast(U8)[:, 2 * nt * P : 2 * (nt + 1) * P].bitcast(FP4X4),
+                    lhsT=en4_w.bitcast(U8)[:, 2 * nt * P : 2 * (nt + 1) * P].bitcast(FP4X4),
                     lhsT_scale=en_s[:].bitcast(U8)[:, nt * P : (nt + 1) * P],
                     rhs=hq_w[:, c, 1, :].bitcast(FP8X4),
                     rhs_scale=hq_s[:, c, 1, :],
@@ -190,23 +185,35 @@ def tile_list_kg_gate_mix_none_kernel(tc, tab_words, tab_scales, tab2_words, tab
                 nc.scalar.copy(out=y_sb[:, c, 1, :], in_=banks[1][:])
                 nc.scalar.dma_start(out=out[P : 2 * P, cols], in_=y_sb[:, c, 1, :])
 
+        for c in range(0, CHUNKS, 2):
+            gather(v2_w, tab2_w[:].bitcast(U32), list2, c, c + 2)
+            gather(v2_s, tab2_s[:].bitcast(U8), list2, c, c + 2)
+        en_w = reuse.tile([P, N + N // 2], I32, name="words", align_bytes=64)
+        en8_w = en_w[:, 0:N]
+        en4_w = en_w[:, N : N + N // 2]
+        nc.sync.dma_start(out=en8_w, in_=words8(en8_words))
+        nc.sync.dma_start(out=en4_w, in_=en4_words[0].bitcast(I32))
         for c in range(CHUNKS):
-            gather(c, v2_w, v2_s, tab2_w, tab2_s, list2)
             gate_stage(c)
+        gather(v_w, tab_w[:].bitcast(U32), list1, 0, 4)
         for c in range(CHUNKS):
-            gather(c, v_w, v_s, tab_w, tab_s, list1)
+            gather(v_s, tab_s[:].bitcast(U8), list1, c, c + 1)
         last = CHUNKS - 1
-        for c in range(CHUNKS):
-            product_stage(c, 0)
+        units = [(c, b) for c in range(CHUNKS) for b in range(HALVES)]
+        sums = {}
+        for c, b in units[:4]:
+            sums[c, b] = project_stage(c, b)
+        for i, (c, b) in enumerate(units):
+            product_stage(c, b, sums[c, b])
+            if i + 4 < len(units):
+                sums[units[i + 4]] = project_stage(*units[i + 4])
             if c == last:
-                turn_stage(c, 0, 1)
-            if c > 0:
+                turn_stage(c, b, b + 1)
+            elif b == 1:
+                turn_stage(c, 0, 2)
+            if b == 1 and c > 0:
                 quant_stage(c - 1, 0, 2)
                 score_stage(c - 1)
-            product_stage(c, 1)
-            if c < last:
-                turn_stage(c, 0, 2)
-        turn_stage(last, 1, 2)
         quant_stage(last, 0, 1)
         quant_stage(last, 1, 2)
         score_stage(last)

@@ -40,44 +40,48 @@ def tile_list_kg_gate_mix_none_kernel(tc, tab_words, tab_scales, tab2_words, tab
     with ExitStack() as ctx:
         keep = ctx.enter_context(tc.tile_pool(name="keep", bufs=1))
         psum = ctx.enter_context(tc.psum_pool(name="psum", bufs=8))
-        reuse = ctx.enter_context(tc.tile_pool(name="reuse", bufs=1))
 
         list1 = keep.tile([P, J // 16], U16, name="list1")
         list2 = keep.tile([P, J // 16], U16, name="list2")
         tab_w = keep.tile([P, T], I32, name="tab_w", align_bytes=64)
-        tab2_w = reuse.tile([P, T], I32, name="words", align_bytes=64)
+        tab2_w = keep.tile([P, T], I32, name="tab2_w", align_bytes=64)
         tab_s = keep.tile([P, T // 4], I32, name="tab_s", align_bytes=64)
         tab2_s = keep.tile([P, T // 4], I32, name="tab2_s", align_bytes=64)
         wa_w = keep.tile([P, R], I32, name="wa_w", align_bytes=64)
         wb_w = keep.tile([P, R // 2], I32, name="wb_w", align_bytes=64)
         wb_s = keep.tile([P, R // 4], I32, name="wb_s", align_bytes=64)
         wa_s = keep.tile([P, R // 4], I32, name="wa_s", align_bytes=64)
-        en_s = keep.tile([P, N // 4], I32, name="en_s", align_bytes=64)
+        en8_s = keep.tile([P, N // 4], I32, name="en8_s", align_bytes=64)
+        en4_s = keep.tile([P, N // 4], I32, name="en4_s", align_bytes=64)
+        en8_w = keep.tile([P, N], I32, name="en8_w", align_bytes=64)
+        en4_w = keep.tile([P, N // 2], I32, name="en4_w", align_bytes=64)
         ident = keep.tile([P, P], F32, name="ident", align_bytes=64)
         warm = keep.tile([P, 8], F32, name="warm")
 
         nc.vector.memset(tab2_s[:], 0)
         nc.vector.memset(wb_s[:], 0)
         nc.vector.memset(tab_s[:], 0)
-        nc.vector.memset(wa_s[:], 0)
-        nc.vector.memset(en_s[:], 0)
         nc.vector.memset(warm[:, 0:1], 0.0)
-
-        nc.gpsimd.dma_start(out=tab_w[:], in_=words8(tab_words))
-        nc.gpsimd.dma_start(out=wa_w[:], in_=words8(wa_words))
+        nc.vector.memset(en8_s[:], 0)
+        nc.vector.memset(en4_s[:], 0)
+        nc.gpsimd.memset(wa_s[:], 0)
+        load_scales(nc.gpsimd, wa_s, wa_scales, WA_ROW)
         make_identity(nc, ident[:])
+        load_scales(nc.gpsimd, en4_s, en4_scales, 0)
+        nc.scalar.activation(out=warm[:, 1:2], in_=warm[:, 0:1], func=SIGMOID)
 
         nc.sync.dma_start(list2[:], offs2)
+        load_scales(nc.sync, tab2_s, tab2_scales, 0)
         nc.sync.dma_start(out=tab2_w[:], in_=words8(tab2_words))
-        nc.sync.dma_start(list1[:], offs)
         nc.sync.dma_start(out=wb_w[:], in_=wb_words[0].bitcast(I32))
-        load_scales(nc.scalar, tab2_s, tab2_scales, 0)
-        nc.scalar.activation(out=warm[:, 1:2], in_=warm[:, 0:1], func=SIGMOID)
         load_scales(nc.sync, wb_s, wb_scales, 0)
+        nc.sync.dma_start(list1[:], offs)
+        nc.sync.dma_start(out=tab_w[:], in_=words8(tab_words))
+        nc.sync.dma_start(out=wa_w[:], in_=words8(wa_words))
         load_scales(nc.sync, tab_s, tab_scales, TAB_ROW)
-        load_scales(nc.sync, wa_s, wa_scales, WA_ROW)
-        load_scales(nc.sync, en_s, en8_scales, EN8_ROW)
-        load_scales(nc.sync, en_s, en4_scales, 0)
+        load_scales(nc.sync, en8_s, en8_scales, EN8_ROW)
+        nc.sync.dma_start(out=en8_w[:], in_=words8(en8_words))
+        nc.sync.dma_start(out=en4_w[:], in_=en4_words[0].bitcast(I32))
 
         v_w = keep.tile([P, J], U32, name="v_w", align_bytes=64)
         v_s = keep.tile([P, J], U8, name="v_s", align_bytes=64)
@@ -152,47 +156,37 @@ def tile_list_kg_gate_mix_none_kernel(tc, tab_words, tab_scales, tab2_words, tab
                 in_=ht[:, c, b0:b1, :].rearrange("p b w -> p (b w)"),
             )
 
+        def score_pass(c, nt, b, dst):
+            if b == 0:
+                words = en8_w[:, nt * P : (nt + 1) * P].bitcast(FP8X4)
+                scales = en8_s[EN8_ROW:P, :].bitcast(U8)[:, nt * P : (nt + 1) * P]
+            else:
+                words = en4_w[:].bitcast(U8)[:, 2 * nt * P : 2 * (nt + 1) * P].bitcast(FP4X4)
+                scales = en4_s[:].bitcast(U8)[:, nt * P : (nt + 1) * P]
+            nc.tensor.matmul_mx(out=dst, lhsT=words, lhsT_scale=scales, rhs=hq_w[:, c, b, :].bitcast(FP8X4), rhs_scale=hq_s[:, c, b, :], start=(b == 0), stop=(b == 1))
+
         def score_stage(c):
-            banks = [psum.tile([P, P], F32, name="bank") for nt in range(N // P)]
-            for nt in range(N // P):
-                nc.tensor.matmul_mx(
-                    out=banks[nt][:],
-                    lhsT=en8_w[:, nt * P : (nt + 1) * P].bitcast(FP8X4),
-                    lhsT_scale=en_s[EN8_ROW:P, :].bitcast(U8)[:, nt * P : (nt + 1) * P],
-                    rhs=hq_w[:, c, 0, :].bitcast(FP8X4),
-                    rhs_scale=hq_s[:, c, 0, :],
-                    start=True,
-                    stop=False,
-                )
-            for nt in range(N // P):
-                nc.tensor.matmul_mx(
-                    out=banks[nt][:],
-                    lhsT=en4_w.bitcast(U8)[:, 2 * nt * P : 2 * (nt + 1) * P].bitcast(FP4X4),
-                    lhsT_scale=en_s[:].bitcast(U8)[:, nt * P : (nt + 1) * P],
-                    rhs=hq_w[:, c, 1, :].bitcast(FP8X4),
-                    rhs_scale=hq_s[:, c, 1, :],
-                    start=False,
-                    stop=True,
-                )
             cols = slice(c * P, (c + 1) * P)
             if c < CHUNKS - 1:
+                bank = psum.tile([P, N // P, P], F32, name="bank")
                 for nt in range(N // P):
-                    nc.scalar.copy(out=y_sb[:, c, nt, :], in_=banks[nt][:])
+                    for b in range(HALVES):
+                        score_pass(c, nt, b, bank[:, nt, :])
+                nc.scalar.copy(out=y_sb[:, c, :, :], in_=bank[:])
                 nc.sync.dma_start(out=out.rearrange("(a p) j -> p a j", p=P)[:, :, cols], in_=y_sb[:, c, :, :])
             else:
+                banks = [psum.tile([P, P], F32, name="bank") for nt in range(N // P)]
+                for b in range(HALVES):
+                    for nt in range(N // P):
+                        score_pass(c, nt, b, banks[nt][:])
                 nc.vector.tensor_copy(out=y_sb[:, c, 0, :], in_=banks[0][:])
                 nc.sync.dma_start(out=out[0:P, cols], in_=y_sb[:, c, 0, :])
                 nc.scalar.copy(out=y_sb[:, c, 1, :], in_=banks[1][:])
                 nc.scalar.dma_start(out=out[P : 2 * P, cols], in_=y_sb[:, c, 1, :])
 
-        for c in range(0, CHUNKS, 2):
-            gather(v2_w, tab2_w[:].bitcast(U32), list2, c, c + 2)
-            gather(v2_s, tab2_s[:].bitcast(U8), list2, c, c + 2)
-        en_w = reuse.tile([P, N + N // 2], I32, name="words", align_bytes=64)
-        en8_w = en_w[:, 0:N]
-        en4_w = en_w[:, N : N + N // 2]
-        nc.sync.dma_start(out=en8_w, in_=words8(en8_words))
-        nc.sync.dma_start(out=en4_w, in_=en4_words[0].bitcast(I32))
+        gather(v2_s, tab2_s[:].bitcast(U8), list2, 0, CHUNKS)
+        for c in range(CHUNKS):
+            gather(v2_w, tab2_w[:].bitcast(U32), list2, c, c + 1)
         for c in range(CHUNKS):
             gate_stage(c)
         gather(v_w, tab_w[:].bitcast(U32), list1, 0, 4)

@@ -25,9 +25,9 @@ LIST_COLS = P // 16
 WA_ROW, TAB_ROW, EN8_ROW = 4, 8, 12
 
 
-def load_scales(queue, plane, scales, first_row):
+def load_scales(queue, plane, scales, first_row, quadrants=range(4)):
     rows = scales[0].bitcast(I32)
-    for q in range(4):
+    for q in quadrants:
         queue.dma_start(out=plane[32 * q + first_row : 32 * q + first_row + 4, :], in_=rows[4 * q : 4 * q + 4, :])
 
 
@@ -59,29 +59,32 @@ def tile_list_kg_gate_mix_none_kernel(tc, tab_words, tab_scales, tab2_words, tab
         warm = keep.tile([P, 8], F32, name="warm")
 
         nc.vector.memset(tab2_s[:], 0)
+        nc.gpsimd.memset(wa_s[:], 0)
         nc.vector.memset(wb_s[:], 0)
-        nc.vector.memset(tab_s[:], 0)
         nc.vector.memset(warm[:, 0:1], 0.0)
+        nc.vector.memset(tab_s[:], 0)
         nc.vector.memset(en8_s[:], 0)
         nc.vector.memset(en4_s[:], 0)
-        nc.gpsimd.memset(wa_s[:], 0)
-        load_scales(nc.gpsimd, wa_s, wa_scales, WA_ROW)
+        load_scales(nc.gpsimd, wa_s, wa_scales, WA_ROW, range(0, 2))
         make_identity(nc, ident[:])
         load_scales(nc.gpsimd, en4_s, en4_scales, 0)
+        load_scales(nc.scalar, tab2_s, tab2_scales, 0, range(2, 4))
+        load_scales(nc.scalar, wb_s, wb_scales, 0, range(0, 1))
         nc.scalar.activation(out=warm[:, 1:2], in_=warm[:, 0:1], func=SIGMOID)
 
         nc.sync.dma_start(list2[:], offs2)
-        load_scales(nc.sync, tab2_s, tab2_scales, 0)
+        nc.sync.dma_start(list1[:], offs)
+        load_scales(nc.sync, tab2_s, tab2_scales, 0, range(0, 2))
         nc.sync.dma_start(out=tab2_w[:], in_=words8(tab2_words))
         nc.sync.dma_start(out=wb_w[:], in_=wb_words[0].bitcast(I32))
-        load_scales(nc.sync, wb_s, wb_scales, 0)
-        nc.sync.dma_start(list1[:], offs)
+        load_scales(nc.sync, wb_s, wb_scales, 0, range(1, 4))
         nc.sync.dma_start(out=tab_w[:], in_=words8(tab_words))
         nc.sync.dma_start(out=wa_w[:], in_=words8(wa_words))
         load_scales(nc.sync, tab_s, tab_scales, TAB_ROW)
+        load_scales(nc.sync, wa_s, wa_scales, WA_ROW, range(2, 4))
+        nc.sync.dma_start(out=en4_w[:], in_=en4_words[0].bitcast(I32))
         load_scales(nc.sync, en8_s, en8_scales, EN8_ROW)
         nc.sync.dma_start(out=en8_w[:], in_=words8(en8_words))
-        nc.sync.dma_start(out=en4_w[:], in_=en4_words[0].bitcast(I32))
 
         v_w = keep.tile([P, J], U32, name="v_w", align_bytes=64)
         v_s = keep.tile([P, J], U8, name="v_s", align_bytes=64)
@@ -185,13 +188,13 @@ def tile_list_kg_gate_mix_none_kernel(tc, tab_words, tab_scales, tab2_words, tab
                 nc.scalar.dma_start(out=out[P : 2 * P, cols], in_=y_sb[:, c, 1, :])
 
         gather(v2_s, tab2_s[:].bitcast(U8), list2, 0, CHUNKS)
-        for c in range(CHUNKS):
-            gather(v2_w, tab2_w[:].bitcast(U32), list2, c, c + 1)
+        gather(v2_w, tab2_w[:].bitcast(U32), list2, 0, 1)
+        gather(v2_w, tab2_w[:].bitcast(U32), list2, 1, CHUNKS)
         for c in range(CHUNKS):
             gate_stage(c)
         gather(v_w, tab_w[:].bitcast(U32), list1, 0, 4)
-        for c in range(CHUNKS):
-            gather(v_s, tab_s[:].bitcast(U8), list1, c, c + 1)
+        gather(v_s, tab_s[:].bitcast(U8), list1, 0, 1)
+        gather(v_s, tab_s[:].bitcast(U8), list1, 1, CHUNKS)
         last = CHUNKS - 1
         units = [(c, b) for c in range(CHUNKS) for b in range(HALVES)]
         sums = {}
@@ -205,9 +208,12 @@ def tile_list_kg_gate_mix_none_kernel(tc, tab_words, tab_scales, tab2_words, tab
                 turn_stage(c, b, b + 1)
             elif b == 1:
                 turn_stage(c, 0, 2)
-            if b == 1 and c > 0:
-                quant_stage(c - 1, 0, 2)
-                score_stage(c - 1)
+            if b == 1 and c == 1:
+                quant_stage(0, 0, 2)
+                score_stage(0)
+        for c in range(1, last):
+            quant_stage(c, 0, 2)
+            score_stage(c)
         quant_stage(last, 0, 1)
         quant_stage(last, 1, 2)
         score_stage(last)

@@ -22,13 +22,19 @@ PASS = 512
 CHUNKS = J // P
 HALVES = R // PASS
 LIST_COLS = P // 16
-WA_ROW, TAB_ROW, EN8_ROW = 4, 8, 12
+WA_ROW, TAB_ROW, EN8_ROW = 0, 8, 12
 
 
 def load_scales(queue, plane, scales, first_row, quadrants=range(4)):
     rows = scales[0].bitcast(I32)
     for q in quadrants:
         queue.dma_start(out=plane[32 * q + first_row : 32 * q + first_row + 4, :], in_=rows[4 * q : 4 * q + 4, :])
+
+
+def load_plane(queue, plane, scales, first_row):
+    rows = scales[0].bitcast(I32)
+    queue.dma_start(out=plane[first_row : first_row + 98, :], in_=rows[0:14, :].partition_broadcast(7))
+    queue.dma_start(out=plane[first_row + 98 : P, :], in_=rows[14:16, :].partition_broadcast((P - 98 - first_row) // 2))
 
 
 def words8(w):
@@ -39,7 +45,7 @@ def tile_list_kg_gate_mix_none_kernel(tc, tab_words, tab_scales, tab2_words, tab
     nc = tc.nc
     with ExitStack() as ctx:
         keep = ctx.enter_context(tc.tile_pool(name="keep", bufs=1))
-        psum = ctx.enter_context(tc.psum_pool(name="psum", bufs=8))
+        psum = ctx.enter_context(tc.psum_pool(name="psum", bufs=1))
 
         list1 = keep.tile([P, J // 16], U16, name="list1")
         list2 = keep.tile([P, J // 16], U16, name="list2")
@@ -47,7 +53,7 @@ def tile_list_kg_gate_mix_none_kernel(tc, tab_words, tab_scales, tab2_words, tab
         tab2_w = keep.tile([P, T], I32, name="tab2_w", align_bytes=64)
         tab_s = keep.tile([P, T // 4], I32, name="tab_s", align_bytes=64)
         tab2_s = keep.tile([P, T // 4], I32, name="tab2_s", align_bytes=64)
-        wa_w = keep.tile([P, R], I32, name="wa_w", align_bytes=64)
+        wa_w = [keep.tile([P, PASS], I32, name="wa_w%d" % b, align_bytes=64) for b in range(HALVES)]
         wb_w = keep.tile([P, R // 2], I32, name="wb_w", align_bytes=64)
         wb_s = keep.tile([P, R // 4], I32, name="wb_s", align_bytes=64)
         wa_s = keep.tile([P, R // 4], I32, name="wa_s", align_bytes=64)
@@ -56,45 +62,41 @@ def tile_list_kg_gate_mix_none_kernel(tc, tab_words, tab_scales, tab2_words, tab
         en8_w = keep.tile([P, N], I32, name="en8_w", align_bytes=64)
         en4_w = keep.tile([P, N // 2], I32, name="en4_w", align_bytes=64)
         ident = keep.tile([P, P], F32, name="ident", align_bytes=64)
-        warm = keep.tile([P, 8], F32, name="warm")
 
         nc.vector.memset(tab2_s[:], 0)
-        nc.gpsimd.memset(wa_s[:], 0)
         nc.vector.memset(wb_s[:], 0)
-        nc.vector.memset(warm[:, 0:1], 0.0)
         nc.vector.memset(tab_s[:], 0)
-        nc.vector.memset(en8_s[:], 0)
-        nc.vector.memset(en4_s[:], 0)
-        load_scales(nc.gpsimd, wa_s, wa_scales, WA_ROW, range(0, 2))
         make_identity(nc, ident[:])
-        load_scales(nc.gpsimd, en4_s, en4_scales, 0)
-        load_scales(nc.scalar, tab2_s, tab2_scales, 0, range(2, 4))
-        load_scales(nc.scalar, wb_s, wb_scales, 0, range(0, 1))
-        nc.scalar.activation(out=warm[:, 1:2], in_=warm[:, 0:1], func=SIGMOID)
+        load_plane(nc.gpsimd, wa_s, wa_scales, WA_ROW)
+        load_plane(nc.gpsimd, en8_s, en8_scales, EN8_ROW)
+        load_plane(nc.gpsimd, en4_s, en4_scales, 0)
+        load_scales(nc.scalar, tab2_s, tab2_scales, 0, range(0, 2))
 
         nc.sync.dma_start(list2[:], offs2)
-        nc.sync.dma_start(list1[:], offs)
-        load_scales(nc.sync, tab2_s, tab2_scales, 0, range(0, 2))
+        load_scales(nc.sync, tab2_s, tab2_scales, 0, range(2, 4))
+        load_scales(nc.sync, wb_s, wb_scales, 0, range(0, 1))
         nc.sync.dma_start(out=tab2_w[:], in_=words8(tab2_words))
         nc.sync.dma_start(out=wb_w[:], in_=wb_words[0].bitcast(I32))
         load_scales(nc.sync, wb_s, wb_scales, 0, range(1, 4))
+        nc.sync.dma_start(list1[:], offs)
         nc.sync.dma_start(out=tab_w[:], in_=words8(tab_words))
-        nc.sync.dma_start(out=wa_w[:], in_=words8(wa_words))
-        load_scales(nc.sync, tab_s, tab_scales, TAB_ROW)
-        load_scales(nc.sync, wa_s, wa_scales, WA_ROW, range(2, 4))
-        nc.sync.dma_start(out=en4_w[:], in_=en4_words[0].bitcast(I32))
-        load_scales(nc.sync, en8_s, en8_scales, EN8_ROW)
+        load_scales(nc.sync, tab_s, tab_scales, TAB_ROW, range(0, 1))
+        nc.sync.dma_start(out=wa_w[0][:], in_=words8(wa_words)[:, 0:PASS])
+        load_scales(nc.sync, tab_s, tab_scales, TAB_ROW, range(1, 4))
+        nc.sync.dma_start(out=wa_w[1][:], in_=words8(wa_words)[:, PASS:R])
         nc.sync.dma_start(out=en8_w[:], in_=words8(en8_words))
+        nc.sync.dma_start(out=en4_w[:], in_=en4_words[0].bitcast(I32))
 
         v_w = keep.tile([P, J], U32, name="v_w", align_bytes=64)
         v_s = keep.tile([P, J], U8, name="v_s", align_bytes=64)
         v2_w = keep.tile([P, J], U32, name="v2_w", align_bytes=64)
         v2_s = keep.tile([P, J], U8, name="v2_s", align_bytes=64)
-        gate = keep.tile([P, CHUNKS, HALVES, PASS], F32, name="gate", align_bytes=64)
-        h = keep.tile([P, CHUNKS, HALVES, PASS], BF16, name="h", align_bytes=64)
-        ht = keep.tile([P, CHUNKS, HALVES, PASS], BF16, name="ht", align_bytes=64)
-        hq_w = keep.tile([P, CHUNKS, HALVES, P], U32, name="hq_w", align_bytes=64)
-        hq_s = keep.tile([P, CHUNKS, HALVES, P], U8, name="hq_s", align_bytes=64)
+        gate = {(c, b): keep.tile([P, PASS], F32, name="gate%d%d" % (c, b), tag="gate%d%d" % (c, b), align_bytes=64) for c in range(CHUNKS) for b in range(HALVES)}
+        h = {(c, b): keep.tile([P, PASS], BF16, name="h%d%d" % (c, b), align_bytes=64) for c in range(CHUNKS) for b in range(HALVES)}
+        spans = [(c, 0, 2) for c in range(CHUNKS - 1)] + [(CHUNKS - 1, 0, 1), (CHUNKS - 1, 1, 2)]
+        ht = {(c, b0): keep.tile([P, (b1 - b0) * PASS], BF16, name="ht%d%d" % (c, b0), align_bytes=64) for c, b0, b1 in spans}
+        hq_s = {}
+        hq_w = {}
         y_sb = keep.tile([P, CHUNKS, N // P, P], F32, name="y_sb", align_bytes=64)
 
         def gather(dst, window, lst, c0, c1):
@@ -103,10 +105,10 @@ def tile_list_kg_gate_mix_none_kernel(tc, tab_words, tab_scales, tab2_words, tab
         def by_pair(bank):
             return bank[:].rearrange("p (m u e) -> p u m e", u=2, e=2)
 
-        def gate_stage(c):
+        def gate_stage(c, b, bank):
             cols = slice(c * P, (c + 1) * P)
-            for b in range(HALVES):
-                hb = psum.tile([P, PASS], F32, name="bank")
+            if True:
+                hb = psum.tile([P, PASS], F32, name="bank%d" % bank)
                 nc.tensor.matmul_mx(
                     out=hb[:],
                     lhsT=v2_w[:, cols].bitcast(FP8X4),
@@ -116,16 +118,16 @@ def tile_list_kg_gate_mix_none_kernel(tc, tab_words, tab_scales, tab2_words, tab
                     start=True,
                     stop=True,
                 )
-                nc.scalar.activation(out=gate[:, c, b, :].rearrange("p (u m e) -> p u m e", u=2, e=2), in_=by_pair(hb), func=SIGMOID)
+                nc.scalar.activation(out=gate[c, b][:].rearrange("p (u m e) -> p u m e", u=2, e=2), in_=by_pair(hb), func=SIGMOID)
 
-        def project_stage(c, b):
+        def project_stage(c, b, bank):
             cols = slice(c * P, (c + 1) * P)
-            ha = psum.tile([P, PASS], F32, name="bank")
+            ha = psum.tile([P, PASS], F32, name="bank%d" % bank)
             nc.tensor.matmul_mx(
                 out=ha[:],
                 lhsT=v_w[:, cols].bitcast(FP8X4),
                 lhsT_scale=v_s[TAB_ROW:P, cols],
-                rhs=wa_w[:, b * PASS : (b + 1) * PASS].bitcast(FP8X4),
+                rhs=wa_w[b][:].bitcast(FP8X4),
                 rhs_scale=wa_s[WA_ROW:P, :].bitcast(U8)[:, b * PASS : (b + 1) * PASS],
                 start=True,
                 stop=True,
@@ -134,30 +136,32 @@ def tile_list_kg_gate_mix_none_kernel(tc, tab_words, tab_scales, tab2_words, tab
 
         def product_stage(c, b, ha):
             nc.vector.tensor_tensor(
-                out=h[:, c, b, :].rearrange("p (u m e) -> p u m e", u=2, e=2),
+                out=h[c, b][:].rearrange("p (u m e) -> p u m e", u=2, e=2),
                 in0=by_pair(ha),
-                in1=gate[:, c, b, :].rearrange("p (u m e) -> p u m e", u=2, e=2),
+                in1=gate[c, b][:].rearrange("p (u m e) -> p u m e", u=2, e=2),
                 op=MULT,
             )
 
-        def turn_stage(c, b0, b1):
+        def turn_stage(c, b0, b1, bank):
             nb = b1 - b0
-            xt = psum.tile([P, HALVES, 2, P], F32, name="bank")
+            xt = psum.tile([P, HALVES, 2, P], F32, name="bank%d" % bank)
             for b in range(b0, b1):
-                pairs = h[:, c, b, :].bitcast(F32)
+                pairs = h[c, b][:].bitcast(F32)
                 for u in range(2):
                     nc.tensor.transpose(xt[:, b, u, :], pairs[:, u * P : (u + 1) * P], ident[:])
             nc.scalar.copy(
-                out=ht[:, c, b0:b1, :].rearrange("p b w -> p (b w)").bitcast(F32).rearrange("p (b j u) -> p b j u", b=nb, u=2),
+                out=ht[c, b0][:].bitcast(F32).rearrange("p (b j u) -> p b j u", b=nb, u=2),
                 in_=xt[:, b0:b1, :, :].rearrange("p b u j -> p b j u"),
             )
 
-        def quant_stage(c, b0, b1):
-            nc.vector.quantize_mx(
-                out=hq_w[:, c, b0:b1, :].rearrange("p b w -> p (b w)").bitcast(FP8X4),
-                scales=hq_s[:, c, b0:b1, :].rearrange("p b w -> p (b w)"),
-                in_=ht[:, c, b0:b1, :].rearrange("p b w -> p (b w)"),
-            )
+        def quant_stage(c, b0, b1, tag):
+            nb = b1 - b0
+            words = keep.tile([P, nb * P], U32, name="hq_w%d%d" % (c, b0), tag=tag, align_bytes=64)
+            plane = keep.tile([P, nb * P], U8, name="hq_s%d%d" % (c, b0), align_bytes=64)
+            nc.vector.quantize_mx(out=words[:].bitcast(FP8X4), scales=plane[:], in_=ht[c, b0][:])
+            for b in range(b0, b1):
+                hq_w[c, b] = words[:, (b - b0) * P : (b - b0 + 1) * P]
+                hq_s[c, b] = plane[:, (b - b0) * P : (b - b0 + 1) * P]
 
         def score_pass(c, nt, b, dst):
             if b == 0:
@@ -166,19 +170,19 @@ def tile_list_kg_gate_mix_none_kernel(tc, tab_words, tab_scales, tab2_words, tab
             else:
                 words = en4_w[:].bitcast(U8)[:, 2 * nt * P : 2 * (nt + 1) * P].bitcast(FP4X4)
                 scales = en4_s[:].bitcast(U8)[:, nt * P : (nt + 1) * P]
-            nc.tensor.matmul_mx(out=dst, lhsT=words, lhsT_scale=scales, rhs=hq_w[:, c, b, :].bitcast(FP8X4), rhs_scale=hq_s[:, c, b, :], start=(b == 0), stop=(b == 1))
+            nc.tensor.matmul_mx(out=dst, lhsT=words, lhsT_scale=scales, rhs=hq_w[c, b].bitcast(FP8X4), rhs_scale=hq_s[c, b], start=(b == 0), stop=(b == 1))
 
-        def score_stage(c):
+        def score_stage(c, bks):
             cols = slice(c * P, (c + 1) * P)
             if c < CHUNKS - 1:
-                bank = psum.tile([P, N // P, P], F32, name="bank")
+                bank = psum.tile([P, N // P, P], F32, name="bank%d" % bks[0])
                 for nt in range(N // P):
                     for b in range(HALVES):
                         score_pass(c, nt, b, bank[:, nt, :])
                 nc.scalar.copy(out=y_sb[:, c, :, :], in_=bank[:])
                 nc.sync.dma_start(out=out.rearrange("(a p) j -> p a j", p=P)[:, :, cols], in_=y_sb[:, c, :, :])
             else:
-                banks = [psum.tile([P, P], F32, name="bank") for nt in range(N // P)]
+                banks = [psum.tile([P, P], F32, name="bank%d" % bks[nt]) for nt in range(N // P)]
                 for b in range(HALVES):
                     for nt in range(N // P):
                         score_pass(c, nt, b, banks[nt][:])
@@ -190,30 +194,36 @@ def tile_list_kg_gate_mix_none_kernel(tc, tab_words, tab_scales, tab2_words, tab
         gather(v2_s, tab2_s[:].bitcast(U8), list2, 0, CHUNKS)
         gather(v2_w, tab2_w[:].bitcast(U32), list2, 0, 1)
         gather(v2_w, tab2_w[:].bitcast(U32), list2, 1, CHUNKS)
-        for c in range(CHUNKS):
-            gate_stage(c)
-        gather(v_w, tab_w[:].bitcast(U32), list1, 0, 4)
+        gather(v_w, tab_w[:].bitcast(U32), list1, 0, CHUNKS)
         gather(v_s, tab_s[:].bitcast(U8), list1, 0, 1)
         gather(v_s, tab_s[:].bitcast(U8), list1, 1, CHUNKS)
         last = CHUNKS - 1
-        units = [(c, b) for c in range(CHUNKS) for b in range(HALVES)]
+        units = [(0, 0), (1, 0), (0, 1), (1, 1), (2, 0), (2, 1), (3, 0), (3, 1)]
+        gate_bank = [0, 1, 2, 3, 4, 5, 6, 7]
+        proj_bank = [6, 7, 0, 1, 2, 0, 1, 2]
+        turn_bank = {2: 3, 3: 4, 5: 5, 6: 6, 7: 7}
+        for i in range(6):
+            gate_stage(*units[i], gate_bank[i])
         sums = {}
-        for c, b in units[:4]:
-            sums[c, b] = project_stage(c, b)
+        for i in range(3):
+            sums[i] = project_stage(*units[i], proj_bank[i])
         for i, (c, b) in enumerate(units):
-            product_stage(c, b, sums[c, b])
-            if i + 4 < len(units):
-                sums[units[i + 4]] = project_stage(*units[i + 4])
+            product_stage(c, b, sums[i])
+            if i + 6 < len(units):
+                gate_stage(*units[i + 6], gate_bank[i + 6])
+            if i + 3 < len(units):
+                sums[i + 3] = project_stage(*units[i + 3], proj_bank[i + 3])
             if c == last:
-                turn_stage(c, b, b + 1)
+                turn_stage(c, b, b + 1, turn_bank[i])
             elif b == 1:
-                turn_stage(c, 0, 2)
-            if b == 1 and c == 1:
-                quant_stage(0, 0, 2)
-                score_stage(0)
-        for c in range(1, last):
-            quant_stage(c, 0, 2)
-            score_stage(c)
-        quant_stage(last, 0, 1)
-        quant_stage(last, 1, 2)
-        score_stage(last)
+                turn_stage(c, 0, 2, turn_bank[i])
+            if i == 4:
+                quant_stage(0, 0, 2, "gate%d%d" % units[i])
+                score_stage(0, [3])
+        quant_stage(1, 0, 2, "gate31")
+        quant_stage(2, 0, 2, "hq2")
+        quant_stage(last, 0, 1, "hq30")
+        quant_stage(last, 1, 2, "hq31")
+        score_stage(1, [4])
+        score_stage(2, [0])
+        score_stage(3, [1, 5])

@@ -22,7 +22,7 @@ PASS = 512
 CHUNKS = J // P
 HALVES = R // PASS
 LIST_COLS = P // 16
-WA_ROW, TAB_ROW, EN8_ROW = 0, 8, 12
+WA_ROW, TAB_ROW, EN8_ROW = 4, 8, 12
 
 
 def load_scales(queue, plane, scales, first_row, quadrants=range(4)):
@@ -64,28 +64,26 @@ def tile_list_kg_gate_mix_none_kernel(tc, tab_words, tab_scales, tab2_words, tab
         ident = keep.tile([P, P], F32, name="ident", align_bytes=64)
 
         nc.vector.memset(tab2_s[:], 0)
-        nc.vector.memset(wb_s[:], 0)
         nc.vector.memset(tab_s[:], 0)
+        nc.vector.memset(wa_s[:], 0)
+        load_plane(nc.gpsimd, wb_s, wb_scales, 0)
         make_identity(nc, ident[:])
-        load_plane(nc.gpsimd, wa_s, wa_scales, WA_ROW)
-        load_plane(nc.gpsimd, en8_s, en8_scales, EN8_ROW)
-        load_plane(nc.gpsimd, en4_s, en4_scales, 0)
-        load_scales(nc.scalar, tab2_s, tab2_scales, 0, range(0, 2))
+        load_scales(nc.scalar, tab2_s, tab2_scales, 0, range(0, 4))
 
         nc.sync.dma_start(list2[:], offs2)
-        load_scales(nc.sync, tab2_s, tab2_scales, 0, range(2, 4))
-        load_scales(nc.sync, wb_s, wb_scales, 0, range(0, 1))
         nc.sync.dma_start(out=tab2_w[:], in_=words8(tab2_words))
         nc.sync.dma_start(out=wb_w[:], in_=wb_words[0].bitcast(I32))
-        load_scales(nc.sync, wb_s, wb_scales, 0, range(1, 4))
         nc.sync.dma_start(list1[:], offs)
         nc.sync.dma_start(out=tab_w[:], in_=words8(tab_words))
         load_scales(nc.sync, tab_s, tab_scales, TAB_ROW, range(0, 1))
         nc.sync.dma_start(out=wa_w[0][:], in_=words8(wa_words)[:, 0:PASS])
         load_scales(nc.sync, tab_s, tab_scales, TAB_ROW, range(1, 4))
+        load_scales(nc.sync, wa_s, wa_scales, WA_ROW)
         nc.sync.dma_start(out=wa_w[1][:], in_=words8(wa_words)[:, PASS:R])
         nc.sync.dma_start(out=en8_w[:], in_=words8(en8_words))
         nc.sync.dma_start(out=en4_w[:], in_=en4_words[0].bitcast(I32))
+        load_plane(nc.sync, en8_s, en8_scales, EN8_ROW)
+        load_plane(nc.sync, en4_s, en4_scales, 0)
 
         v_w = keep.tile([P, J], U32, name="v_w", align_bytes=64)
         v_s = keep.tile([P, J], U8, name="v_s", align_bytes=64)
@@ -191,12 +189,13 @@ def tile_list_kg_gate_mix_none_kernel(tc, tab_words, tab_scales, tab2_words, tab
                 nc.scalar.copy(out=y_sb[:, c, 1, :], in_=banks[1][:])
                 nc.scalar.dma_start(out=out[P : 2 * P, cols], in_=y_sb[:, c, 1, :])
 
-        gather(v2_s, tab2_s[:].bitcast(U8), list2, 0, CHUNKS)
-        gather(v2_w, tab2_w[:].bitcast(U32), list2, 0, 1)
-        gather(v2_w, tab2_w[:].bitcast(U32), list2, 1, CHUNKS)
+        gather(v2_w, tab2_w[:].bitcast(U32), list2, 0, 2)
+        gather(v2_s, tab2_s[:].bitcast(U8), list2, 0, 2)
+        gather(v2_w, tab2_w[:].bitcast(U32), list2, 2, CHUNKS)
+        gather(v2_s, tab2_s[:].bitcast(U8), list2, 2, CHUNKS)
         gather(v_w, tab_w[:].bitcast(U32), list1, 0, CHUNKS)
-        gather(v_s, tab_s[:].bitcast(U8), list1, 0, 1)
-        gather(v_s, tab_s[:].bitcast(U8), list1, 1, CHUNKS)
+        gather(v_s, tab_s[:].bitcast(U8), list1, 0, 2)
+        gather(v_s, tab_s[:].bitcast(U8), list1, 2, CHUNKS)
         last = CHUNKS - 1
         units = [(0, 0), (1, 0), (0, 1), (1, 1), (2, 0), (2, 1), (3, 0), (3, 1)]
         gate_bank = [0, 1, 2, 3, 4, 5, 6, 7]
@@ -217,7 +216,7 @@ def tile_list_kg_gate_mix_none_kernel(tc, tab_words, tab_scales, tab2_words, tab
                 turn_stage(c, b, b + 1, turn_bank[i])
             elif b == 1:
                 turn_stage(c, 0, 2, turn_bank[i])
-            if i == 4:
+            if i == 5:
                 quant_stage(0, 0, 2, "gate%d%d" % units[i])
                 score_stage(0, [3])
         quant_stage(1, 0, 2, "gate31")

@@ -1,7 +1,6 @@
 from contextlib import ExitStack
 
 import concourse.mybir as mybir
-from concourse.masks import make_identity
 
 K, L, R, N, T, J = 512, 512, 1024, 256, 1024, 512
 FLOPS = 2 * J * (K * R + L * R + R * N)
@@ -22,7 +21,7 @@ PASS = 512
 CHUNKS = J // P
 HALVES = R // PASS
 LIST_COLS = P // 16
-WA_ROW, TAB_ROW, EN8_ROW = 4, 8, 12
+WA_ROW, TAB_ROW, EN8_ROW = 0, 8, 12
 
 
 def load_scales(queue, plane, scales, first_row, quadrants=range(4)):
@@ -65,9 +64,10 @@ def tile_list_kg_gate_mix_none_kernel(tc, tab_words, tab_scales, tab2_words, tab
 
         nc.vector.memset(tab2_s[:], 0)
         nc.vector.memset(tab_s[:], 0)
-        nc.vector.memset(wa_s[:], 0)
+        nc.vector.memset(ident[:], 1.0)
         load_plane(nc.gpsimd, wb_s, wb_scales, 0)
-        make_identity(nc, ident[:])
+        load_plane(nc.gpsimd, wa_s, wa_scales, WA_ROW)
+        nc.gpsimd.affine_select(out=ident[:], in_=ident[:], pattern=[[-1, P]], compare_op=mybir.AluOpType.is_equal, fill=0.0, base=0, channel_multiplier=1)
         load_scales(nc.scalar, tab2_s, tab2_scales, 0, range(0, 4))
 
         nc.sync.dma_start(list2[:], offs2)
@@ -78,7 +78,6 @@ def tile_list_kg_gate_mix_none_kernel(tc, tab_words, tab_scales, tab2_words, tab
         load_scales(nc.sync, tab_s, tab_scales, TAB_ROW, range(0, 1))
         nc.sync.dma_start(out=wa_w[0][:], in_=words8(wa_words)[:, 0:PASS])
         load_scales(nc.sync, tab_s, tab_scales, TAB_ROW, range(1, 4))
-        load_scales(nc.sync, wa_s, wa_scales, WA_ROW)
         nc.sync.dma_start(out=wa_w[1][:], in_=words8(wa_words)[:, PASS:R])
         nc.sync.dma_start(out=en8_w[:], in_=words8(en8_words))
         nc.sync.dma_start(out=en4_w[:], in_=en4_words[0].bitcast(I32))

@@ -36,6 +36,14 @@ def load_plane(queue, plane, scales, first_row):
     queue.dma_start(out=plane[first_row + 98 : P, :], in_=rows[14:16, :].partition_broadcast((P - 98 - first_row) // 2))
 
 
+def load_first_rows(queue, plane, scales):
+    queue.dma_start(out=plane[0:98, :], in_=scales[0].bitcast(I32)[0:14, :].partition_broadcast(7))
+
+
+def load_last_rows(queue, plane, scales):
+    queue.dma_start(out=plane[98:100, :], in_=scales[0].bitcast(I32)[14:16, :])
+
+
 def words8(w):
     return w[0].rearrange("p n t -> p (n t)").bitcast(I32)
 
@@ -63,21 +71,25 @@ def tile_list_kg_gate_mix_none_kernel(tc, tab_words, tab_scales, tab2_words, tab
         ident = keep.tile([P, P], F32, name="ident", align_bytes=64)
 
         nc.vector.memset(tab2_s[:], 0)
+        nc.gpsimd.memset(wb_s[96:P, :], 0)
+        nc.vector.memset(wa_s[96:P, :], 0)
         nc.vector.memset(tab_s[:], 0)
         nc.vector.memset(ident[:], 1.0)
-        load_plane(nc.gpsimd, wb_s, wb_scales, 0)
-        load_plane(nc.gpsimd, wa_s, wa_scales, WA_ROW)
+        load_first_rows(nc.gpsimd, wb_s, wb_scales)
+        load_first_rows(nc.gpsimd, wa_s, wa_scales)
         nc.gpsimd.affine_select(out=ident[:], in_=ident[:], pattern=[[-1, P]], compare_op=mybir.AluOpType.is_equal, fill=0.0, base=0, channel_multiplier=1)
-        load_scales(nc.scalar, tab2_s, tab2_scales, 0, range(0, 4))
+        load_scales(nc.scalar, tab2_s, tab2_scales, 0, range(0, 2))
 
         nc.sync.dma_start(list2[:], offs2)
+        load_scales(nc.sync, tab2_s, tab2_scales, 0, range(2, 4))
+        load_last_rows(nc.sync, wb_s, wb_scales)
         nc.sync.dma_start(out=tab2_w[:], in_=words8(tab2_words))
         nc.sync.dma_start(out=wb_w[:], in_=wb_words[0].bitcast(I32))
         nc.sync.dma_start(list1[:], offs)
+        load_scales(nc.sync, tab_s, tab_scales, TAB_ROW)
         nc.sync.dma_start(out=tab_w[:], in_=words8(tab_words))
-        load_scales(nc.sync, tab_s, tab_scales, TAB_ROW, range(0, 1))
         nc.sync.dma_start(out=wa_w[0][:], in_=words8(wa_words)[:, 0:PASS])
-        load_scales(nc.sync, tab_s, tab_scales, TAB_ROW, range(1, 4))
+        load_last_rows(nc.sync, wa_s, wa_scales)
         nc.sync.dma_start(out=wa_w[1][:], in_=words8(wa_words)[:, PASS:R])
         nc.sync.dma_start(out=en8_w[:], in_=words8(en8_words))
         nc.sync.dma_start(out=en4_w[:], in_=en4_words[0].bitcast(I32))
@@ -188,29 +200,29 @@ def tile_list_kg_gate_mix_none_kernel(tc, tab_words, tab_scales, tab2_words, tab
                 nc.scalar.copy(out=y_sb[:, c, 1, :], in_=banks[1][:])
                 nc.scalar.dma_start(out=out[P : 2 * P, cols], in_=y_sb[:, c, 1, :])
 
-        gather(v2_w, tab2_w[:].bitcast(U32), list2, 0, 2)
-        gather(v2_s, tab2_s[:].bitcast(U8), list2, 0, 2)
-        gather(v2_w, tab2_w[:].bitcast(U32), list2, 2, CHUNKS)
-        gather(v2_s, tab2_s[:].bitcast(U8), list2, 2, CHUNKS)
-        gather(v_w, tab_w[:].bitcast(U32), list1, 0, CHUNKS)
-        gather(v_s, tab_s[:].bitcast(U8), list1, 0, 2)
-        gather(v_s, tab_s[:].bitcast(U8), list1, 2, CHUNKS)
+        gather(v2_s, tab2_s[:].bitcast(U8), list2, 0, CHUNKS)
+        gather(v2_w, tab2_w[:].bitcast(U32), list2, 0, 1)
+        gather(v2_w, tab2_w[:].bitcast(U32), list2, 1, CHUNKS)
+        gather(v_s, tab_s[:].bitcast(U8), list1, 0, CHUNKS)
+        gather(v_w, tab_w[:].bitcast(U32), list1, 0, 2)
+        gather(v_w, tab_w[:].bitcast(U32), list1, 2, CHUNKS)
         last = CHUNKS - 1
         units = [(0, 0), (1, 0), (0, 1), (1, 1), (2, 0), (2, 1), (3, 0), (3, 1)]
         gate_bank = [0, 1, 2, 3, 4, 5, 6, 7]
-        proj_bank = [6, 7, 0, 1, 2, 0, 1, 2]
-        turn_bank = {2: 3, 3: 4, 5: 5, 6: 6, 7: 7}
-        for i in range(6):
+        proj_bank = [5, 6, 7, 0, 1, 2, 0, 5]
+        turn_bank = {2: 3, 3: 4, 5: 1, 6: 2, 7: 6}
+        for i in (0, 2, 1, 3, 4):
             gate_stage(*units[i], gate_bank[i])
         sums = {}
-        for i in range(3):
+        for i in range(4):
             sums[i] = project_stage(*units[i], proj_bank[i])
         for i, (c, b) in enumerate(units):
             product_stage(c, b, sums[i])
-            if i + 6 < len(units):
-                gate_stage(*units[i + 6], gate_bank[i + 6])
-            if i + 3 < len(units):
-                sums[i + 3] = project_stage(*units[i + 3], proj_bank[i + 3])
+            if i + 5 < len(units):
+                gate_stage(*units[i + 5], gate_bank[i + 5])
+            ahead = {0: 4, 1: 5, 3: 6, 4: 7}
+            if i in ahead:
+                sums[ahead[i]] = project_stage(*units[ahead[i]], proj_bank[ahead[i]])
             if c == last:
                 turn_stage(c, b, b + 1, turn_bank[i])
             elif b == 1:
@@ -223,5 +235,5 @@ def tile_list_kg_gate_mix_none_kernel(tc, tab_words, tab_scales, tab2_words, tab
         quant_stage(last, 0, 1, "hq30")
         quant_stage(last, 1, 2, "hq31")
         score_stage(1, [4])
-        score_stage(2, [0])
-        score_stage(3, [1, 5])
+        score_stage(2, [7])
+        score_stage(3, [0, 5])

@@ -19,15 +19,20 @@ MULT = mybir.AluOpType.mult
 P = 128
 PASS = 512
 CHUNKS = J // P
-HALVES = R // PASS
 LIST_COLS = P // 16
-WA_ROW, TAB_ROW, EN8_ROW = 0, 8, 12
+TAB_ROW, EN8_ROW = 8, 12
 
 
 def load_scales(queue, plane, scales, first_row, quadrants=range(4)):
     rows = scales[0].bitcast(I32)
     for q in quadrants:
         queue.dma_start(out=plane[32 * q + first_row : 32 * q + first_row + 4, :], in_=rows[4 * q : 4 * q + 4, :])
+
+
+def load_quadrants(queue, plane, scales, quadrants):
+    rows = scales[0].bitcast(I32)
+    for q in quadrants:
+        queue.dma_start(out=plane[32 * q : 32 * q + 32, :], in_=rows[4 * q : 4 * q + 4, :].partition_broadcast(8))
 
 
 def load_plane(queue, plane, scales, first_row):
@@ -60,7 +65,7 @@ def tile_list_kg_gate_mix_none_kernel(tc, tab_words, tab_scales, tab2_words, tab
         tab2_w = keep.tile([P, T], I32, name="tab2_w", align_bytes=64)
         tab_s = keep.tile([P, T // 4], I32, name="tab_s", align_bytes=64)
         tab2_s = keep.tile([P, T // 4], I32, name="tab2_s", align_bytes=64)
-        wa_w = [keep.tile([P, PASS], I32, name="wa_w%d" % b, align_bytes=64) for b in range(HALVES)]
+        wa_w = [keep.tile([P, PASS], I32, name="wa_w%d" % b, align_bytes=64) for b in range(2)]
         wb_w = keep.tile([P, R // 2], I32, name="wb_w", align_bytes=64)
         wb_s = keep.tile([P, R // 4], I32, name="wb_s", align_bytes=64)
         wa_s = keep.tile([P, R // 4], I32, name="wa_s", align_bytes=64)
@@ -70,7 +75,6 @@ def tile_list_kg_gate_mix_none_kernel(tc, tab_words, tab_scales, tab2_words, tab
         en4_w = keep.tile([P, N // 2], I32, name="en4_w", align_bytes=64)
         ident = keep.tile([P, P], F32, name="ident", align_bytes=64)
 
-        nc.vector.memset(tab2_s[:], 0)
         nc.gpsimd.memset(wb_s[96:P, :], 0)
         nc.vector.memset(wa_s[96:P, :], 0)
         nc.vector.memset(tab_s[:], 0)
@@ -78,14 +82,14 @@ def tile_list_kg_gate_mix_none_kernel(tc, tab_words, tab_scales, tab2_words, tab
         load_first_rows(nc.gpsimd, wb_s, wb_scales)
         load_first_rows(nc.gpsimd, wa_s, wa_scales)
         nc.gpsimd.affine_select(out=ident[:], in_=ident[:], pattern=[[-1, P]], compare_op=mybir.AluOpType.is_equal, fill=0.0, base=0, channel_multiplier=1)
-        load_scales(nc.scalar, tab2_s, tab2_scales, 0, range(0, 2))
+        load_quadrants(nc.scalar, tab2_s, tab2_scales, range(0, 2))
 
         nc.sync.dma_start(list2[:], offs2)
-        load_scales(nc.sync, tab2_s, tab2_scales, 0, range(2, 4))
-        load_last_rows(nc.sync, wb_s, wb_scales)
+        load_quadrants(nc.sync, tab2_s, tab2_scales, range(2, 4))
+        nc.sync.dma_start(list1[:], offs)
         nc.sync.dma_start(out=tab2_w[:], in_=words8(tab2_words))
         nc.sync.dma_start(out=wb_w[:], in_=wb_words[0].bitcast(I32))
-        nc.sync.dma_start(list1[:], offs)
+        load_last_rows(nc.sync, wb_s, wb_scales)
         load_scales(nc.sync, tab_s, tab_scales, TAB_ROW)
         nc.sync.dma_start(out=tab_w[:], in_=words8(tab_words))
         nc.sync.dma_start(out=wa_w[0][:], in_=words8(wa_words)[:, 0:PASS])
@@ -96,14 +100,22 @@ def tile_list_kg_gate_mix_none_kernel(tc, tab_words, tab_scales, tab2_words, tab
         load_plane(nc.sync, en8_s, en8_scales, EN8_ROW)
         load_plane(nc.sync, en4_s, en4_scales, 0)
 
+        wb_ds = keep.tile([P, PASS], U8, name="wb_ds", align_bytes=64)
+        wb_dw = keep.tile([P, 2 * PASS], U8, name="wb_dw", align_bytes=64)
+        wa_ds = keep.tile([P, PASS], U8, name="wa_ds", align_bytes=64)
+        wa_dw = keep.tile([P, PASS], I32, name="wa_dw", align_bytes=64)
+        nc.gpsimd.tensor_copy(out=wb_ds[:].rearrange("p (t m) -> p t m", t=4), in_=wb_s[:].bitcast(U8)[:, PASS:R].rearrange("p (m t) -> p t m", t=4))
+        nc.gpsimd.tensor_copy(out=wb_dw[:].rearrange("p (t m e) -> p t m e", t=4, e=2), in_=wb_w[:].bitcast(U8)[:, 2 * PASS : 2 * R].rearrange("p (m t e) -> p t m e", t=4, e=2))
+        nc.gpsimd.tensor_copy(out=wa_ds[:].rearrange("p (t m) -> p t m", t=4), in_=wa_s[:].bitcast(U8)[:, PASS:R].rearrange("p (m t) -> p t m", t=4))
+        nc.gpsimd.tensor_copy(out=wa_dw[:].rearrange("p (t m) -> p t m", t=4), in_=wa_w[1][:].rearrange("p (m t) -> p t m", t=4))
+
         v_w = keep.tile([P, J], U32, name="v_w", align_bytes=64)
         v_s = keep.tile([P, J], U8, name="v_s", align_bytes=64)
         v2_w = keep.tile([P, J], U32, name="v2_w", align_bytes=64)
         v2_s = keep.tile([P, J], U8, name="v2_s", align_bytes=64)
-        gate = {(c, b): keep.tile([P, PASS], F32, name="gate%d%d" % (c, b), tag="gate%d%d" % (c, b), align_bytes=64) for c in range(CHUNKS) for b in range(HALVES)}
-        h = {(c, b): keep.tile([P, PASS], BF16, name="h%d%d" % (c, b), align_bytes=64) for c in range(CHUNKS) for b in range(HALVES)}
-        spans = [(c, 0, 2) for c in range(CHUNKS - 1)] + [(CHUNKS - 1, 0, 1), (CHUNKS - 1, 1, 2)]
-        ht = {(c, b0): keep.tile([P, (b1 - b0) * PASS], BF16, name="ht%d%d" % (c, b0), align_bytes=64) for c, b0, b1 in spans}
+        gate = {(c, b): keep.tile([P, PASS], F32, name="gate%d%d" % (c, b), tag="gate%d%d" % (c, b), align_bytes=64) for c in range(CHUNKS) for b in range(2)}
+        h = {(c, b): keep.tile([P, PASS], BF16, name="h%d%d" % (c, b), align_bytes=64) for c in range(CHUNKS) for b in range(2)}
+        turned = [keep.tile([P, 2 * PASS], BF16, name="turned%d" % i, align_bytes=64) for i in range(2)]
         hq_s = {}
         hq_w = {}
         y_sb = keep.tile([P, CHUNKS, N // P, P], F32, name="y_sb", align_bytes=64)
@@ -111,66 +123,57 @@ def tile_list_kg_gate_mix_none_kernel(tc, tab_words, tab_scales, tab2_words, tab
         def gather(dst, window, lst, c0, c1):
             nc.vector.tensor_copy(dst[:, c0 * P : c1 * P], window.indirect(lst[:, c0 * LIST_COLS : c1 * LIST_COLS]))
 
-        def by_pair(bank):
-            return bank[:].rearrange("p (m u e) -> p u m e", u=2, e=2)
+        def bank_view(bank, b):
+            if b == 0:
+                return bank[:].rearrange("p (m u e) -> p u m e", u=2, e=2)
+            return bank[:].rearrange("p (t j) -> p j t", t=4)
+
+        def flat_view(tile, b):
+            if b == 0:
+                return tile[:].rearrange("p (u m e) -> p u m e", u=2, e=2)
+            return tile[:].rearrange("p (j t) -> p j t", t=4)
+
+        def first_product(c, b, bank, cols_w, cols_s, w_words, w_scales):
+            acc = psum.tile([P, PASS], F32, name="bank%d" % bank)
+            if b == 0:
+                nc.tensor.matmul_mx(out=acc[:], lhsT=cols_w, lhsT_scale=cols_s, rhs=w_words(0, PASS), rhs_scale=w_scales(0, PASS), start=True, stop=True)
+            else:
+                for t in range(4):
+                    nc.tensor.matmul_mx(out=acc[:, t * P : (t + 1) * P], lhsT=w_words(t * P, (t + 1) * P), lhsT_scale=w_scales(t * P, (t + 1) * P), rhs=cols_w, rhs_scale=cols_s, start=True, stop=True)
+            return acc
 
         def gate_stage(c, b, bank):
             cols = slice(c * P, (c + 1) * P)
-            if True:
-                hb = psum.tile([P, PASS], F32, name="bank%d" % bank)
-                nc.tensor.matmul_mx(
-                    out=hb[:],
-                    lhsT=v2_w[:, cols].bitcast(FP8X4),
-                    lhsT_scale=v2_s[:, cols],
-                    rhs=wb_w[:].bitcast(U8)[:, 2 * b * PASS : 2 * (b + 1) * PASS].bitcast(FP4X4),
-                    rhs_scale=wb_s[:].bitcast(U8)[:, b * PASS : (b + 1) * PASS],
-                    start=True,
-                    stop=True,
-                )
-                nc.scalar.activation(out=gate[c, b][:].rearrange("p (u m e) -> p u m e", u=2, e=2), in_=by_pair(hb), func=SIGMOID)
+            words = wb_w[:].bitcast(U8) if b == 0 else wb_dw[:]
+            scales = wb_s[:].bitcast(U8) if b == 0 else wb_ds[:]
+            hb = first_product(c, b, bank, v2_w[:, cols].bitcast(FP8X4), v2_s[:, cols], lambda lo, hi: words[:, 2 * lo : 2 * hi].bitcast(FP4X4), lambda lo, hi: scales[:, lo:hi])
+            nc.scalar.activation(out=flat_view(gate[c, b], b), in_=bank_view(hb, b), func=SIGMOID)
 
         def project_stage(c, b, bank):
             cols = slice(c * P, (c + 1) * P)
-            ha = psum.tile([P, PASS], F32, name="bank%d" % bank)
-            nc.tensor.matmul_mx(
-                out=ha[:],
-                lhsT=v_w[:, cols].bitcast(FP8X4),
-                lhsT_scale=v_s[TAB_ROW:P, cols],
-                rhs=wa_w[b][:].bitcast(FP8X4),
-                rhs_scale=wa_s[WA_ROW:P, :].bitcast(U8)[:, b * PASS : (b + 1) * PASS],
-                start=True,
-                stop=True,
-            )
-            return ha
+            words = wa_w[0][:] if b == 0 else wa_dw[:]
+            scales = wa_s[:].bitcast(U8) if b == 0 else wa_ds[:]
+            return first_product(c, b, bank, v_w[:, cols].bitcast(FP8X4), v_s[TAB_ROW:P, cols], lambda lo, hi: words[:, lo:hi].bitcast(FP8X4), lambda lo, hi: scales[:, lo:hi])
 
         def product_stage(c, b, ha):
-            nc.vector.tensor_tensor(
-                out=h[c, b][:].rearrange("p (u m e) -> p u m e", u=2, e=2),
-                in0=by_pair(ha),
-                in1=gate[c, b][:].rearrange("p (u m e) -> p u m e", u=2, e=2),
-                op=MULT,
-            )
+            nc.vector.tensor_tensor(out=flat_view(h[c, b], b), in0=bank_view(ha, b), in1=flat_view(gate[c, b], b), op=MULT)
 
-        def turn_stage(c, b0, b1, bank):
-            nb = b1 - b0
-            xt = psum.tile([P, HALVES, 2, P], F32, name="bank%d" % bank)
-            for b in range(b0, b1):
-                pairs = h[c, b][:].bitcast(F32)
+        def turn_stage(i, bank):
+            xt = psum.tile([P, 2, 2, P], F32, name="bank%d" % bank)
+            for a in range(2):
+                pairs = h[2 * i + a, 0][:].bitcast(F32)
                 for u in range(2):
-                    nc.tensor.transpose(xt[:, b, u, :], pairs[:, u * P : (u + 1) * P], ident[:])
-            nc.scalar.copy(
-                out=ht[c, b0][:].bitcast(F32).rearrange("p (b j u) -> p b j u", b=nb, u=2),
-                in_=xt[:, b0:b1, :, :].rearrange("p b u j -> p b j u"),
-            )
+                    nc.tensor.transpose(xt[:, a, u, :], pairs[:, u * P : (u + 1) * P], ident[:])
+            nc.scalar.copy(out=turned[i][:].bitcast(F32).rearrange("p (a j u) -> p a j u", a=2, u=2), in_=xt[:].rearrange("p a u j -> p a j u"))
 
-        def quant_stage(c, b0, b1, tag):
-            nb = b1 - b0
-            words = keep.tile([P, nb * P], U32, name="hq_w%d%d" % (c, b0), tag=tag, align_bytes=64)
-            plane = keep.tile([P, nb * P], U8, name="hq_s%d%d" % (c, b0), align_bytes=64)
-            nc.vector.quantize_mx(out=words[:].bitcast(FP8X4), scales=plane[:], in_=ht[c, b0][:])
-            for b in range(b0, b1):
-                hq_w[c, b] = words[:, (b - b0) * P : (b - b0 + 1) * P]
-                hq_s[c, b] = plane[:, (b - b0) * P : (b - b0 + 1) * P]
+        def quant_stage(source, units, tag):
+            width = len(units) * P
+            words = keep.tile([P, width], U32, name="hq_w%d%d" % units[0], tag=tag, align_bytes=64)
+            plane = keep.tile([P, width], U8, name="hq_s%d%d" % units[0], align_bytes=64)
+            nc.vector.quantize_mx(out=words[:].bitcast(FP8X4), scales=plane[:], in_=source[:])
+            for i, unit in enumerate(units):
+                hq_w[unit] = words[:, i * P : (i + 1) * P]
+                hq_s[unit] = plane[:, i * P : (i + 1) * P]
 
         def score_pass(c, nt, b, dst):
             if b == 0:
@@ -186,13 +189,13 @@ def tile_list_kg_gate_mix_none_kernel(tc, tab_words, tab_scales, tab2_words, tab
             if c < CHUNKS - 1:
                 bank = psum.tile([P, N // P, P], F32, name="bank%d" % bks[0])
                 for nt in range(N // P):
-                    for b in range(HALVES):
+                    for b in range(2):
                         score_pass(c, nt, b, bank[:, nt, :])
                 nc.scalar.copy(out=y_sb[:, c, :, :], in_=bank[:])
                 nc.sync.dma_start(out=out.rearrange("(a p) j -> p a j", p=P)[:, :, cols], in_=y_sb[:, c, :, :])
             else:
                 banks = [psum.tile([P, P], F32, name="bank%d" % bks[nt]) for nt in range(N // P)]
-                for b in range(HALVES):
+                for b in range(2):
                     for nt in range(N // P):
                         score_pass(c, nt, b, banks[nt][:])
                 nc.vector.tensor_copy(out=y_sb[:, c, 0, :], in_=banks[0][:])
@@ -206,34 +209,36 @@ def tile_list_kg_gate_mix_none_kernel(tc, tab_words, tab_scales, tab2_words, tab
         gather(v_s, tab_s[:].bitcast(U8), list1, 0, CHUNKS)
         gather(v_w, tab_w[:].bitcast(U32), list1, 0, 2)
         gather(v_w, tab_w[:].bitcast(U32), list1, 2, CHUNKS)
-        last = CHUNKS - 1
-        units = [(0, 0), (1, 0), (0, 1), (1, 1), (2, 0), (2, 1), (3, 0), (3, 1)]
-        gate_bank = [0, 1, 2, 3, 4, 5, 6, 7]
-        proj_bank = [5, 6, 7, 0, 1, 2, 0, 5]
-        turn_bank = {2: 3, 3: 4, 5: 1, 6: 2, 7: 6}
-        for i in (0, 2, 1, 3, 4):
-            gate_stage(*units[i], gate_bank[i])
-        sums = {}
-        for i in range(4):
-            sums[i] = project_stage(*units[i], proj_bank[i])
-        for i, (c, b) in enumerate(units):
-            product_stage(c, b, sums[i])
-            if i + 5 < len(units):
-                gate_stage(*units[i + 5], gate_bank[i + 5])
-            ahead = {0: 4, 1: 5, 3: 6, 4: 7}
-            if i in ahead:
-                sums[ahead[i]] = project_stage(*units[ahead[i]], proj_bank[ahead[i]])
-            if c == last:
-                turn_stage(c, b, b + 1, turn_bank[i])
-            elif b == 1:
-                turn_stage(c, 0, 2, turn_bank[i])
-            if i == 5:
-                quant_stage(0, 0, 2, "gate%d%d" % units[i])
-                score_stage(0, [3])
-        quant_stage(1, 0, 2, "gate31")
-        quant_stage(2, 0, 2, "hq2")
-        quant_stage(last, 0, 1, "hq30")
-        quant_stage(last, 1, 2, "hq31")
-        score_stage(1, [4])
-        score_stage(2, [7])
-        score_stage(3, [0, 5])
+        for c in range(CHUNKS):
+            gate_stage(c, 0, c)
+        gate_stage(0, 1, 4)
+        ha = {}
+        for c in range(CHUNKS):
+            ha[c, 0] = project_stage(c, 0, [5, 6, 7, 0][c])
+        product_stage(0, 0, ha[0, 0])
+        gate_stage(1, 1, 5)
+        product_stage(1, 0, ha[1, 0])
+        ha[0, 1] = project_stage(0, 1, 1)
+        gate_stage(2, 1, 6)
+        turn_stage(0, 4)
+        product_stage(2, 0, ha[2, 0])
+        ha[1, 1] = project_stage(1, 1, 2)
+        gate_stage(3, 1, 7)
+        product_stage(3, 0, ha[3, 0])
+        ha[2, 1] = project_stage(2, 1, 3)
+        ha[3, 1] = project_stage(3, 1, 0)
+        turn_stage(1, 5)
+        product_stage(0, 1, ha[0, 1])
+        product_stage(1, 1, ha[1, 1])
+        quant_stage(h[0, 1], [(0, 1)], "hq01")
+        product_stage(2, 1, ha[2, 1])
+        quant_stage(turned[0], [(0, 0), (1, 0)], "hqa")
+        score_stage(0, [6])
+        product_stage(3, 1, ha[3, 1])
+        quant_stage(h[1, 1], [(1, 1)], "hq11")
+        score_stage(1, [1])
+        quant_stage(turned[1], [(2, 0), (3, 0)], "hqb")
+        quant_stage(h[2, 1], [(2, 1)], "hq21")
+        score_stage(2, [4])
+        quant_stage(h[3, 1], [(3, 1)], "hq31")
+        score_stage(3, [2, 7])

@@ -29,12 +29,6 @@ def load_scales(queue, plane, scales, first_row, quadrants=range(4)):
         queue.dma_start(out=plane[32 * q + first_row : 32 * q + first_row + 4, :], in_=rows[4 * q : 4 * q + 4, :])
 
 
-def load_quadrants(queue, plane, scales, quadrants):
-    rows = scales[0].bitcast(I32)
-    for q in quadrants:
-        queue.dma_start(out=plane[32 * q : 32 * q + 32, :], in_=rows[4 * q : 4 * q + 4, :].partition_broadcast(8))
-
-
 def load_plane(queue, plane, scales, first_row):
     rows = scales[0].bitcast(I32)
     queue.dma_start(out=plane[first_row : first_row + 98, :], in_=rows[0:14, :].partition_broadcast(7))
@@ -75,25 +69,26 @@ def tile_list_kg_gate_mix_none_kernel(tc, tab_words, tab_scales, tab2_words, tab
         en4_w = keep.tile([P, N // 2], I32, name="en4_w", align_bytes=64)
         ident = keep.tile([P, P], F32, name="ident", align_bytes=64)
 
+        nc.vector.memset(tab2_s[:], 0)
         nc.gpsimd.memset(wb_s[96:P, :], 0)
+        nc.vector.memset(ident[:], 1.0)
         nc.vector.memset(wa_s[96:P, :], 0)
         nc.vector.memset(tab_s[:], 0)
-        nc.vector.memset(ident[:], 1.0)
         load_first_rows(nc.gpsimd, wb_s, wb_scales)
-        load_first_rows(nc.gpsimd, wa_s, wa_scales)
         nc.gpsimd.affine_select(out=ident[:], in_=ident[:], pattern=[[-1, P]], compare_op=mybir.AluOpType.is_equal, fill=0.0, base=0, channel_multiplier=1)
-        load_quadrants(nc.scalar, tab2_s, tab2_scales, range(0, 2))
+        load_first_rows(nc.gpsimd, wa_s, wa_scales)
+        load_scales(nc.scalar, tab2_s, tab2_scales, 0, range(0, 2))
 
         nc.sync.dma_start(list2[:], offs2)
-        load_quadrants(nc.sync, tab2_s, tab2_scales, range(2, 4))
-        nc.sync.dma_start(list1[:], offs)
-        nc.sync.dma_start(out=tab2_w[:], in_=words8(tab2_words))
         nc.sync.dma_start(out=wb_w[:], in_=wb_words[0].bitcast(I32))
+        load_scales(nc.sync, tab2_s, tab2_scales, 0, range(2, 4))
         load_last_rows(nc.sync, wb_s, wb_scales)
+        nc.sync.dma_start(out=tab2_w[:], in_=words8(tab2_words))
+        nc.sync.dma_start(list1[:], offs)
         load_scales(nc.sync, tab_s, tab_scales, TAB_ROW)
         nc.sync.dma_start(out=tab_w[:], in_=words8(tab_words))
-        nc.sync.dma_start(out=wa_w[0][:], in_=words8(wa_words)[:, 0:PASS])
         load_last_rows(nc.sync, wa_s, wa_scales)
+        nc.sync.dma_start(out=wa_w[0][:], in_=words8(wa_words)[:, 0:PASS])
         nc.sync.dma_start(out=wa_w[1][:], in_=words8(wa_words)[:, PASS:R])
         nc.sync.dma_start(out=en8_w[:], in_=words8(en8_words))
         nc.sync.dma_start(out=en4_w[:], in_=en4_words[0].bitcast(I32))

@@ -71,11 +71,10 @@ def tile_list_kg_gate_mix_none_kernel(tc, tab_words, tab_scales, tab2_words, tab
 
         nc.vector.memset(tab2_s[:], 0)
         nc.gpsimd.memset(wb_s[96:P, :], 0)
-        nc.vector.memset(ident[:], 1.0)
         nc.vector.memset(wa_s[96:P, :], 0)
         nc.vector.memset(tab_s[:], 0)
+        nc.vector.memset(ident[:], 1.0)
         load_first_rows(nc.gpsimd, wb_s, wb_scales)
-        nc.gpsimd.affine_select(out=ident[:], in_=ident[:], pattern=[[-1, P]], compare_op=mybir.AluOpType.is_equal, fill=0.0, base=0, channel_multiplier=1)
         load_first_rows(nc.gpsimd, wa_s, wa_scales)
         load_scales(nc.scalar, tab2_s, tab2_scales, 0, range(0, 2))
 
@@ -84,12 +83,12 @@ def tile_list_kg_gate_mix_none_kernel(tc, tab_words, tab_scales, tab2_words, tab
         load_scales(nc.sync, tab2_s, tab2_scales, 0, range(2, 4))
         load_last_rows(nc.sync, wb_s, wb_scales)
         nc.sync.dma_start(out=tab2_w[:], in_=words8(tab2_words))
+        nc.sync.dma_start(out=wa_w[1][:], in_=words8(wa_words)[:, PASS:R])
         nc.sync.dma_start(list1[:], offs)
         load_scales(nc.sync, tab_s, tab_scales, TAB_ROW)
         nc.sync.dma_start(out=tab_w[:], in_=words8(tab_words))
-        load_last_rows(nc.sync, wa_s, wa_scales)
         nc.sync.dma_start(out=wa_w[0][:], in_=words8(wa_words)[:, 0:PASS])
-        nc.sync.dma_start(out=wa_w[1][:], in_=words8(wa_words)[:, PASS:R])
+        load_last_rows(nc.sync, wa_s, wa_scales)
         nc.sync.dma_start(out=en8_w[:], in_=words8(en8_words))
         nc.sync.dma_start(out=en4_w[:], in_=en4_words[0].bitcast(I32))
         load_plane(nc.sync, en8_s, en8_scales, EN8_ROW)
@@ -99,21 +98,24 @@ def tile_list_kg_gate_mix_none_kernel(tc, tab_words, tab_scales, tab2_words, tab
         wb_dw = keep.tile([P, 2 * PASS], U8, name="wb_dw", align_bytes=64)
         wa_ds = keep.tile([P, PASS], U8, name="wa_ds", align_bytes=64)
         wa_dw = keep.tile([P, PASS], I32, name="wa_dw", align_bytes=64)
-        nc.gpsimd.tensor_copy(out=wb_ds[:].rearrange("p (t m) -> p t m", t=4), in_=wb_s[:].bitcast(U8)[:, PASS:R].rearrange("p (m t) -> p t m", t=4))
         nc.gpsimd.tensor_copy(out=wb_dw[:].rearrange("p (t m e) -> p t m e", t=4, e=2), in_=wb_w[:].bitcast(U8)[:, 2 * PASS : 2 * R].rearrange("p (m t e) -> p t m e", t=4, e=2))
-        nc.gpsimd.tensor_copy(out=wa_ds[:].rearrange("p (t m) -> p t m", t=4), in_=wa_s[:].bitcast(U8)[:, PASS:R].rearrange("p (m t) -> p t m", t=4))
+        nc.gpsimd.tensor_copy(out=wb_ds[:].rearrange("p (t m) -> p t m", t=4), in_=wb_s[:].bitcast(U8)[:, PASS:R].rearrange("p (m t) -> p t m", t=4))
         nc.gpsimd.tensor_copy(out=wa_dw[:].rearrange("p (t m) -> p t m", t=4), in_=wa_w[1][:].rearrange("p (m t) -> p t m", t=4))
+        nc.gpsimd.tensor_copy(out=wa_ds[:].rearrange("p (t m) -> p t m", t=4), in_=wa_s[:].bitcast(U8)[:, PASS:R].rearrange("p (m t) -> p t m", t=4))
+        nc.gpsimd.affine_select(out=ident[:], in_=ident[:], pattern=[[-1, P]], compare_op=mybir.AluOpType.is_equal, fill=0.0, base=0, channel_multiplier=1)
 
         v_w = keep.tile([P, J], U32, name="v_w", align_bytes=64)
         v_s = keep.tile([P, J], U8, name="v_s", align_bytes=64)
         v2_w = keep.tile([P, J], U32, name="v2_w", align_bytes=64)
         v2_s = keep.tile([P, J], U8, name="v2_s", align_bytes=64)
         gate = {(c, b): keep.tile([P, PASS], F32, name="gate%d%d" % (c, b), tag="gate%d%d" % (c, b), align_bytes=64) for c in range(CHUNKS) for b in range(2)}
-        h = {(c, b): keep.tile([P, PASS], BF16, name="h%d%d" % (c, b), align_bytes=64) for c in range(CHUNKS) for b in range(2)}
-        turned = [keep.tile([P, 2 * PASS], BF16, name="turned%d" % i, align_bytes=64) for i in range(2)]
+        h = {(c, 0): keep.tile([P, PASS], BF16, name="h%d0" % c, align_bytes=64) for c in range(CHUNKS)}
+        h_pair = [keep.tile([P, 2 * PASS], BF16, name="h_pair%d" % i, align_bytes=64) for i in range(2)]
+        for c in range(CHUNKS):
+            h[c, 1] = h_pair[c // 2][:, (c % 2) * PASS : (c % 2 + 1) * PASS]
+        turned = {c: keep.tile([P, n * PASS], BF16, name="turned%d" % c, align_bytes=64) for c, n in ((0, 2), (2, 1), (3, 1))}
         hq_s = {}
         hq_w = {}
-        y_sb = keep.tile([P, CHUNKS, N // P, P], F32, name="y_sb", align_bytes=64)
 
         def gather(dst, window, lst, c0, c1):
             nc.vector.tensor_copy(dst[:, c0 * P : c1 * P], window.indirect(lst[:, c0 * LIST_COLS : c1 * LIST_COLS]))
@@ -151,89 +153,104 @@ def tile_list_kg_gate_mix_none_kernel(tc, tab_words, tab_scales, tab2_words, tab
             return first_product(c, b, bank, v_w[:, cols].bitcast(FP8X4), v_s[TAB_ROW:P, cols], lambda lo, hi: words[:, lo:hi].bitcast(FP8X4), lambda lo, hi: scales[:, lo:hi])
 
         def product_stage(c, b, ha):
-            nc.vector.tensor_tensor(out=flat_view(h[c, b], b), in0=bank_view(ha, b), in1=flat_view(gate[c, b], b), op=MULT)
+            nc.vector.tensor_tensor(out=flat_view(h[c, b], b), in0=flat_view(gate[c, b], b), in1=bank_view(ha, b), op=MULT)
 
-        def turn_stage(i, bank):
+        def product_on_gpsimd(c, ha):
+            ha_sb = keep.tile([P, PASS], F32, name="ha_sb%d" % c, align_bytes=64)
+            nc.scalar.copy(out=flat_view(ha_sb, 0), in_=bank_view(ha, 0))
+            nc.gpsimd.tensor_tensor(out=h[c, 0][:], in0=ha_sb[:], in1=gate[c, 0][:], op=MULT)
+
+        def turn_stage(chunks, bank):
             xt = psum.tile([P, 2, 2, P], F32, name="bank%d" % bank)
-            for a in range(2):
-                pairs = h[2 * i + a, 0][:].bitcast(F32)
+            for a, c in enumerate(chunks):
+                pairs = h[c, 0][:].bitcast(F32)
                 for u in range(2):
                     nc.tensor.transpose(xt[:, a, u, :], pairs[:, u * P : (u + 1) * P], ident[:])
-            nc.scalar.copy(out=turned[i][:].bitcast(F32).rearrange("p (a j u) -> p a j u", a=2, u=2), in_=xt[:].rearrange("p a u j -> p a j u"))
+            return xt
+
+        def weave(dst, xt, a0, a1):
+            nc.scalar.copy(out=dst[:].bitcast(F32).rearrange("p (a j u) -> p a j u", a=a1 - a0, u=2), in_=xt[:, a0:a1, :, :].rearrange("p a u j -> p a j u"))
 
         def quant_stage(source, units, tag):
             width = len(units) * P
             words = keep.tile([P, width], U32, name="hq_w%d%d" % units[0], tag=tag, align_bytes=64)
             plane = keep.tile([P, width], U8, name="hq_s%d%d" % units[0], align_bytes=64)
-            nc.vector.quantize_mx(out=words[:].bitcast(FP8X4), scales=plane[:], in_=source[:])
+            nc.vector.quantize_mx(out=words[:].bitcast(FP8X4), scales=plane[:], in_=source[:, :])
             for i, unit in enumerate(units):
                 hq_w[unit] = words[:, i * P : (i + 1) * P]
                 hq_s[unit] = plane[:, i * P : (i + 1) * P]
+            return words[:], plane[:]
 
-        def score_pass(c, nt, b, dst):
+        def score_pass(dst, nt, b, words, plane, start, stop):
             if b == 0:
-                words = en8_w[:, nt * P : (nt + 1) * P].bitcast(FP8X4)
-                scales = en8_s[EN8_ROW:P, :].bitcast(U8)[:, nt * P : (nt + 1) * P]
+                en_words = en8_w[:, nt * P : (nt + 1) * P].bitcast(FP8X4)
+                en_scales = en8_s[EN8_ROW:P, :].bitcast(U8)[:, nt * P : (nt + 1) * P]
             else:
-                words = en4_w[:].bitcast(U8)[:, 2 * nt * P : 2 * (nt + 1) * P].bitcast(FP4X4)
-                scales = en4_s[:].bitcast(U8)[:, nt * P : (nt + 1) * P]
-            nc.tensor.matmul_mx(out=dst, lhsT=words, lhsT_scale=scales, rhs=hq_w[c, b].bitcast(FP8X4), rhs_scale=hq_s[c, b], start=(b == 0), stop=(b == 1))
+                en_words = en4_w[:].bitcast(U8)[:, 2 * nt * P : 2 * (nt + 1) * P].bitcast(FP4X4)
+                en_scales = en4_s[:].bitcast(U8)[:, nt * P : (nt + 1) * P]
+            nc.tensor.matmul_mx(out=dst, lhsT=en_words, lhsT_scale=en_scales, rhs=words.bitcast(FP8X4), rhs_scale=plane, start=start, stop=stop)
 
-        def score_stage(c, bks):
-            cols = slice(c * P, (c + 1) * P)
-            if c < CHUNKS - 1:
-                bank = psum.tile([P, N // P, P], F32, name="bank%d" % bks[0])
-                for nt in range(N // P):
-                    for b in range(2):
-                        score_pass(c, nt, b, bank[:, nt, :])
-                nc.scalar.copy(out=y_sb[:, c, :, :], in_=bank[:])
-                nc.sync.dma_start(out=out.rearrange("(a p) j -> p a j", p=P)[:, :, cols], in_=y_sb[:, c, :, :])
-            else:
-                banks = [psum.tile([P, P], F32, name="bank%d" % bks[nt]) for nt in range(N // P)]
-                for b in range(2):
-                    for nt in range(N // P):
-                        score_pass(c, nt, b, banks[nt][:])
-                nc.vector.tensor_copy(out=y_sb[:, c, 0, :], in_=banks[0][:])
-                nc.sync.dma_start(out=out[0:P, cols], in_=y_sb[:, c, 0, :])
-                nc.scalar.copy(out=y_sb[:, c, 1, :], in_=banks[1][:])
-                nc.scalar.dma_start(out=out[P : 2 * P, cols], in_=y_sb[:, c, 1, :])
+        def store(engine_copy, queue, name, bank, dst):
+            y = keep.tile(list(bank.shape), F32, name=name, align_bytes=64)
+            engine_copy(out=y[:], in_=bank)
+            queue.dma_start(out=dst, in_=y[:])
 
         gather(v2_s, tab2_s[:].bitcast(U8), list2, 0, CHUNKS)
         gather(v2_w, tab2_w[:].bitcast(U32), list2, 0, 1)
         gather(v2_w, tab2_w[:].bitcast(U32), list2, 1, CHUNKS)
         gather(v_s, tab_s[:].bitcast(U8), list1, 0, CHUNKS)
-        gather(v_w, tab_w[:].bitcast(U32), list1, 0, 2)
-        gather(v_w, tab_w[:].bitcast(U32), list1, 2, CHUNKS)
+        gather(v_w, tab_w[:].bitcast(U32), list1, 0, 1)
+        gather(v_w, tab_w[:].bitcast(U32), list1, 3, 4)
+        gather(v_w, tab_w[:].bitcast(U32), list1, 1, 3)
         for c in range(CHUNKS):
             gate_stage(c, 0, c)
         gate_stage(0, 1, 4)
         ha = {}
-        for c in range(CHUNKS):
-            ha[c, 0] = project_stage(c, 0, [5, 6, 7, 0][c])
-        product_stage(0, 0, ha[0, 0])
-        gate_stage(1, 1, 5)
-        product_stage(1, 0, ha[1, 0])
+        for c, bank in ((0, 5), (3, 6), (1, 7), (2, 0)):
+            ha[c, 0] = project_stage(c, 0, bank)
+        product_on_gpsimd(3, ha[3, 0])
+        for c in (0, 1, 2):
+            product_stage(c, 0, ha[c, 0])
         ha[0, 1] = project_stage(0, 1, 1)
+        gate_stage(1, 1, 5)
         gate_stage(2, 1, 6)
-        turn_stage(0, 4)
-        product_stage(2, 0, ha[2, 0])
         ha[1, 1] = project_stage(1, 1, 2)
         gate_stage(3, 1, 7)
-        product_stage(3, 0, ha[3, 0])
         ha[2, 1] = project_stage(2, 1, 3)
-        ha[3, 1] = project_stage(3, 1, 0)
-        turn_stage(1, 5)
+        ha[3, 1] = project_stage(3, 1, 4)
+        xa = turn_stage([0, 1], 0)
+        xb = turn_stage([2, 3], 5)
+        weave(turned[0], xa, 0, 2)
+        weave(turned[2], xb, 0, 1)
+        weave(turned[3], xb, 1, 2)
         product_stage(0, 1, ha[0, 1])
         product_stage(1, 1, ha[1, 1])
-        quant_stage(h[0, 1], [(0, 1)], "hq01")
         product_stage(2, 1, ha[2, 1])
-        quant_stage(turned[0], [(0, 0), (1, 0)], "hqa")
-        score_stage(0, [6])
+        quant_stage(h_pair[0], [(0, 1), (1, 1)], "hq01")
         product_stage(3, 1, ha[3, 1])
-        quant_stage(h[1, 1], [(1, 1)], "hq11")
-        score_stage(1, [1])
-        quant_stage(turned[1], [(2, 0), (3, 0)], "hqb")
         quant_stage(h[2, 1], [(2, 1)], "hq21")
-        score_stage(2, [4])
+        y01 = [psum.tile([P, 2 * P], F32, name="bank%d" % bk) for bk in (6, 1)]
+        for c in range(2):
+            for nt in range(2):
+                score_pass(y01[nt][:, c * P : (c + 1) * P], nt, 1, hq_w[c, 1], hq_s[c, 1], c == 0, False)
+        pair_w, pair_s = quant_stage(turned[0], [(0, 0), (1, 0)], "hqa")
         quant_stage(h[3, 1], [(3, 1)], "hq31")
-        score_stage(3, [2, 7])
+        y2 = [psum.tile([P, P], F32, name="bank%d" % bk) for bk in (2, 7)]
+        for nt in range(2):
+            score_pass(y2[nt][:], nt, 1, hq_w[2, 1], hq_s[2, 1], True, False)
+        for nt in range(2):
+            score_pass(y01[nt][:], nt, 0, pair_w, pair_s, False, True)
+        for nt in range(2):
+            store(nc.scalar.copy, nc.sync, "y01%d" % nt, y01[nt][:], out[nt * P : (nt + 1) * P, 0 : 2 * P])
+        y3 = [psum.tile([P, P], F32, name="bank%d" % bk) for bk in (3, 4)]
+        for nt in range(2):
+            score_pass(y3[nt][:], nt, 1, hq_w[3, 1], hq_s[3, 1], True, False)
+        quant_stage(turned[2], [(2, 0)], "hq20")
+        quant_stage(turned[3], [(3, 0)], "hq30")
+        for nt in range(2):
+            score_pass(y2[nt][:], nt, 0, hq_w[2, 0], hq_s[2, 0], False, True)
+        for nt in range(2):
+            score_pass(y3[nt][:], nt, 0, hq_w[3, 0], hq_s[3, 0], False, True)
+        for c, y in ((2, y2), (3, y3)):
+            store(nc.vector.tensor_copy, nc.sync, "y%d0" % c, y[0][:], out[0:P, c * P : (c + 1) * P])
+            store(nc.scalar.copy, nc.sync if c == 2 else nc.scalar, "y%d1" % c, y[1][:], out[P : 2 * P, c * P : (c + 1) * P])

@@ -77,11 +77,11 @@ def tile_list_kg_gate_mix_none_kernel(tc, tab_words, tab_scales, tab2_words, tab
         load_first_rows(nc.gpsimd, wb_s, wb_scales)
         load_first_rows(nc.gpsimd, wa_s, wa_scales)
         load_scales(nc.scalar, tab2_s, tab2_scales, 0, range(0, 2))
+        load_last_rows(nc.scalar, wb_s, wb_scales)
 
-        nc.sync.dma_start(list2[:], offs2)
         nc.sync.dma_start(out=wb_w[:], in_=wb_words[0].bitcast(I32))
+        nc.sync.dma_start(list2[:], offs2)
         load_scales(nc.sync, tab2_s, tab2_scales, 0, range(2, 4))
-        load_last_rows(nc.sync, wb_s, wb_scales)
         nc.sync.dma_start(out=tab2_w[:], in_=words8(tab2_words))
         nc.sync.dma_start(out=wa_w[1][:], in_=words8(wa_words)[:, PASS:R])
         nc.sync.dma_start(list1[:], offs)
@@ -160,16 +160,12 @@ def tile_list_kg_gate_mix_none_kernel(tc, tab_words, tab_scales, tab2_words, tab
             nc.scalar.copy(out=flat_view(ha_sb, 0), in_=bank_view(ha, 0))
             nc.gpsimd.tensor_tensor(out=h[c, 0][:], in0=ha_sb[:], in1=gate[c, 0][:], op=MULT)
 
-        def turn_stage(chunks, bank):
-            xt = psum.tile([P, 2, 2, P], F32, name="bank%d" % bank)
-            for a, c in enumerate(chunks):
-                pairs = h[c, 0][:].bitcast(F32)
-                for u in range(2):
-                    nc.tensor.transpose(xt[:, a, u, :], pairs[:, u * P : (u + 1) * P], ident[:])
-            return xt
-
-        def weave(dst, xt, a0, a1):
-            nc.scalar.copy(out=dst[:].bitcast(F32).rearrange("p (a j u) -> p a j u", a=a1 - a0, u=2), in_=xt[:, a0:a1, :, :].rearrange("p a u j -> p a j u"))
+        def turn_stage(c, bank, dst):
+            xt = psum.tile([P, 2, P], F32, name="bank%d" % bank)
+            pairs = h[c, 0][:].bitcast(F32)
+            for u in range(2):
+                nc.tensor.transpose(xt[:, u, :], pairs[:, u * P : (u + 1) * P], ident[:])
+            nc.scalar.copy(out=dst.bitcast(F32).rearrange("p (j u) -> p j u", u=2), in_=xt[:].rearrange("p u j -> p j u"))
 
         def quant_stage(source, units, tag):
             width = len(units) * P
@@ -217,40 +213,31 @@ def tile_list_kg_gate_mix_none_kernel(tc, tab_words, tab_scales, tab2_words, tab
         ha[1, 1] = project_stage(1, 1, 2)
         gate_stage(3, 1, 7)
         ha[2, 1] = project_stage(2, 1, 3)
+        turn_stage(0, 0, turned[0][:, 0:PASS])
+        turn_stage(1, 5, turned[0][:, PASS : 2 * PASS])
         ha[3, 1] = project_stage(3, 1, 4)
-        xa = turn_stage([0, 1], 0)
-        xb = turn_stage([2, 3], 5)
-        weave(turned[0], xa, 0, 2)
-        weave(turned[2], xb, 0, 1)
-        weave(turned[3], xb, 1, 2)
-        product_stage(0, 1, ha[0, 1])
-        product_stage(1, 1, ha[1, 1])
-        product_stage(2, 1, ha[2, 1])
+        turn_stage(2, 6, turned[2][:])
+        turn_stage(3, 7, turned[3][:])
+        for c in range(3):
+            product_stage(c, 1, ha[c, 1])
         quant_stage(h_pair[0], [(0, 1), (1, 1)], "hq01")
+        pair_w, pair_s = quant_stage(turned[0], [(0, 0), (1, 0)], "hqa")
         product_stage(3, 1, ha[3, 1])
-        quant_stage(h[2, 1], [(2, 1)], "hq21")
-        y01 = [psum.tile([P, 2 * P], F32, name="bank%d" % bk) for bk in (6, 1)]
+        y01 = [psum.tile([P, 2 * P], F32, name="bank%d" % bk) for bk in (1, 2)]
         for c in range(2):
             for nt in range(2):
                 score_pass(y01[nt][:, c * P : (c + 1) * P], nt, 1, hq_w[c, 1], hq_s[c, 1], c == 0, False)
-        pair_w, pair_s = quant_stage(turned[0], [(0, 0), (1, 0)], "hqa")
-        quant_stage(h[3, 1], [(3, 1)], "hq31")
-        y2 = [psum.tile([P, P], F32, name="bank%d" % bk) for bk in (2, 7)]
-        for nt in range(2):
-            score_pass(y2[nt][:], nt, 1, hq_w[2, 1], hq_s[2, 1], True, False)
         for nt in range(2):
             score_pass(y01[nt][:], nt, 0, pair_w, pair_s, False, True)
         for nt in range(2):
             store(nc.scalar.copy, nc.sync, "y01%d" % nt, y01[nt][:], out[nt * P : (nt + 1) * P, 0 : 2 * P])
-        y3 = [psum.tile([P, P], F32, name="bank%d" % bk) for bk in (3, 4)]
-        for nt in range(2):
-            score_pass(y3[nt][:], nt, 1, hq_w[3, 1], hq_s[3, 1], True, False)
-        quant_stage(turned[2], [(2, 0)], "hq20")
-        quant_stage(turned[3], [(3, 0)], "hq30")
-        for nt in range(2):
-            score_pass(y2[nt][:], nt, 0, hq_w[2, 0], hq_s[2, 0], False, True)
-        for nt in range(2):
-            score_pass(y3[nt][:], nt, 0, hq_w[3, 0], hq_s[3, 0], False, True)
-        for c, y in ((2, y2), (3, y3)):
+        for c, banks in ((2, (3, 0)), (3, (4, 5))):
+            quant_stage(h[c, 1], [(c, 1)], "hq%d1" % c)
+            quant_stage(turned[c], [(c, 0)], "hq%d0" % c)
+        for c, banks in ((2, (3, 0)), (3, (4, 5))):
+            y = [psum.tile([P, P], F32, name="bank%d" % bk) for bk in banks]
+            for b in (1, 0):
+                for nt in range(2):
+                    score_pass(y[nt][:], nt, b, hq_w[c, b], hq_s[c, b], b == 1, b == 0)
             store(nc.vector.tensor_copy, nc.sync, "y%d0" % c, y[0][:], out[0:P, c * P : (c + 1) * P])
             store(nc.scalar.copy, nc.sync if c == 2 else nc.scalar, "y%d1" % c, y[1][:], out[P : 2 * P, c * P : (c + 1) * P])

@@ -59,7 +59,8 @@ def tile_list_kg_gate_mix_none_kernel(tc, tab_words, tab_scales, tab2_words, tab
         tab2_w = keep.tile([P, T], I32, name="tab2_w", align_bytes=64)
         tab_s = keep.tile([P, T // 4], I32, name="tab_s", align_bytes=64)
         tab2_s = keep.tile([P, T // 4], I32, name="tab2_s", align_bytes=64)
-        wa_w = [keep.tile([P, PASS], I32, name="wa_w%d" % b, align_bytes=64) for b in range(2)]
+        wa_w = [keep.tile([P, PASS], I32, name="wa_w0", align_bytes=64)]
+        wa_piece = [keep.tile([P, PASS // 2], I32, name="wa_piece%d" % i, align_bytes=64) for i in range(2)]
         wb_w = keep.tile([P, R // 2], I32, name="wb_w", align_bytes=64)
         wb_s = keep.tile([P, R // 4], I32, name="wb_s", align_bytes=64)
         wa_s = keep.tile([P, R // 4], I32, name="wa_s", align_bytes=64)
@@ -83,12 +84,13 @@ def tile_list_kg_gate_mix_none_kernel(tc, tab_words, tab_scales, tab2_words, tab
         nc.sync.dma_start(list2[:], offs2)
         load_scales(nc.sync, tab2_s, tab2_scales, 0, range(2, 4))
         nc.sync.dma_start(out=tab2_w[:], in_=words8(tab2_words))
-        nc.sync.dma_start(out=wa_w[1][:], in_=words8(wa_words)[:, PASS:R])
+        nc.sync.dma_start(out=wa_piece[0][:], in_=words8(wa_words)[:, PASS : PASS + PASS // 2])
         nc.sync.dma_start(list1[:], offs)
         load_scales(nc.sync, tab_s, tab_scales, TAB_ROW)
         nc.sync.dma_start(out=tab_w[:], in_=words8(tab_words))
-        nc.sync.dma_start(out=wa_w[0][:], in_=words8(wa_words)[:, 0:PASS])
         load_last_rows(nc.sync, wa_s, wa_scales)
+        nc.sync.dma_start(out=wa_w[0][:], in_=words8(wa_words)[:, 0:PASS])
+        nc.sync.dma_start(out=wa_piece[1][:], in_=words8(wa_words)[:, PASS + PASS // 2 : R])
         nc.sync.dma_start(out=en8_w[:], in_=words8(en8_words))
         nc.sync.dma_start(out=en4_w[:], in_=en4_words[0].bitcast(I32))
         load_plane(nc.sync, en8_s, en8_scales, EN8_ROW)
@@ -100,8 +102,9 @@ def tile_list_kg_gate_mix_none_kernel(tc, tab_words, tab_scales, tab2_words, tab
         wa_dw = keep.tile([P, PASS], I32, name="wa_dw", align_bytes=64)
         nc.gpsimd.tensor_copy(out=wb_dw[:].rearrange("p (t m e) -> p t m e", t=4, e=2), in_=wb_w[:].bitcast(U8)[:, 2 * PASS : 2 * R].rearrange("p (m t e) -> p t m e", t=4, e=2))
         nc.gpsimd.tensor_copy(out=wb_ds[:].rearrange("p (t m) -> p t m", t=4), in_=wb_s[:].bitcast(U8)[:, PASS:R].rearrange("p (m t) -> p t m", t=4))
-        nc.gpsimd.tensor_copy(out=wa_dw[:].rearrange("p (t m) -> p t m", t=4), in_=wa_w[1][:].rearrange("p (m t) -> p t m", t=4))
+        nc.gpsimd.tensor_copy(out=wa_dw[:].rearrange("p (t m) -> p t m", t=4)[:, :, 0 : P // 2], in_=wa_piece[0][:].rearrange("p (m t) -> p t m", t=4))
         nc.gpsimd.tensor_copy(out=wa_ds[:].rearrange("p (t m) -> p t m", t=4), in_=wa_s[:].bitcast(U8)[:, PASS:R].rearrange("p (m t) -> p t m", t=4))
+        nc.gpsimd.tensor_copy(out=wa_dw[:].rearrange("p (t m) -> p t m", t=4)[:, :, P // 2 : P], in_=wa_piece[1][:].rearrange("p (m t) -> p t m", t=4))
         nc.gpsimd.affine_select(out=ident[:], in_=ident[:], pattern=[[-1, P]], compare_op=mybir.AluOpType.is_equal, fill=0.0, base=0, channel_multiplier=1)
 
         v_w = keep.tile([P, J], U32, name="v_w", align_bytes=64)

@@ -19,28 +19,33 @@ MULT = mybir.AluOpType.mult
 P = 128
 PASS = 512
 CHUNKS = J // P
+N_TILES = N // P
 LIST_COLS = P // 16
+TURNED, DEALT = 0, 1
+POOL_CHUNK = CHUNKS - 1
 TAB_ROW, EN8_ROW = 8, 12
+PERIOD, REPEATS = 14, 7
+SPAN = PERIOD * REPEATS
+LAST_QUADRANT = 96
 
 
-def load_scales(queue, plane, scales, first_row, quadrants=range(4)):
+def load_quadrants(queue, plane, scales, first_row, quadrants):
     rows = scales[0].bitcast(I32)
     for q in quadrants:
         queue.dma_start(out=plane[32 * q + first_row : 32 * q + first_row + 4, :], in_=rows[4 * q : 4 * q + 4, :])
 
 
-def load_plane(queue, plane, scales, first_row):
-    rows = scales[0].bitcast(I32)
-    queue.dma_start(out=plane[first_row : first_row + 98, :], in_=rows[0:14, :].partition_broadcast(7))
-    queue.dma_start(out=plane[first_row + 98 : P, :], in_=rows[14:16, :].partition_broadcast((P - 98 - first_row) // 2))
-
-
-def load_first_rows(queue, plane, scales):
-    queue.dma_start(out=plane[0:98, :], in_=scales[0].bitcast(I32)[0:14, :].partition_broadcast(7))
+def load_first_rows(queue, plane, scales, first_row=0):
+    queue.dma_start(out=plane[first_row : first_row + SPAN, :], in_=scales[0].bitcast(I32)[0:PERIOD, :].partition_broadcast(REPEATS))
 
 
 def load_last_rows(queue, plane, scales):
-    queue.dma_start(out=plane[98:100, :], in_=scales[0].bitcast(I32)[14:16, :])
+    queue.dma_start(out=plane[SPAN : SPAN + 2, :], in_=scales[0].bitcast(I32)[PERIOD:16, :])
+
+
+def load_plane(queue, plane, scales, first_row):
+    load_first_rows(queue, plane, scales, first_row)
+    queue.dma_start(out=plane[first_row + SPAN : P, :], in_=scales[0].bitcast(I32)[PERIOD:16, :].partition_broadcast((P - SPAN - first_row) // 2))
 
 
 def words8(w):
@@ -59,7 +64,7 @@ def tile_list_kg_gate_mix_none_kernel(tc, tab_words, tab_scales, tab2_words, tab
         tab2_w = keep.tile([P, T], I32, name="tab2_w", align_bytes=64)
         tab_s = keep.tile([P, T // 4], I32, name="tab_s", align_bytes=64)
         tab2_s = keep.tile([P, T // 4], I32, name="tab2_s", align_bytes=64)
-        wa_w = [keep.tile([P, PASS], I32, name="wa_w0", align_bytes=64)]
+        wa_w0 = keep.tile([P, PASS], I32, name="wa_w0", align_bytes=64)
         wa_piece = [keep.tile([P, PASS // 2], I32, name="wa_piece%d" % i, align_bytes=64) for i in range(2)]
         wb_w = keep.tile([P, R // 2], I32, name="wb_w", align_bytes=64)
         wb_s = keep.tile([P, R // 4], I32, name="wb_s", align_bytes=64)
@@ -71,25 +76,26 @@ def tile_list_kg_gate_mix_none_kernel(tc, tab_words, tab_scales, tab2_words, tab
         ident = keep.tile([P, P], F32, name="ident", align_bytes=64)
 
         nc.vector.memset(tab2_s[:], 0)
-        nc.gpsimd.memset(wb_s[96:P, :], 0)
-        nc.vector.memset(wa_s[96:P, :], 0)
+        nc.gpsimd.memset(wb_s[LAST_QUADRANT:P, :], 0)
+        nc.vector.memset(wa_s[LAST_QUADRANT:P, :], 0)
         nc.vector.memset(tab_s[:], 0)
         nc.vector.memset(ident[:], 1.0)
+
         load_first_rows(nc.gpsimd, wb_s, wb_scales)
         load_first_rows(nc.gpsimd, wa_s, wa_scales)
-        load_scales(nc.scalar, tab2_s, tab2_scales, 0, range(0, 2))
+        load_quadrants(nc.scalar, tab2_s, tab2_scales, 0, range(0, 2))
         load_last_rows(nc.scalar, wb_s, wb_scales)
 
         nc.sync.dma_start(out=wb_w[:], in_=wb_words[0].bitcast(I32))
         nc.sync.dma_start(list2[:], offs2)
-        load_scales(nc.sync, tab2_s, tab2_scales, 0, range(2, 4))
+        load_quadrants(nc.sync, tab2_s, tab2_scales, 0, range(2, 4))
         nc.sync.dma_start(out=tab2_w[:], in_=words8(tab2_words))
         nc.sync.dma_start(out=wa_piece[0][:], in_=words8(wa_words)[:, PASS : PASS + PASS // 2])
         nc.sync.dma_start(list1[:], offs)
-        load_scales(nc.sync, tab_s, tab_scales, TAB_ROW)
+        load_quadrants(nc.sync, tab_s, tab_scales, TAB_ROW, range(4))
         nc.sync.dma_start(out=tab_w[:], in_=words8(tab_words))
         load_last_rows(nc.sync, wa_s, wa_scales)
-        nc.sync.dma_start(out=wa_w[0][:], in_=words8(wa_words)[:, 0:PASS])
+        nc.sync.dma_start(out=wa_w0[:], in_=words8(wa_words)[:, 0:PASS])
         nc.sync.dma_start(out=wa_piece[1][:], in_=words8(wa_words)[:, PASS + PASS // 2 : R])
         nc.sync.dma_start(out=en8_w[:], in_=words8(en8_words))
         nc.sync.dma_start(out=en4_w[:], in_=en4_words[0].bitcast(I32))
@@ -100,88 +106,98 @@ def tile_list_kg_gate_mix_none_kernel(tc, tab_words, tab_scales, tab2_words, tab
         wb_dw = keep.tile([P, 2 * PASS], U8, name="wb_dw", align_bytes=64)
         wa_ds = keep.tile([P, PASS], U8, name="wa_ds", align_bytes=64)
         wa_dw = keep.tile([P, PASS], I32, name="wa_dw", align_bytes=64)
+
+        def deal(dst, src):
+            nc.gpsimd.tensor_copy(out=dst, in_=src.rearrange("p (m t) -> p t m", t=4))
+
+        def by_place(tile):
+            return tile[:].rearrange("p (t m) -> p t m", t=4)
+
         nc.gpsimd.tensor_copy(out=wb_dw[:].rearrange("p (t m e) -> p t m e", t=4, e=2), in_=wb_w[:].bitcast(U8)[:, 2 * PASS : 2 * R].rearrange("p (m t e) -> p t m e", t=4, e=2))
-        nc.gpsimd.tensor_copy(out=wb_ds[:].rearrange("p (t m) -> p t m", t=4), in_=wb_s[:].bitcast(U8)[:, PASS:R].rearrange("p (m t) -> p t m", t=4))
-        nc.gpsimd.tensor_copy(out=wa_dw[:].rearrange("p (t m) -> p t m", t=4)[:, :, 0 : P // 2], in_=wa_piece[0][:].rearrange("p (m t) -> p t m", t=4))
-        nc.gpsimd.tensor_copy(out=wa_ds[:].rearrange("p (t m) -> p t m", t=4), in_=wa_s[:].bitcast(U8)[:, PASS:R].rearrange("p (m t) -> p t m", t=4))
-        nc.gpsimd.tensor_copy(out=wa_dw[:].rearrange("p (t m) -> p t m", t=4)[:, :, P // 2 : P], in_=wa_piece[1][:].rearrange("p (m t) -> p t m", t=4))
+        deal(by_place(wb_ds), wb_s[:].bitcast(U8)[:, PASS:R])
+        deal(by_place(wa_dw)[:, :, 0 : P // 2], wa_piece[0][:])
+        deal(by_place(wa_ds), wa_s[:].bitcast(U8)[:, PASS:R])
+        deal(by_place(wa_dw)[:, :, P // 2 : P], wa_piece[1][:])
         nc.gpsimd.affine_select(out=ident[:], in_=ident[:], pattern=[[-1, P]], compare_op=mybir.AluOpType.is_equal, fill=0.0, base=0, channel_multiplier=1)
 
         v_w = keep.tile([P, J], U32, name="v_w", align_bytes=64)
         v_s = keep.tile([P, J], U8, name="v_s", align_bytes=64)
         v2_w = keep.tile([P, J], U32, name="v2_w", align_bytes=64)
         v2_s = keep.tile([P, J], U8, name="v2_s", align_bytes=64)
-        gate = {(c, b): keep.tile([P, PASS], F32, name="gate%d%d" % (c, b), tag="gate%d%d" % (c, b), align_bytes=64) for c in range(CHUNKS) for b in range(2)}
-        h = {(c, 0): keep.tile([P, PASS], BF16, name="h%d0" % c, align_bytes=64) for c in range(CHUNKS)}
-        h_pair = [keep.tile([P, 2 * PASS], BF16, name="h_pair%d" % i, align_bytes=64) for i in range(2)]
+        gate = {(c, b): keep.tile([P, PASS], F32, name="gate%d%d" % (c, b), align_bytes=64) for c in range(CHUNKS) for b in (TURNED, DEALT)}
+        h = {(c, TURNED): keep.tile([P, PASS], BF16, name="h%d0" % c, align_bytes=64) for c in range(CHUNKS)}
+        h_pair = [keep.tile([P, 2 * PASS], BF16, name="h_pair%d" % i, align_bytes=64) for i in range(CHUNKS // 2)]
         for c in range(CHUNKS):
-            h[c, 1] = h_pair[c // 2][:, (c % 2) * PASS : (c % 2 + 1) * PASS]
+            h[c, DEALT] = h_pair[c // 2][:, (c % 2) * PASS : (c % 2 + 1) * PASS]
         turned = {c: keep.tile([P, n * PASS], BF16, name="turned%d" % c, align_bytes=64) for c, n in ((0, 2), (2, 1), (3, 1))}
         hq_s = {}
         hq_w = {}
+
+        def bank_tile(bank, shape):
+            return psum.tile(shape, F32, name="bank%d" % bank)
 
         def gather(dst, window, lst, c0, c1):
             nc.vector.tensor_copy(dst[:, c0 * P : c1 * P], window.indirect(lst[:, c0 * LIST_COLS : c1 * LIST_COLS]))
 
         def bank_view(bank, b):
-            if b == 0:
+            if b == TURNED:
                 return bank[:].rearrange("p (m u e) -> p u m e", u=2, e=2)
             return bank[:].rearrange("p (t j) -> p j t", t=4)
 
         def flat_view(tile, b):
-            if b == 0:
+            if b == TURNED:
                 return tile[:].rearrange("p (u m e) -> p u m e", u=2, e=2)
             return tile[:].rearrange("p (j t) -> p j t", t=4)
 
-        def first_product(c, b, bank, cols_w, cols_s, w_words, w_scales):
-            acc = psum.tile([P, PASS], F32, name="bank%d" % bank)
-            if b == 0:
+        def first_product(b, bank, cols_w, cols_s, w_words, w_scales):
+            acc = bank_tile(bank, [P, PASS])
+            if b == TURNED:
                 nc.tensor.matmul_mx(out=acc[:], lhsT=cols_w, lhsT_scale=cols_s, rhs=w_words(0, PASS), rhs_scale=w_scales(0, PASS), start=True, stop=True)
             else:
                 for t in range(4):
                     nc.tensor.matmul_mx(out=acc[:, t * P : (t + 1) * P], lhsT=w_words(t * P, (t + 1) * P), lhsT_scale=w_scales(t * P, (t + 1) * P), rhs=cols_w, rhs_scale=cols_s, start=True, stop=True)
             return acc
 
-        def gate_stage(c, b, bank):
+        def make_gate(c, b, bank):
             cols = slice(c * P, (c + 1) * P)
-            words = wb_w[:].bitcast(U8) if b == 0 else wb_dw[:]
-            scales = wb_s[:].bitcast(U8) if b == 0 else wb_ds[:]
-            hb = first_product(c, b, bank, v2_w[:, cols].bitcast(FP8X4), v2_s[:, cols], lambda lo, hi: words[:, 2 * lo : 2 * hi].bitcast(FP4X4), lambda lo, hi: scales[:, lo:hi])
+            words = wb_w[:].bitcast(U8) if b == TURNED else wb_dw[:]
+            scales = wb_s[:].bitcast(U8) if b == TURNED else wb_ds[:]
+            hb = first_product(b, bank, v2_w[:, cols].bitcast(FP8X4), v2_s[:, cols], lambda lo, hi: words[:, 2 * lo : 2 * hi].bitcast(FP4X4), lambda lo, hi: scales[:, lo:hi])
             nc.scalar.activation(out=flat_view(gate[c, b], b), in_=bank_view(hb, b), func=SIGMOID)
 
-        def project_stage(c, b, bank):
+        def project(c, b, bank):
             cols = slice(c * P, (c + 1) * P)
-            words = wa_w[0][:] if b == 0 else wa_dw[:]
-            scales = wa_s[:].bitcast(U8) if b == 0 else wa_ds[:]
-            return first_product(c, b, bank, v_w[:, cols].bitcast(FP8X4), v_s[TAB_ROW:P, cols], lambda lo, hi: words[:, lo:hi].bitcast(FP8X4), lambda lo, hi: scales[:, lo:hi])
+            words = wa_w0[:] if b == TURNED else wa_dw[:]
+            scales = wa_s[:].bitcast(U8) if b == TURNED else wa_ds[:]
+            return first_product(b, bank, v_w[:, cols].bitcast(FP8X4), v_s[TAB_ROW:P, cols], lambda lo, hi: words[:, lo:hi].bitcast(FP8X4), lambda lo, hi: scales[:, lo:hi])
 
-        def product_stage(c, b, ha):
+        def multiply(c, b, ha):
             nc.vector.tensor_tensor(out=flat_view(h[c, b], b), in0=flat_view(gate[c, b], b), in1=bank_view(ha, b), op=MULT)
 
-        def product_on_gpsimd(c, ha):
+        def multiply_on_gpsimd(c, ha):
             ha_sb = keep.tile([P, PASS], F32, name="ha_sb%d" % c, align_bytes=64)
-            nc.scalar.copy(out=flat_view(ha_sb, 0), in_=bank_view(ha, 0))
-            nc.gpsimd.tensor_tensor(out=h[c, 0][:], in0=ha_sb[:], in1=gate[c, 0][:], op=MULT)
+            nc.scalar.copy(out=flat_view(ha_sb, TURNED), in_=bank_view(ha, TURNED))
+            nc.gpsimd.tensor_tensor(out=h[c, TURNED][:], in0=ha_sb[:], in1=gate[c, TURNED][:], op=MULT)
 
-        def turn_stage(c, bank, dst):
-            xt = psum.tile([P, 2, P], F32, name="bank%d" % bank)
-            pairs = h[c, 0][:].bitcast(F32)
+        def turn(c, bank, dst):
+            xt = bank_tile(bank, [P, 2, P])
+            pairs = h[c, TURNED][:].bitcast(F32)
             for u in range(2):
                 nc.tensor.transpose(xt[:, u, :], pairs[:, u * P : (u + 1) * P], ident[:])
             nc.scalar.copy(out=dst.bitcast(F32).rearrange("p (j u) -> p j u", u=2), in_=xt[:].rearrange("p u j -> p j u"))
 
-        def quant_stage(source, units, tag):
-            width = len(units) * P
-            words = keep.tile([P, width], U32, name="hq_w%d%d" % units[0], tag=tag, align_bytes=64)
-            plane = keep.tile([P, width], U8, name="hq_s%d%d" % units[0], align_bytes=64)
-            nc.vector.quantize_mx(out=words[:].bitcast(FP8X4), scales=plane[:], in_=source[:, :])
-            for i, unit in enumerate(units):
-                hq_w[unit] = words[:, i * P : (i + 1) * P]
-                hq_s[unit] = plane[:, i * P : (i + 1) * P]
+        def quantise(source, chunks, b):
+            width = len(chunks) * P
+            words = keep.tile([P, width], U32, name="hq_w%d%d" % (chunks[0], b), align_bytes=64)
+            plane = keep.tile([P, width], U8, name="hq_s%d%d" % (chunks[0], b), align_bytes=64)
+            nc.vector.quantize_mx(out=words[:].bitcast(FP8X4), scales=plane[:], in_=source)
+            for i, c in enumerate(chunks):
+                hq_w[c, b] = words[:, i * P : (i + 1) * P]
+                hq_s[c, b] = plane[:, i * P : (i + 1) * P]
             return words[:], plane[:]
 
-        def score_pass(dst, nt, b, words, plane, start, stop):
-            if b == 0:
+        def score(dst, nt, b, words, plane, start, stop):
+            if b == TURNED:
                 en_words = en8_w[:, nt * P : (nt + 1) * P].bitcast(FP8X4)
                 en_scales = en8_s[EN8_ROW:P, :].bitcast(U8)[:, nt * P : (nt + 1) * P]
             else:
@@ -199,48 +215,54 @@ def tile_list_kg_gate_mix_none_kernel(tc, tab_words, tab_scales, tab2_words, tab
         gather(v2_w, tab2_w[:].bitcast(U32), list2, 1, CHUNKS)
         gather(v_s, tab_s[:].bitcast(U8), list1, 0, CHUNKS)
         gather(v_w, tab_w[:].bitcast(U32), list1, 0, 1)
-        gather(v_w, tab_w[:].bitcast(U32), list1, 3, 4)
-        gather(v_w, tab_w[:].bitcast(U32), list1, 1, 3)
+        gather(v_w, tab_w[:].bitcast(U32), list1, POOL_CHUNK, CHUNKS)
+        gather(v_w, tab_w[:].bitcast(U32), list1, 1, POOL_CHUNK)
+
         for c in range(CHUNKS):
-            gate_stage(c, 0, c)
-        gate_stage(0, 1, 4)
+            make_gate(c, TURNED, c)
+        make_gate(0, DEALT, 4)
         ha = {}
-        for c, bank in ((0, 5), (3, 6), (1, 7), (2, 0)):
-            ha[c, 0] = project_stage(c, 0, bank)
-        product_on_gpsimd(3, ha[3, 0])
-        for c in (0, 1, 2):
-            product_stage(c, 0, ha[c, 0])
-        ha[0, 1] = project_stage(0, 1, 1)
-        gate_stage(1, 1, 5)
-        gate_stage(2, 1, 6)
-        ha[1, 1] = project_stage(1, 1, 2)
-        gate_stage(3, 1, 7)
-        ha[2, 1] = project_stage(2, 1, 3)
-        turn_stage(0, 0, turned[0][:, 0:PASS])
-        turn_stage(1, 5, turned[0][:, PASS : 2 * PASS])
-        ha[3, 1] = project_stage(3, 1, 4)
-        turn_stage(2, 6, turned[2][:])
-        turn_stage(3, 7, turned[3][:])
-        for c in range(3):
-            product_stage(c, 1, ha[c, 1])
-        quant_stage(h_pair[0], [(0, 1), (1, 1)], "hq01")
-        pair_w, pair_s = quant_stage(turned[0], [(0, 0), (1, 0)], "hqa")
-        product_stage(3, 1, ha[3, 1])
-        y01 = [psum.tile([P, 2 * P], F32, name="bank%d" % bk) for bk in (1, 2)]
+        for c, bank in ((0, 5), (POOL_CHUNK, 6), (1, 7), (2, 0)):
+            ha[c, TURNED] = project(c, TURNED, bank)
+        multiply_on_gpsimd(POOL_CHUNK, ha[POOL_CHUNK, TURNED])
+        for c in range(POOL_CHUNK):
+            multiply(c, TURNED, ha[c, TURNED])
+
+        ha[0, DEALT] = project(0, DEALT, 1)
+        make_gate(1, DEALT, 5)
+        make_gate(2, DEALT, 6)
+        ha[1, DEALT] = project(1, DEALT, 2)
+        make_gate(3, DEALT, 7)
+        ha[2, DEALT] = project(2, DEALT, 3)
+        turn(0, 0, turned[0][:, 0:PASS])
+        turn(1, 5, turned[0][:, PASS : 2 * PASS])
+        ha[3, DEALT] = project(3, DEALT, 4)
+        turn(2, 6, turned[2][:])
+        turn(3, 7, turned[3][:])
+
+        for c in range(CHUNKS - 1):
+            multiply(c, DEALT, ha[c, DEALT])
+        quantise(h_pair[0][:], [0, 1], DEALT)
+        quantise(h[2, DEALT], [2], DEALT)
+        pair_w, pair_s = quantise(turned[0][:], [0, 1], TURNED)
+        multiply(3, DEALT, ha[3, DEALT])
+
+        y01 = [bank_tile(bank, [P, 2 * P]) for bank in (1, 2)]
         for c in range(2):
-            for nt in range(2):
-                score_pass(y01[nt][:, c * P : (c + 1) * P], nt, 1, hq_w[c, 1], hq_s[c, 1], c == 0, False)
-        for nt in range(2):
-            score_pass(y01[nt][:], nt, 0, pair_w, pair_s, False, True)
-        for nt in range(2):
+            for nt in range(N_TILES):
+                score(y01[nt][:, c * P : (c + 1) * P], nt, DEALT, hq_w[c, DEALT], hq_s[c, DEALT], c == 0, False)
+        for nt in range(N_TILES):
+            score(y01[nt][:], nt, TURNED, pair_w, pair_s, False, True)
+        for nt in range(N_TILES):
             store(nc.scalar.copy, nc.sync, "y01%d" % nt, y01[nt][:], out[nt * P : (nt + 1) * P, 0 : 2 * P])
-        for c, banks in ((2, (3, 0)), (3, (4, 5))):
-            quant_stage(h[c, 1], [(c, 1)], "hq%d1" % c)
-            quant_stage(turned[c], [(c, 0)], "hq%d0" % c)
-        for c, banks in ((2, (3, 0)), (3, (4, 5))):
-            y = [psum.tile([P, P], F32, name="bank%d" % bk) for bk in banks]
-            for b in (1, 0):
-                for nt in range(2):
-                    score_pass(y[nt][:], nt, b, hq_w[c, b], hq_s[c, b], b == 1, b == 0)
+
+        for c in (2, 3):
+            quantise(turned[c][:], [c], TURNED)
+        quantise(h[3, DEALT], [3], DEALT)
+        for c, banks, halves, last_queue in ((2, (3, 0), (DEALT, TURNED), nc.sync), (3, (4, 5), (TURNED, DEALT), nc.scalar)):
+            y = [bank_tile(bank, [P, P]) for bank in banks]
+            for b in halves:
+                for nt in range(N_TILES):
+                    score(y[nt][:], nt, b, hq_w[c, b], hq_s[c, b], b == halves[0], b == halves[1])
             store(nc.vector.tensor_copy, nc.sync, "y%d0" % c, y[0][:], out[0:P, c * P : (c + 1) * P])
-            store(nc.scalar.copy, nc.sync if c == 2 else nc.scalar, "y%d1" % c, y[1][:], out[P : 2 * P, c * P : (c + 1) * P])
+            store(nc.scalar.copy, last_queue, "y%d1" % c, y[1][:], out[P : 2 * P, c * P : (c + 1) * P])

@@ -35,6 +35,12 @@ def load_quadrants(queue, plane, scales, first_row, quadrants):
         queue.dma_start(out=plane[32 * q + first_row : 32 * q + first_row + 4, :], in_=rows[4 * q : 4 * q + 4, :])
 
 
+def load_filled_quadrants(queue, plane, scales, quadrants):
+    rows = scales[0].bitcast(I32)
+    for q in quadrants:
+        queue.dma_start(out=plane[32 * q : 32 * q + 32, :], in_=rows[4 * q : 4 * q + 4, :].partition_broadcast(8))
+
+
 def load_first_rows(queue, plane, scales, first_row=0):
     queue.dma_start(out=plane[first_row : first_row + SPAN, :], in_=scales[0].bitcast(I32)[0:PERIOD, :].partition_broadcast(REPEATS))
 
@@ -65,7 +71,7 @@ def tile_list_kg_gate_mix_none_kernel(tc, tab_words, tab_scales, tab2_words, tab
         tab_s = keep.tile([P, T // 4], I32, name="tab_s", align_bytes=64)
         tab2_s = keep.tile([P, T // 4], I32, name="tab2_s", align_bytes=64)
         wa_w0 = keep.tile([P, PASS], I32, name="wa_w0", align_bytes=64)
-        wa_piece = [keep.tile([P, PASS // 2], I32, name="wa_piece%d" % i, align_bytes=64) for i in range(2)]
+        wa_w1 = keep.tile([P, PASS], I32, name="wa_w1", align_bytes=64)
         wb_w = keep.tile([P, R // 2], I32, name="wb_w", align_bytes=64)
         wb_s = keep.tile([P, R // 4], I32, name="wb_s", align_bytes=64)
         wa_s = keep.tile([P, R // 4], I32, name="wa_s", align_bytes=64)
@@ -75,7 +81,6 @@ def tile_list_kg_gate_mix_none_kernel(tc, tab_words, tab_scales, tab2_words, tab
         en4_w = keep.tile([P, N // 2], I32, name="en4_w", align_bytes=64)
         ident = keep.tile([P, P], F32, name="ident", align_bytes=64)
 
-        nc.vector.memset(tab2_s[:], 0)
         nc.gpsimd.memset(wb_s[LAST_QUADRANT:P, :], 0)
         nc.vector.memset(wa_s[LAST_QUADRANT:P, :], 0)
         nc.vector.memset(tab_s[:], 0)
@@ -83,20 +88,22 @@ def tile_list_kg_gate_mix_none_kernel(tc, tab_words, tab_scales, tab2_words, tab
 
         load_first_rows(nc.gpsimd, wb_s, wb_scales)
         load_first_rows(nc.gpsimd, wa_s, wa_scales)
-        load_quadrants(nc.scalar, tab2_s, tab2_scales, 0, range(0, 2))
+        load_filled_quadrants(nc.scalar, tab2_s, tab2_scales, range(0, 2))
         load_last_rows(nc.scalar, wb_s, wb_scales)
+        warm = keep.tile([P, 2], F32, name="warm")
+        nc.vector.memset(warm[:, 0:1], 0.0)
+        nc.scalar.activation(out=warm[:, 1:2], in_=warm[:, 0:1], func=SIGMOID)
 
-        nc.sync.dma_start(out=wb_w[:], in_=wb_words[0].bitcast(I32))
         nc.sync.dma_start(list2[:], offs2)
-        load_quadrants(nc.sync, tab2_s, tab2_scales, 0, range(2, 4))
+        load_filled_quadrants(nc.sync, tab2_s, tab2_scales, range(2, 4))
         nc.sync.dma_start(out=tab2_w[:], in_=words8(tab2_words))
-        nc.sync.dma_start(out=wa_piece[0][:], in_=words8(wa_words)[:, PASS : PASS + PASS // 2])
+        nc.sync.dma_start(out=wb_w[:], in_=wb_words[0].bitcast(I32))
         nc.sync.dma_start(list1[:], offs)
         load_quadrants(nc.sync, tab_s, tab_scales, TAB_ROW, range(4))
         nc.sync.dma_start(out=tab_w[:], in_=words8(tab_words))
         load_last_rows(nc.sync, wa_s, wa_scales)
         nc.sync.dma_start(out=wa_w0[:], in_=words8(wa_words)[:, 0:PASS])
-        nc.sync.dma_start(out=wa_piece[1][:], in_=words8(wa_words)[:, PASS + PASS // 2 : R])
+        nc.sync.dma_start(out=wa_w1[:], in_=words8(wa_words)[:, PASS:R])
         nc.sync.dma_start(out=en8_w[:], in_=words8(en8_words))
         nc.sync.dma_start(out=en4_w[:], in_=en4_words[0].bitcast(I32))
         load_plane(nc.sync, en8_s, en8_scales, EN8_ROW)
@@ -113,11 +120,10 @@ def tile_list_kg_gate_mix_none_kernel(tc, tab_words, tab_scales, tab2_words, tab
         def by_place(tile):
             return tile[:].rearrange("p (t m) -> p t m", t=4)
 
-        nc.gpsimd.tensor_copy(out=wb_dw[:].rearrange("p (t m e) -> p t m e", t=4, e=2), in_=wb_w[:].bitcast(U8)[:, 2 * PASS : 2 * R].rearrange("p (m t e) -> p t m e", t=4, e=2))
+        nc.scalar.copy(out=wb_dw[:].bitcast(U16).rearrange("p (t m) -> p m t", t=4), in_=wb_w[:].bitcast(U16)[:, PASS:R].rearrange("p (m t) -> p m t", t=4))
         deal(by_place(wb_ds), wb_s[:].bitcast(U8)[:, PASS:R])
-        deal(by_place(wa_dw)[:, :, 0 : P // 2], wa_piece[0][:])
         deal(by_place(wa_ds), wa_s[:].bitcast(U8)[:, PASS:R])
-        deal(by_place(wa_dw)[:, :, P // 2 : P], wa_piece[1][:])
+        deal(by_place(wa_dw), wa_w1[:])
         nc.gpsimd.affine_select(out=ident[:], in_=ident[:], pattern=[[-1, P]], compare_op=mybir.AluOpType.is_equal, fill=0.0, base=0, channel_multiplier=1)
 
         v_w = keep.tile([P, J], U32, name="v_w", align_bytes=64)

@@ -101,8 +101,8 @@ def tile_list_kg_gate_mix_none_kernel(tc, tab_words, tab_scales, tab2_words, tab
         nc.sync.dma_start(list1[:], offs)
         load_quadrants(nc.sync, tab_s, tab_scales, TAB_ROW, range(4))
         nc.sync.dma_start(out=tab_w[:], in_=words8(tab_words))
-        load_last_rows(nc.sync, wa_s, wa_scales)
         nc.sync.dma_start(out=wa_w0[:], in_=words8(wa_words)[:, 0:PASS])
+        load_last_rows(nc.sync, wa_s, wa_scales)
         nc.sync.dma_start(out=wa_w1[:], in_=words8(wa_words)[:, PASS:R])
         nc.sync.dma_start(out=en8_w[:], in_=words8(en8_words))
         nc.sync.dma_start(out=en4_w[:], in_=en4_words[0].bitcast(I32))
@@ -218,7 +218,8 @@ def tile_list_kg_gate_mix_none_kernel(tc, tab_words, tab_scales, tab2_words, tab
 
         gather(v2_s, tab2_s[:].bitcast(U8), list2, 0, CHUNKS)
         gather(v2_w, tab2_w[:].bitcast(U32), list2, 0, 1)
-        gather(v2_w, tab2_w[:].bitcast(U32), list2, 1, CHUNKS)
+        gather(v2_w, tab2_w[:].bitcast(U32), list2, 1, 2)
+        gather(v2_w, tab2_w[:].bitcast(U32), list2, 2, CHUNKS)
         gather(v_s, tab_s[:].bitcast(U8), list1, 0, CHUNKS)
         gather(v_w, tab_w[:].bitcast(U32), list1, 0, 1)
         gather(v_w, tab_w[:].bitcast(U32), list1, POOL_CHUNK, CHUNKS)

@@ -54,6 +54,10 @@ def load_plane(queue, plane, scales, first_row):
     queue.dma_start(out=plane[first_row + SPAN : P, :], in_=scales[0].bitcast(I32)[PERIOD:16, :].partition_broadcast((P - SPAN - first_row) // 2))
 
 
+def is_turned(c, b):
+    return b == 0 or c == 0
+
+
 def words8(w):
     return w[0].rearrange("p n t -> p (n t)").bitcast(I32)
 
@@ -130,14 +134,14 @@ def tile_list_kg_gate_mix_none_kernel(tc, tab_words, tab_scales, tab2_words, tab
         v_s = keep.tile([P, J], U8, name="v_s", align_bytes=64)
         v2_w = keep.tile([P, J], U32, name="v2_w", align_bytes=64)
         v2_s = keep.tile([P, J], U8, name="v2_s", align_bytes=64)
-        gate = {(c, b): keep.tile([P, PASS], F32, name="gate%d%d" % (c, b), align_bytes=64) for c in range(CHUNKS) for b in (TURNED, DEALT)}
-        h = {(c, TURNED): keep.tile([P, PASS], BF16, name="h%d0" % c, align_bytes=64) for c in range(CHUNKS)}
-        h_pair = [keep.tile([P, 2 * PASS], BF16, name="h_pair%d" % i, align_bytes=64) for i in range(CHUNKS // 2)]
-        for c in range(CHUNKS):
-            h[c, DEALT] = h_pair[c // 2][:, (c % 2) * PASS : (c % 2 + 1) * PASS]
-        turned = {c: keep.tile([P, n * PASS], BF16, name="turned%d" % c, align_bytes=64) for c, n in ((0, 2), (2, 1), (3, 1))}
-        hq_s = {}
-        hq_w = {}
+        gate = {(c, b): keep.tile([P, PASS], F32, name="gate%d%d" % (c, b), align_bytes=64) for c in range(CHUNKS) for b in range(2)}
+        ready = {(b, c0): keep.tile([P, n * PASS], BF16, name="ready%d%d" % (b, c0), align_bytes=64) for b, c0, n in ((0, 0, 2), (0, 2, 1), (0, 3, 1), (1, 0, 2), (1, 2, 1), (1, 3, 1))}
+        unturned = {(c, b): keep.tile([P, PASS], BF16, name="unturned%d%d" % (c, b), align_bytes=64) for c in range(CHUNKS) for b in range(2) if is_turned(c, b)}
+        quantised = {}
+
+        def ready_part(c, b):
+            c0 = max(first for half, first in ready if half == b and first <= c)
+            return ready[b, c0][:, (c - c0) * PASS : (c - c0 + 1) * PASS]
 
         def bank_tile(bank, shape):
             return psum.tile(shape, F32, name="bank%d" % bank)
@@ -145,76 +149,82 @@ def tile_list_kg_gate_mix_none_kernel(tc, tab_words, tab_scales, tab2_words, tab
         def gather(dst, window, lst, c0, c1):
             nc.vector.tensor_copy(dst[:, c0 * P : c1 * P], window.indirect(lst[:, c0 * LIST_COLS : c1 * LIST_COLS]))
 
-        def bank_view(bank, b):
-            if b == TURNED:
+        def bank_view(bank, c, b):
+            if is_turned(c, b):
                 return bank[:].rearrange("p (m u e) -> p u m e", u=2, e=2)
             return bank[:].rearrange("p (t j) -> p j t", t=4)
 
-        def flat_view(tile, b):
-            if b == TURNED:
-                return tile[:].rearrange("p (u m e) -> p u m e", u=2, e=2)
-            return tile[:].rearrange("p (j t) -> p j t", t=4)
+        def flat_view(ap, c, b):
+            if is_turned(c, b):
+                return ap.rearrange("p (u m e) -> p u m e", u=2, e=2)
+            return ap.rearrange("p (j t) -> p j t", t=4)
 
-        def first_product(b, bank, cols_w, cols_s, w_words, w_scales):
+        def first_product(c, b, bank, cols_w, cols_s, w_words, w_scales):
             acc = bank_tile(bank, [P, PASS])
-            if b == TURNED:
-                nc.tensor.matmul_mx(out=acc[:], lhsT=cols_w, lhsT_scale=cols_s, rhs=w_words(0, PASS), rhs_scale=w_scales(0, PASS), start=True, stop=True)
+            if is_turned(c, b):
+                nc.tensor.matmul_mx(out=acc[:], lhsT=cols_w, lhsT_scale=cols_s, rhs=w_words(0, PASS), rhs_scale=w_scales[:, 0:PASS], start=True, stop=True)
             else:
                 for t in range(4):
-                    nc.tensor.matmul_mx(out=acc[:, t * P : (t + 1) * P], lhsT=w_words(t * P, (t + 1) * P), lhsT_scale=w_scales(t * P, (t + 1) * P), rhs=cols_w, rhs_scale=cols_s, start=True, stop=True)
+                    nc.tensor.matmul_mx(out=acc[:, t * P : (t + 1) * P], lhsT=w_words(t * P, (t + 1) * P), lhsT_scale=w_scales[:, t * P : (t + 1) * P], rhs=cols_w, rhs_scale=cols_s, start=True, stop=True)
             return acc
 
         def make_gate(c, b, bank):
             cols = slice(c * P, (c + 1) * P)
-            words = wb_w[:].bitcast(U8) if b == TURNED else wb_dw[:]
-            scales = wb_s[:].bitcast(U8) if b == TURNED else wb_ds[:]
-            hb = first_product(b, bank, v2_w[:, cols].bitcast(FP8X4), v2_s[:, cols], lambda lo, hi: words[:, 2 * lo : 2 * hi].bitcast(FP4X4), lambda lo, hi: scales[:, lo:hi])
-            nc.scalar.activation(out=flat_view(gate[c, b], b), in_=bank_view(hb, b), func=SIGMOID)
+            words = wb_w[:].bitcast(U8)[:, 2 * b * PASS : 2 * (b + 1) * PASS] if is_turned(c, b) else wb_dw[:]
+            scales = wb_s[:].bitcast(U8)[:, b * PASS : (b + 1) * PASS] if is_turned(c, b) else wb_ds[:]
+            hb = first_product(c, b, bank, v2_w[:, cols].bitcast(FP8X4), v2_s[:, cols], lambda lo, hi: words[:, 2 * lo : 2 * hi].bitcast(FP4X4), scales)
+            nc.scalar.activation(out=flat_view(gate[c, b][:], c, b), in_=bank_view(hb, c, b), func=SIGMOID)
 
         def project(c, b, bank):
             cols = slice(c * P, (c + 1) * P)
-            words = wa_w0[:] if b == TURNED else wa_dw[:]
-            scales = wa_s[:].bitcast(U8) if b == TURNED else wa_ds[:]
-            return first_product(b, bank, v_w[:, cols].bitcast(FP8X4), v_s[TAB_ROW:P, cols], lambda lo, hi: words[:, lo:hi].bitcast(FP8X4), lambda lo, hi: scales[:, lo:hi])
+            words = (wa_w0, wa_w1)[b][:] if is_turned(c, b) else wa_dw[:]
+            scales = wa_s[:].bitcast(U8)[:, b * PASS : (b + 1) * PASS] if is_turned(c, b) else wa_ds[:]
+            return first_product(c, b, bank, v_w[:, cols].bitcast(FP8X4), v_s[TAB_ROW:P, cols], lambda lo, hi: words[:, lo:hi].bitcast(FP8X4), scales)
 
-        def multiply(c, b, ha):
-            nc.vector.tensor_tensor(out=flat_view(h[c, b], b), in0=flat_view(gate[c, b], b), in1=bank_view(ha, b), op=MULT)
+        def multiply(c, b):
+            dst = unturned[c, b][:] if is_turned(c, b) else ready_part(c, b)
+            nc.vector.tensor_tensor(out=flat_view(dst, c, b), in0=flat_view(gate[c, b][:], c, b), in1=bank_view(ha[c, b], c, b), op=MULT)
 
-        def multiply_on_gpsimd(c, ha):
-            ha_sb = keep.tile([P, PASS], F32, name="ha_sb%d" % c, align_bytes=64)
-            nc.scalar.copy(out=flat_view(ha_sb, TURNED), in_=bank_view(ha, TURNED))
-            nc.gpsimd.tensor_tensor(out=h[c, TURNED][:], in0=ha_sb[:], in1=gate[c, TURNED][:], op=MULT)
+        def multiply_on_gpsimd(c, b):
+            ha_sb = keep.tile([P, PASS], F32, name="ha_sb", align_bytes=64)
+            nc.scalar.copy(out=flat_view(ha_sb[:], c, b), in_=bank_view(ha[c, b], c, b))
+            nc.gpsimd.tensor_tensor(out=unturned[c, b][:], in0=ha_sb[:], in1=gate[c, b][:], op=MULT)
 
-        def turn(c, bank, dst):
+        def turn(c, b, bank):
             xt = bank_tile(bank, [P, 2, P])
-            pairs = h[c, TURNED][:].bitcast(F32)
+            pairs = unturned[c, b][:].bitcast(F32)
             for u in range(2):
                 nc.tensor.transpose(xt[:, u, :], pairs[:, u * P : (u + 1) * P], ident[:])
-            nc.scalar.copy(out=dst.bitcast(F32).rearrange("p (j u) -> p j u", u=2), in_=xt[:].rearrange("p u j -> p j u"))
+            nc.scalar.copy(out=ready_part(c, b).bitcast(F32).rearrange("p (j u) -> p j u", u=2), in_=xt[:].rearrange("p u j -> p j u"))
 
-        def quantise(source, chunks, b):
-            width = len(chunks) * P
-            words = keep.tile([P, width], U32, name="hq_w%d%d" % (chunks[0], b), align_bytes=64)
-            plane = keep.tile([P, width], U8, name="hq_s%d%d" % (chunks[0], b), align_bytes=64)
-            nc.vector.quantize_mx(out=words[:].bitcast(FP8X4), scales=plane[:], in_=source)
-            for i, c in enumerate(chunks):
-                hq_w[c, b] = words[:, i * P : (i + 1) * P]
-                hq_s[c, b] = plane[:, i * P : (i + 1) * P]
-            return words[:], plane[:]
+        def quantise(b, c0):
+            width = ready[b, c0].shape[1] // 4
+            words = keep.tile([P, width], U32, name="hq_w%d%d" % (b, c0), align_bytes=64)
+            plane = keep.tile([P, width], U8, name="hq_s%d%d" % (b, c0), align_bytes=64)
+            nc.vector.quantize_mx(out=words[:].bitcast(FP8X4), scales=plane[:], in_=ready[b, c0][:])
+            for c in range(c0, c0 + width // P):
+                quantised[c, b] = (words, plane, c0)
 
-        def score(dst, nt, b, words, plane, start, stop):
-            if b == TURNED:
+        def score(dst, nt, b, c0, c1, start, stop):
+            if b == 0:
                 en_words = en8_w[:, nt * P : (nt + 1) * P].bitcast(FP8X4)
                 en_scales = en8_s[EN8_ROW:P, :].bitcast(U8)[:, nt * P : (nt + 1) * P]
             else:
                 en_words = en4_w[:].bitcast(U8)[:, 2 * nt * P : 2 * (nt + 1) * P].bitcast(FP4X4)
                 en_scales = en4_s[:].bitcast(U8)[:, nt * P : (nt + 1) * P]
-            nc.tensor.matmul_mx(out=dst, lhsT=en_words, lhsT_scale=en_scales, rhs=words.bitcast(FP8X4), rhs_scale=plane, start=start, stop=stop)
+            words, plane, first = quantised[c0, b]
+            cols = slice((c0 - first) * P, (c1 - first) * P)
+            nc.tensor.matmul_mx(out=dst, lhsT=en_words, lhsT_scale=en_scales, rhs=words[:, cols].bitcast(FP8X4), rhs_scale=plane[:, cols], start=start, stop=stop)
 
-        def store(engine_copy, queue, name, bank, dst):
-            y = keep.tile(list(bank.shape), F32, name=name, align_bytes=64)
-            engine_copy(out=y[:], in_=bank)
-            queue.dma_start(out=dst, in_=y[:])
+        def finish(c0, c1, banks, halves, copies, queues):
+            y = [bank_tile(bank, [P, (c1 - c0) * P]) for bank in banks]
+            for b in halves:
+                for nt in range(N_TILES):
+                    score(y[nt][:], nt, b, c0, c1, b == halves[0], b == halves[1])
+            for nt in range(N_TILES):
+                y_sb = keep.tile([P, (c1 - c0) * P], F32, name="y%d%d" % (c0, nt), align_bytes=64)
+                copies[nt](out=y_sb[:], in_=y[nt][:])
+                queues[nt].dma_start(out=out[nt * P : (nt + 1) * P, c0 * P : c1 * P], in_=y_sb[:])
 
         gather(v2_s, tab2_s[:].bitcast(U8), list2, 0, CHUNKS)
         gather(v2_w, tab2_w[:].bitcast(U32), list2, 0, 1)
@@ -226,50 +236,37 @@ def tile_list_kg_gate_mix_none_kernel(tc, tab_words, tab_scales, tab2_words, tab
         gather(v_w, tab_w[:].bitcast(U32), list1, 1, POOL_CHUNK)
 
         for c in range(CHUNKS):
-            make_gate(c, TURNED, c)
-        make_gate(0, DEALT, 4)
+            make_gate(c, 0, c)
+        make_gate(0, 1, 4)
         ha = {}
         for c, bank in ((0, 5), (POOL_CHUNK, 6), (1, 7), (2, 0)):
-            ha[c, TURNED] = project(c, TURNED, bank)
-        multiply_on_gpsimd(POOL_CHUNK, ha[POOL_CHUNK, TURNED])
+            ha[c, 0] = project(c, 0, bank)
+        multiply_on_gpsimd(POOL_CHUNK, 0)
+        ha[0, 1] = project(0, 1, 1)
         for c in range(POOL_CHUNK):
-            multiply(c, TURNED, ha[c, TURNED])
+            multiply(c, 0)
+        multiply(0, 1)
 
-        ha[0, DEALT] = project(0, DEALT, 1)
-        make_gate(1, DEALT, 5)
-        make_gate(2, DEALT, 6)
-        ha[1, DEALT] = project(1, DEALT, 2)
-        make_gate(3, DEALT, 7)
-        ha[2, DEALT] = project(2, DEALT, 3)
-        turn(0, 0, turned[0][:, 0:PASS])
-        turn(1, 5, turned[0][:, PASS : 2 * PASS])
-        ha[3, DEALT] = project(3, DEALT, 4)
-        turn(2, 6, turned[2][:])
-        turn(3, 7, turned[3][:])
+        make_gate(1, 1, 5)
+        make_gate(2, 1, 6)
+        ha[1, 1] = project(1, 1, 2)
+        ha[2, 1] = project(2, 1, 3)
+        turn(0, 0, 0)
+        turn(1, 0, 5)
+        turn(0, 1, 1)
+        make_gate(3, 1, 0)
+        ha[3, 1] = project(3, 1, 4)
+        turn(2, 0, 7)
+        turn(3, 0, 6)
 
-        for c in range(CHUNKS - 1):
-            multiply(c, DEALT, ha[c, DEALT])
-        quantise(h_pair[0][:], [0, 1], DEALT)
-        quantise(h[2, DEALT], [2], DEALT)
-        pair_w, pair_s = quantise(turned[0][:], [0, 1], TURNED)
-        multiply(3, DEALT, ha[3, DEALT])
-
-        y01 = [bank_tile(bank, [P, 2 * P]) for bank in (1, 2)]
-        for c in range(2):
-            for nt in range(N_TILES):
-                score(y01[nt][:, c * P : (c + 1) * P], nt, DEALT, hq_w[c, DEALT], hq_s[c, DEALT], c == 0, False)
-        for nt in range(N_TILES):
-            score(y01[nt][:], nt, TURNED, pair_w, pair_s, False, True)
-        for nt in range(N_TILES):
-            store(nc.scalar.copy, nc.sync, "y01%d" % nt, y01[nt][:], out[nt * P : (nt + 1) * P, 0 : 2 * P])
-
-        for c in (2, 3):
-            quantise(turned[c][:], [c], TURNED)
-        quantise(h[3, DEALT], [3], DEALT)
-        for c, banks, halves, last_queue in ((2, (3, 0), (DEALT, TURNED), nc.sync), (3, (4, 5), (TURNED, DEALT), nc.scalar)):
-            y = [bank_tile(bank, [P, P]) for bank in banks]
-            for b in halves:
-                for nt in range(N_TILES):
-                    score(y[nt][:], nt, b, hq_w[c, b], hq_s[c, b], b == halves[0], b == halves[1])
-            store(nc.vector.tensor_copy, nc.sync, "y%d0" % c, y[0][:], out[0:P, c * P : (c + 1) * P])
-            store(nc.scalar.copy, last_queue, "y%d1" % c, y[1][:], out[P : 2 * P, c * P : (c + 1) * P])
+        multiply(1, 1)
+        multiply(2, 1)
+        for b, c0 in ((0, 0), (1, 0), (1, 2)):
+            quantise(b, c0)
+        multiply(3, 1)
+        finish(0, 2, (2, 5), (0, 1), (nc.scalar.copy, nc.scalar.copy), (nc.sync, nc.sync))
+        for b, c0 in ((0, 2), (0, 3), (1, 3)):
+            quantise(b, c0)
+        both = (nc.vector.tensor_copy, nc.scalar.copy)
+        finish(2, 3, (3, 1), (1, 0), both, (nc.sync, nc.sync))
+        finish(3, 4, (4, 0), (0, 1), both, (nc.sync, nc.scalar))

@@ -251,22 +251,22 @@ def tile_list_kg_gate_mix_none_kernel(tc, tab_words, tab_scales, tab2_words, tab
         make_gate(2, 1, 6)
         ha[1, 1] = project(1, 1, 2)
         ha[2, 1] = project(2, 1, 3)
-        turn(0, 0, 0)
+        turn(0, 0, 7)
         turn(1, 0, 5)
         turn(0, 1, 1)
-        make_gate(3, 1, 0)
+        make_gate(3, 1, 6)
         ha[3, 1] = project(3, 1, 4)
-        turn(2, 0, 7)
-        turn(3, 0, 6)
+        turn(2, 0, 0)
+        turn(3, 0, 7)
 
         multiply(1, 1)
         multiply(2, 1)
-        for b, c0 in ((0, 0), (1, 0), (1, 2)):
+        for b, c0 in ((0, 0), (1, 0)):
             quantise(b, c0)
         multiply(3, 1)
         finish(0, 2, (2, 5), (0, 1), (nc.scalar.copy, nc.scalar.copy), (nc.sync, nc.sync))
-        for b, c0 in ((0, 2), (0, 3), (1, 3)):
+        for b, c0 in ((1, 2), (0, 2), (0, 3), (1, 3)):
             quantise(b, c0)
         both = (nc.vector.tensor_copy, nc.scalar.copy)
         finish(2, 3, (3, 1), (1, 0), both, (nc.sync, nc.sync))
-        finish(3, 4, (4, 0), (0, 1), both, (nc.sync, nc.scalar))
+        finish(3, 4, (4, 6), (0, 1), both, (nc.sync, nc.scalar))

@@ -54,10 +54,6 @@ def load_plane(queue, plane, scales, first_row):
     queue.dma_start(out=plane[first_row + SPAN : P, :], in_=scales[0].bitcast(I32)[PERIOD:16, :].partition_broadcast((P - SPAN - first_row) // 2))
 
 
-def is_turned(c, b):
-    return b == 0 or c == 0
-
-
 def words8(w):
     return w[0].rearrange("p n t -> p (n t)").bitcast(I32)
 
@@ -68,22 +64,20 @@ def tile_list_kg_gate_mix_none_kernel(tc, tab_words, tab_scales, tab2_words, tab
         keep = ctx.enter_context(tc.tile_pool(name="keep", bufs=1))
         psum = ctx.enter_context(tc.psum_pool(name="psum", bufs=1))
 
+        def sb(shape, dtype, name):
+            return keep.tile(shape, dtype, name=name, align_bytes=64)
+
         list1 = keep.tile([P, J // 16], U16, name="list1")
         list2 = keep.tile([P, J // 16], U16, name="list2")
-        tab_w = keep.tile([P, T], I32, name="tab_w", align_bytes=64)
-        tab2_w = keep.tile([P, T], I32, name="tab2_w", align_bytes=64)
-        tab_s = keep.tile([P, T // 4], I32, name="tab_s", align_bytes=64)
-        tab2_s = keep.tile([P, T // 4], I32, name="tab2_s", align_bytes=64)
-        wa_w0 = keep.tile([P, PASS], I32, name="wa_w0", align_bytes=64)
-        wa_w1 = keep.tile([P, PASS], I32, name="wa_w1", align_bytes=64)
-        wb_w = keep.tile([P, R // 2], I32, name="wb_w", align_bytes=64)
-        wb_s = keep.tile([P, R // 4], I32, name="wb_s", align_bytes=64)
-        wa_s = keep.tile([P, R // 4], I32, name="wa_s", align_bytes=64)
-        en8_s = keep.tile([P, N // 4], I32, name="en8_s", align_bytes=64)
-        en4_s = keep.tile([P, N // 4], I32, name="en4_s", align_bytes=64)
-        en8_w = keep.tile([P, N], I32, name="en8_w", align_bytes=64)
-        en4_w = keep.tile([P, N // 2], I32, name="en4_w", align_bytes=64)
-        ident = keep.tile([P, P], F32, name="ident", align_bytes=64)
+        tab_w, tab2_w = sb([P, T], I32, "tab_w"), sb([P, T], I32, "tab2_w")
+        tab_s, tab2_s = sb([P, T // 4], I32, "tab_s"), sb([P, T // 4], I32, "tab2_s")
+        wa_w0, wa_w1 = sb([P, PASS], I32, "wa_w0"), sb([P, PASS], I32, "wa_w1")
+        wb_w = sb([P, R // 2], I32, "wb_w")
+        w_s = sb([P, 2 * R // 4], I32, "w_s")
+        wb_s, wa_s = w_s[:, 0 : R // 4], w_s[:, R // 4 : 2 * R // 4]
+        en8_w, en4_w = sb([P, N], I32, "en8_w"), sb([P, N // 2], I32, "en4_w")
+        en8_s, en4_s = sb([P, N // 4], I32, "en8_s"), sb([P, N // 4], I32, "en4_s")
+        ident = sb([P, P], F32, "ident")
 
         nc.gpsimd.memset(wb_s[LAST_QUADRANT:P, :], 0)
         nc.vector.memset(wa_s[LAST_QUADRANT:P, :], 0)
@@ -105,42 +99,37 @@ def tile_list_kg_gate_mix_none_kernel(tc, tab_words, tab_scales, tab2_words, tab
         nc.sync.dma_start(list1[:], offs)
         load_quadrants(nc.sync, tab_s, tab_scales, TAB_ROW, range(4))
         nc.sync.dma_start(out=tab_w[:], in_=words8(tab_words))
-        nc.sync.dma_start(out=wa_w0[:], in_=words8(wa_words)[:, 0:PASS])
         load_last_rows(nc.sync, wa_s, wa_scales)
+        nc.sync.dma_start(out=wa_w0[:], in_=words8(wa_words)[:, 0:PASS])
         nc.sync.dma_start(out=wa_w1[:], in_=words8(wa_words)[:, PASS:R])
         nc.sync.dma_start(out=en8_w[:], in_=words8(en8_words))
         nc.sync.dma_start(out=en4_w[:], in_=en4_words[0].bitcast(I32))
         load_plane(nc.sync, en8_s, en8_scales, EN8_ROW)
         load_plane(nc.sync, en4_s, en4_scales, 0)
 
-        wb_ds = keep.tile([P, PASS], U8, name="wb_ds", align_bytes=64)
-        wb_dw = keep.tile([P, 2 * PASS], U8, name="wb_dw", align_bytes=64)
-        wa_ds = keep.tile([P, PASS], U8, name="wa_ds", align_bytes=64)
-        wa_dw = keep.tile([P, PASS], I32, name="wa_dw", align_bytes=64)
+        w_ds = sb([P, 2 * PASS], U8, "w_ds")
+        wb_ds, wa_ds = w_ds[:, 0:PASS], w_ds[:, PASS : 2 * PASS]
+        wb_dw, wa_dw = sb([P, 2 * PASS], U8, "wb_dw"), sb([P, PASS], I32, "wa_dw")
 
-        def deal(dst, src):
-            nc.gpsimd.tensor_copy(out=dst, in_=src.rearrange("p (m t) -> p t m", t=4))
+        def deal_words(dst, src):
+            nc.scalar.copy(out=dst.rearrange("p (t m) -> p m t", t=4), in_=src.rearrange("p (m t) -> p m t", t=4))
 
-        def by_place(tile):
-            return tile[:].rearrange("p (t m) -> p t m", t=4)
-
-        nc.scalar.copy(out=wb_dw[:].bitcast(U16).rearrange("p (t m) -> p m t", t=4), in_=wb_w[:].bitcast(U16)[:, PASS:R].rearrange("p (m t) -> p m t", t=4))
-        deal(by_place(wb_ds), wb_s[:].bitcast(U8)[:, PASS:R])
-        deal(by_place(wa_ds), wa_s[:].bitcast(U8)[:, PASS:R])
-        deal(by_place(wa_dw), wa_w1[:])
+        deal_words(wb_dw[:].bitcast(U16), wb_w[:].bitcast(U16)[:, PASS:R])
+        deal_words(wa_dw[:].bitcast(U32), wa_w1[:].bitcast(U32))
+        nc.gpsimd.tensor_copy(out=w_ds[:].rearrange("p (w t m) -> p w t m", w=2, t=4), in_=w_s[:].bitcast(U8).rearrange("p (w b m t) -> p w b t m", w=2, b=2, t=4)[:, :, DEALT])
         nc.gpsimd.affine_select(out=ident[:], in_=ident[:], pattern=[[-1, P]], compare_op=mybir.AluOpType.is_equal, fill=0.0, base=0, channel_multiplier=1)
 
-        v_w = keep.tile([P, J], U32, name="v_w", align_bytes=64)
-        v_s = keep.tile([P, J], U8, name="v_s", align_bytes=64)
-        v2_w = keep.tile([P, J], U32, name="v2_w", align_bytes=64)
-        v2_s = keep.tile([P, J], U8, name="v2_s", align_bytes=64)
-        gate = {(c, b): keep.tile([P, PASS], F32, name="gate%d%d" % (c, b), align_bytes=64) for c in range(CHUNKS) for b in range(2)}
-        ready = {(b, c0): keep.tile([P, n * PASS], BF16, name="ready%d%d" % (b, c0), align_bytes=64) for b, c0, n in ((0, 0, 2), (0, 2, 1), (0, 3, 1), (1, 0, 2), (1, 2, 1), (1, 3, 1))}
-        unturned = {(c, b): keep.tile([P, PASS], BF16, name="unturned%d%d" % (c, b), align_bytes=64) for c in range(CHUNKS) for b in range(2) if is_turned(c, b)}
+        v_w, v2_w = sb([P, J], U32, "v_w"), sb([P, J], U32, "v2_w")
+        v_s, v2_s = sb([P, J], U8, "v_s"), sb([P, J], U8, "v2_s")
+        gate = {(c, b): sb([P, PASS], F32, "gate%d%d" % (c, b)) for c in range(CHUNKS) for b in range(2)}
+        groups = ((0, 2), (2, 3), (3, 4))
+        ready = {(b, c0): sb([P, (c1 - c0) * PASS], BF16, "ready%d%d" % (b, c0)) for b in range(2) for c0, c1 in groups}
+        unturned = [sb([P, PASS], BF16, "unturned%d" % c) for c in range(CHUNKS)]
+        ha = {}
         quantised = {}
 
         def ready_part(c, b):
-            c0 = max(first for half, first in ready if half == b and first <= c)
+            c0 = max(first for first, last in groups if first <= c)
             return ready[b, c0][:, (c - c0) * PASS : (c - c0 + 1) * PASS]
 
         def bank_tile(bank, shape):
@@ -149,19 +138,19 @@ def tile_list_kg_gate_mix_none_kernel(tc, tab_words, tab_scales, tab2_words, tab
         def gather(dst, window, lst, c0, c1):
             nc.vector.tensor_copy(dst[:, c0 * P : c1 * P], window.indirect(lst[:, c0 * LIST_COLS : c1 * LIST_COLS]))
 
-        def bank_view(bank, c, b):
-            if is_turned(c, b):
+        def bank_view(bank, b):
+            if b == TURNED:
                 return bank[:].rearrange("p (m u e) -> p u m e", u=2, e=2)
             return bank[:].rearrange("p (t j) -> p j t", t=4)
 
-        def flat_view(ap, c, b):
-            if is_turned(c, b):
+        def flat_view(ap, b):
+            if b == TURNED:
                 return ap.rearrange("p (u m e) -> p u m e", u=2, e=2)
             return ap.rearrange("p (j t) -> p j t", t=4)
 
-        def first_product(c, b, bank, cols_w, cols_s, w_words, w_scales):
+        def first_product(b, bank, cols_w, cols_s, w_words, w_scales):
             acc = bank_tile(bank, [P, PASS])
-            if is_turned(c, b):
+            if b == TURNED:
                 nc.tensor.matmul_mx(out=acc[:], lhsT=cols_w, lhsT_scale=cols_s, rhs=w_words(0, PASS), rhs_scale=w_scales[:, 0:PASS], start=True, stop=True)
             else:
                 for t in range(4):
@@ -170,59 +159,56 @@ def tile_list_kg_gate_mix_none_kernel(tc, tab_words, tab_scales, tab2_words, tab
 
         def make_gate(c, b, bank):
             cols = slice(c * P, (c + 1) * P)
-            words = wb_w[:].bitcast(U8)[:, 2 * b * PASS : 2 * (b + 1) * PASS] if is_turned(c, b) else wb_dw[:]
-            scales = wb_s[:].bitcast(U8)[:, b * PASS : (b + 1) * PASS] if is_turned(c, b) else wb_ds[:]
-            hb = first_product(c, b, bank, v2_w[:, cols].bitcast(FP8X4), v2_s[:, cols], lambda lo, hi: words[:, 2 * lo : 2 * hi].bitcast(FP4X4), scales)
-            nc.scalar.activation(out=flat_view(gate[c, b][:], c, b), in_=bank_view(hb, c, b), func=SIGMOID)
+            words = wb_w[:].bitcast(U8) if b == TURNED else wb_dw[:]
+            scales = wb_s.bitcast(U8) if b == TURNED else wb_ds
+            hb = first_product(b, bank, v2_w[:, cols].bitcast(FP8X4), v2_s[:, cols], lambda lo, hi: words[:, 2 * lo : 2 * hi].bitcast(FP4X4), scales)
+            nc.scalar.activation(out=flat_view(gate[c, b][:], b), in_=bank_view(hb, b), func=SIGMOID)
 
         def project(c, b, bank):
             cols = slice(c * P, (c + 1) * P)
-            words = (wa_w0, wa_w1)[b][:] if is_turned(c, b) else wa_dw[:]
-            scales = wa_s[:].bitcast(U8)[:, b * PASS : (b + 1) * PASS] if is_turned(c, b) else wa_ds[:]
-            return first_product(c, b, bank, v_w[:, cols].bitcast(FP8X4), v_s[TAB_ROW:P, cols], lambda lo, hi: words[:, lo:hi].bitcast(FP8X4), scales)
+            words = wa_w0[:] if b == TURNED else wa_dw[:]
+            scales = wa_s.bitcast(U8) if b == TURNED else wa_ds
+            ha[c, b] = first_product(b, bank, v_w[:, cols].bitcast(FP8X4), v_s[TAB_ROW:P, cols], lambda lo, hi: words[:, lo:hi].bitcast(FP8X4), scales)
 
         def multiply(c, b):
-            dst = unturned[c, b][:] if is_turned(c, b) else ready_part(c, b)
-            nc.vector.tensor_tensor(out=flat_view(dst, c, b), in0=flat_view(gate[c, b][:], c, b), in1=bank_view(ha[c, b], c, b), op=MULT)
+            dst = unturned[c][:] if b == TURNED else ready_part(c, b)
+            nc.vector.tensor_tensor(out=flat_view(dst, b), in0=flat_view(gate[c, b][:], b), in1=bank_view(ha[c, b], b), op=MULT)
 
-        def multiply_on_gpsimd(c, b):
-            ha_sb = keep.tile([P, PASS], F32, name="ha_sb", align_bytes=64)
-            nc.scalar.copy(out=flat_view(ha_sb[:], c, b), in_=bank_view(ha[c, b], c, b))
-            nc.gpsimd.tensor_tensor(out=unturned[c, b][:], in0=ha_sb[:], in1=gate[c, b][:], op=MULT)
+        def multiply_on_gpsimd(c):
+            ha_sb = sb([P, PASS], F32, "ha_sb")
+            nc.scalar.copy(out=flat_view(ha_sb[:], TURNED), in_=bank_view(ha[c, TURNED], TURNED))
+            nc.gpsimd.tensor_tensor(out=unturned[c][:], in0=ha_sb[:], in1=gate[c, TURNED][:], op=MULT)
 
-        def turn(c, b, bank):
+        def turn(c, bank):
             xt = bank_tile(bank, [P, 2, P])
-            pairs = unturned[c, b][:].bitcast(F32)
+            pairs = unturned[c][:].bitcast(F32)
             for u in range(2):
                 nc.tensor.transpose(xt[:, u, :], pairs[:, u * P : (u + 1) * P], ident[:])
-            nc.scalar.copy(out=ready_part(c, b).bitcast(F32).rearrange("p (j u) -> p j u", u=2), in_=xt[:].rearrange("p u j -> p j u"))
+            nc.scalar.copy(out=ready_part(c, TURNED).bitcast(F32).rearrange("p (j u) -> p j u", u=2), in_=xt[:].rearrange("p u j -> p j u"))
 
         def quantise(b, c0):
             width = ready[b, c0].shape[1] // 4
-            words = keep.tile([P, width], U32, name="hq_w%d%d" % (b, c0), align_bytes=64)
-            plane = keep.tile([P, width], U8, name="hq_s%d%d" % (b, c0), align_bytes=64)
+            words, plane = sb([P, width], U32, "hq_w%d%d" % (b, c0)), sb([P, width], U8, "hq_s%d%d" % (b, c0))
             nc.vector.quantize_mx(out=words[:].bitcast(FP8X4), scales=plane[:], in_=ready[b, c0][:])
-            for c in range(c0, c0 + width // P):
-                quantised[c, b] = (words, plane, c0)
+            quantised[b, c0] = (words, plane)
 
-        def score(dst, nt, b, c0, c1, start, stop):
-            if b == 0:
+        def score(dst, nt, b, c0, start, stop):
+            if b == TURNED:
                 en_words = en8_w[:, nt * P : (nt + 1) * P].bitcast(FP8X4)
                 en_scales = en8_s[EN8_ROW:P, :].bitcast(U8)[:, nt * P : (nt + 1) * P]
             else:
                 en_words = en4_w[:].bitcast(U8)[:, 2 * nt * P : 2 * (nt + 1) * P].bitcast(FP4X4)
                 en_scales = en4_s[:].bitcast(U8)[:, nt * P : (nt + 1) * P]
-            words, plane, first = quantised[c0, b]
-            cols = slice((c0 - first) * P, (c1 - first) * P)
-            nc.tensor.matmul_mx(out=dst, lhsT=en_words, lhsT_scale=en_scales, rhs=words[:, cols].bitcast(FP8X4), rhs_scale=plane[:, cols], start=start, stop=stop)
+            words, plane = quantised[b, c0]
+            nc.tensor.matmul_mx(out=dst, lhsT=en_words, lhsT_scale=en_scales, rhs=words[:].bitcast(FP8X4), rhs_scale=plane[:], start=start, stop=stop)
 
         def finish(c0, c1, banks, halves, copies, queues):
             y = [bank_tile(bank, [P, (c1 - c0) * P]) for bank in banks]
             for b in halves:
                 for nt in range(N_TILES):
-                    score(y[nt][:], nt, b, c0, c1, b == halves[0], b == halves[1])
+                    score(y[nt][:], nt, b, c0, b == halves[0], b == halves[1])
             for nt in range(N_TILES):
-                y_sb = keep.tile([P, (c1 - c0) * P], F32, name="y%d%d" % (c0, nt), align_bytes=64)
+                y_sb = sb([P, (c1 - c0) * P], F32, "y%d%d" % (c0, nt))
                 copies[nt](out=y_sb[:], in_=y[nt][:])
                 queues[nt].dma_start(out=out[nt * P : (nt + 1) * P, c0 * P : c1 * P], in_=y_sb[:])
 
@@ -236,37 +222,36 @@ def tile_list_kg_gate_mix_none_kernel(tc, tab_words, tab_scales, tab2_words, tab
         gather(v_w, tab_w[:].bitcast(U32), list1, 1, POOL_CHUNK)
 
         for c in range(CHUNKS):
-            make_gate(c, 0, c)
-        make_gate(0, 1, 4)
-        ha = {}
-        for c, bank in ((0, 5), (POOL_CHUNK, 6), (1, 7), (2, 0)):
-            ha[c, 0] = project(c, 0, bank)
-        multiply_on_gpsimd(POOL_CHUNK, 0)
-        ha[0, 1] = project(0, 1, 1)
+            make_gate(c, TURNED, c)
+        for c, bank in ((0, 4), (POOL_CHUNK, 5), (1, 6)):
+            project(c, TURNED, bank)
+        multiply_on_gpsimd(POOL_CHUNK)
+        make_gate(0, DEALT, 0)
+        project(2, TURNED, 7)
+        make_gate(1, DEALT, 1)
         for c in range(POOL_CHUNK):
-            multiply(c, 0)
-        multiply(0, 1)
-
-        make_gate(1, 1, 5)
-        make_gate(2, 1, 6)
-        ha[1, 1] = project(1, 1, 2)
-        ha[2, 1] = project(2, 1, 3)
-        turn(0, 0, 7)
-        turn(1, 0, 5)
-        turn(0, 1, 1)
-        make_gate(3, 1, 6)
-        ha[3, 1] = project(3, 1, 4)
-        turn(2, 0, 0)
-        turn(3, 0, 7)
-
-        multiply(1, 1)
-        multiply(2, 1)
-        for b, c0 in ((0, 0), (1, 0)):
-            quantise(b, c0)
-        multiply(3, 1)
-        finish(0, 2, (2, 5), (0, 1), (nc.scalar.copy, nc.scalar.copy), (nc.sync, nc.sync))
-        for b, c0 in ((1, 2), (0, 2), (0, 3), (1, 3)):
-            quantise(b, c0)
+            multiply(c, TURNED)
+        project(0, DEALT, 2)
+        project(1, DEALT, 3)
+        turn(0, 4)
+        turn(1, 6)
+        multiply(0, DEALT)
+        multiply(1, DEALT)
+        make_gate(2, DEALT, 0)
+        make_gate(3, DEALT, 1)
+        project(2, DEALT, 5)
+        project(3, DEALT, 7)
+        quantise(TURNED, 0)
+        quantise(DEALT, 0)
+        turn(2, 2)
+        turn(3, 3)
+        multiply(2, DEALT)
+        multiply(3, DEALT)
+        finish(0, 2, (4, 6), (TURNED, DEALT), (nc.scalar.copy, nc.scalar.copy), (nc.sync, nc.sync))
+        quantise(DEALT, 2)
+        quantise(TURNED, 2)
+        quantise(TURNED, 3)
+        quantise(DEALT, 3)
         both = (nc.vector.tensor_copy, nc.scalar.copy)
-        finish(2, 3, (3, 1), (1, 0), both, (nc.sync, nc.sync))
-        finish(3, 4, (4, 6), (0, 1), both, (nc.sync, nc.scalar))
+        finish(2, 3, (0, 5), (DEALT, TURNED), both, (nc.sync, nc.sync))
+        finish(3, 4, (1, 2), (TURNED, DEALT), both, (nc.sync, nc.scalar))

@@ -80,12 +80,13 @@ def tile_list_kg_gate_mix_none_kernel(tc, tab_words, tab_scales, tab2_words, tab
         ident = sb([P, P], F32, "ident")
 
         nc.gpsimd.memset(wb_s[LAST_QUADRANT:P, :], 0)
-        nc.vector.memset(wa_s[LAST_QUADRANT:P, :], 0)
         nc.vector.memset(tab_s[:], 0)
+        nc.vector.memset(wa_s, 0)
         nc.vector.memset(ident[:], 1.0)
 
-        load_first_rows(nc.gpsimd, wb_s, wb_scales)
-        load_first_rows(nc.gpsimd, wa_s, wa_scales)
+        for b in range(2):
+            half = slice(b * PASS // 4, (b + 1) * PASS // 4)
+            nc.gpsimd.dma_start(out=wb_s[0:SPAN, half], in_=wb_scales[0].bitcast(I32)[0:PERIOD, half].partition_broadcast(REPEATS))
         load_filled_quadrants(nc.scalar, tab2_s, tab2_scales, range(0, 2))
         load_last_rows(nc.scalar, wb_s, wb_scales)
         warm = keep.tile([P, 2], F32, name="warm")
@@ -99,7 +100,7 @@ def tile_list_kg_gate_mix_none_kernel(tc, tab_words, tab_scales, tab2_words, tab
         nc.sync.dma_start(list1[:], offs)
         load_quadrants(nc.sync, tab_s, tab_scales, TAB_ROW, range(4))
         nc.sync.dma_start(out=tab_w[:], in_=words8(tab_words))
-        load_last_rows(nc.sync, wa_s, wa_scales)
+        load_quadrants(nc.sync, wa_s, wa_scales, TAB_ROW, range(4))
         nc.sync.dma_start(out=wa_w0[:], in_=words8(wa_words)[:, 0:PASS])
         nc.sync.dma_start(out=wa_w1[:], in_=words8(wa_words)[:, PASS:R])
         nc.sync.dma_start(out=en8_w[:], in_=words8(en8_words))
@@ -167,7 +168,7 @@ def tile_list_kg_gate_mix_none_kernel(tc, tab_words, tab_scales, tab2_words, tab
         def project(c, b, bank):
             cols = slice(c * P, (c + 1) * P)
             words = wa_w0[:] if b == TURNED else wa_dw[:]
-            scales = wa_s.bitcast(U8) if b == TURNED else wa_ds
+            scales = wa_s[TAB_ROW:P, :].bitcast(U8) if b == TURNED else wa_ds[TAB_ROW:P, :]
             ha[c, b] = first_product(b, bank, v_w[:, cols].bitcast(FP8X4), v_s[TAB_ROW:P, cols], lambda lo, hi: words[:, lo:hi].bitcast(FP8X4), scales)
 
         def multiply(c, b):

@@ -100,7 +100,7 @@ def tile_list_kg_gate_mix_none_kernel(tc, tab_words, tab_scales, tab2_words, tab
         nc.sync.dma_start(list1[:], offs)
         load_quadrants(nc.sync, tab_s, tab_scales, TAB_ROW, range(4))
         nc.sync.dma_start(out=tab_w[:], in_=words8(tab_words))
-        load_quadrants(nc.sync, wa_s, wa_scales, TAB_ROW, range(4))
+        load_quadrants(nc.sync, wa_s, wa_scales, 0, range(4))
         nc.sync.dma_start(out=wa_w0[:], in_=words8(wa_words)[:, 0:PASS])
         nc.sync.dma_start(out=wa_w1[:], in_=words8(wa_words)[:, PASS:R])
         nc.sync.dma_start(out=en8_w[:], in_=words8(en8_words))
@@ -168,7 +168,7 @@ def tile_list_kg_gate_mix_none_kernel(tc, tab_words, tab_scales, tab2_words, tab
         def project(c, b, bank):
             cols = slice(c * P, (c + 1) * P)
             words = wa_w0[:] if b == TURNED else wa_dw[:]
-            scales = wa_s[TAB_ROW:P, :].bitcast(U8) if b == TURNED else wa_ds[TAB_ROW:P, :]
+            scales = wa_s.bitcast(U8) if b == TURNED else wa_ds
             ha[c, b] = first_product(b, bank, v_w[:, cols].bitcast(FP8X4), v_s[TAB_ROW:P, cols], lambda lo, hi: words[:, lo:hi].bitcast(FP8X4), scales)
 
         def multiply(c, b):

from contextlib import ExitStack

import concourse.mybir as mybir

K, L, R, N, T, J = 512, 512, 1024, 256, 1024, 512
FLOPS = 2 * J * (K * R + L * R + R * N)

F32 = mybir.dt.float32
BF16 = mybir.dt.bfloat16
I32 = mybir.dt.int32
U32 = mybir.dt.uint32
U16 = mybir.dt.uint16
U8 = mybir.dt.uint8
FP8X4 = mybir.dt.float8_e4m3fn_x4
FP4X4 = mybir.dt.float4_e2m1fn_x4
SIGMOID = mybir.ActivationFunctionType.Sigmoid
MULT = mybir.AluOpType.mult

P = 128
PASS = 512
CHUNKS = J // P
N_TILES = N // P
LIST_COLS = P // 16
TURNED, DEALT = 0, 1
POOL_CHUNK = CHUNKS - 1
TAB_ROW, EN8_ROW = 8, 12
PERIOD, REPEATS = 14, 7
SPAN = PERIOD * REPEATS
LAST_QUADRANT = 96


def load_quadrants(queue, plane, scales, first_row, quadrants):
    rows = scales[0].bitcast(I32)
    for q in quadrants:
        queue.dma_start(out=plane[32 * q + first_row : 32 * q + first_row + 4, :], in_=rows[4 * q : 4 * q + 4, :])


def load_filled_quadrants(queue, plane, scales, quadrants):
    rows = scales[0].bitcast(I32)
    for q in quadrants:
        queue.dma_start(out=plane[32 * q : 32 * q + 32, :], in_=rows[4 * q : 4 * q + 4, :].partition_broadcast(8))


def load_first_rows(queue, plane, scales, first_row=0):
    queue.dma_start(out=plane[first_row : first_row + SPAN, :], in_=scales[0].bitcast(I32)[0:PERIOD, :].partition_broadcast(REPEATS))


def load_last_rows(queue, plane, scales):
    queue.dma_start(out=plane[SPAN : SPAN + 2, :], in_=scales[0].bitcast(I32)[PERIOD:16, :])


def load_plane(queue, plane, scales, first_row):
    load_first_rows(queue, plane, scales, first_row)
    queue.dma_start(out=plane[first_row + SPAN : P, :], in_=scales[0].bitcast(I32)[PERIOD:16, :].partition_broadcast((P - SPAN - first_row) // 2))


def words8(w):
    return w[0].rearrange("p n t -> p (n t)").bitcast(I32)


def tile_list_kg_gate_mix_none_kernel(tc, tab_words, tab_scales, tab2_words, tab2_scales, wa_words, wa_scales, wb_words, wb_scales, en8_words, en8_scales, en4_words, en4_scales, offs, offs2, out):
    nc = tc.nc
    with ExitStack() as ctx:
        keep = ctx.enter_context(tc.tile_pool(name="keep", bufs=1))
        psum = ctx.enter_context(tc.psum_pool(name="psum", bufs=1))

        def sb(shape, dtype, name):
            return keep.tile(shape, dtype, name=name, align_bytes=64)

        list1 = keep.tile([P, J // 16], U16, name="list1")
        list2 = keep.tile([P, J // 16], U16, name="list2")
        tab_w, tab2_w = sb([P, T], I32, "tab_w"), sb([P, T], I32, "tab2_w")
        tab_s, tab2_s = sb([P, T // 4], I32, "tab_s"), sb([P, T // 4], I32, "tab2_s")
        wa_w0, wa_w1 = sb([P, PASS], I32, "wa_w0"), sb([P, PASS], I32, "wa_w1")
        wb_w = sb([P, R // 2], I32, "wb_w")
        w_s = sb([P, 2 * R // 4], I32, "w_s")
        wb_s, wa_s = w_s[:, 0 : R // 4], w_s[:, R // 4 : 2 * R // 4]
        en8_w, en4_w = sb([P, N], I32, "en8_w"), sb([P, N // 2], I32, "en4_w")
        en8_s, en4_s = sb([P, N // 4], I32, "en8_s"), sb([P, N // 4], I32, "en4_s")
        ident = sb([P, P], F32, "ident")

        nc.gpsimd.memset(wb_s[LAST_QUADRANT:P, :], 0)
        nc.vector.memset(tab_s[:], 0)
        nc.vector.memset(wa_s, 0)
        nc.vector.memset(ident[:], 1.0)

        for b in range(2):
            half = slice(b * PASS // 4, (b + 1) * PASS // 4)
            nc.gpsimd.dma_start(out=wb_s[0:SPAN, half], in_=wb_scales[0].bitcast(I32)[0:PERIOD, half].partition_broadcast(REPEATS))
        load_filled_quadrants(nc.scalar, tab2_s, tab2_scales, range(0, 2))
        load_last_rows(nc.scalar, wb_s, wb_scales)
        warm = keep.tile([P, 2], F32, name="warm")
        nc.vector.memset(warm[:, 0:1], 0.0)
        nc.scalar.activation(out=warm[:, 1:2], in_=warm[:, 0:1], func=SIGMOID)

        nc.sync.dma_start(list2[:], offs2)
        load_filled_quadrants(nc.sync, tab2_s, tab2_scales, range(2, 4))
        nc.sync.dma_start(out=tab2_w[:], in_=words8(tab2_words))
        nc.sync.dma_start(out=wb_w[:], in_=wb_words[0].bitcast(I32))
        nc.sync.dma_start(list1[:], offs)
        load_quadrants(nc.sync, tab_s, tab_scales, TAB_ROW, range(4))
        nc.sync.dma_start(out=tab_w[:], in_=words8(tab_words))
        load_quadrants(nc.sync, wa_s, wa_scales, 0, range(4))
        nc.sync.dma_start(out=wa_w0[:], in_=words8(wa_words)[:, 0:PASS])
        nc.sync.dma_start(out=wa_w1[:], in_=words8(wa_words)[:, PASS:R])
        nc.sync.dma_start(out=en8_w[:], in_=words8(en8_words))
        nc.sync.dma_start(out=en4_w[:], in_=en4_words[0].bitcast(I32))
        load_plane(nc.sync, en8_s, en8_scales, EN8_ROW)
        load_plane(nc.sync, en4_s, en4_scales, 0)

        w_ds = sb([P, 2 * PASS], U8, "w_ds")
        wb_ds, wa_ds = w_ds[:, 0:PASS], w_ds[:, PASS : 2 * PASS]
        wb_dw, wa_dw = sb([P, 2 * PASS], U8, "wb_dw"), sb([P, PASS], I32, "wa_dw")

        def deal_words(dst, src):
            nc.scalar.copy(out=dst.rearrange("p (t m) -> p m t", t=4), in_=src.rearrange("p (m t) -> p m t", t=4))

        deal_words(wb_dw[:].bitcast(U16), wb_w[:].bitcast(U16)[:, PASS:R])
        deal_words(wa_dw[:].bitcast(U32), wa_w1[:].bitcast(U32))
        nc.gpsimd.tensor_copy(out=w_ds[:].rearrange("p (w t m) -> p w t m", w=2, t=4), in_=w_s[:].bitcast(U8).rearrange("p (w b m t) -> p w b t m", w=2, b=2, t=4)[:, :, DEALT])
        nc.gpsimd.affine_select(out=ident[:], in_=ident[:], pattern=[[-1, P]], compare_op=mybir.AluOpType.is_equal, fill=0.0, base=0, channel_multiplier=1)

        v_w, v2_w = sb([P, J], U32, "v_w"), sb([P, J], U32, "v2_w")
        v_s, v2_s = sb([P, J], U8, "v_s"), sb([P, J], U8, "v2_s")
        gate = {(c, b): sb([P, PASS], F32, "gate%d%d" % (c, b)) for c in range(CHUNKS) for b in range(2)}
        groups = ((0, 2), (2, 3), (3, 4))
        ready = {(b, c0): sb([P, (c1 - c0) * PASS], BF16, "ready%d%d" % (b, c0)) for b in range(2) for c0, c1 in groups}
        unturned = [sb([P, PASS], BF16, "unturned%d" % c) for c in range(CHUNKS)]
        ha = {}
        quantised = {}

        def ready_part(c, b):
            c0 = max(first for first, last in groups if first <= c)
            return ready[b, c0][:, (c - c0) * PASS : (c - c0 + 1) * PASS]

        def bank_tile(bank, shape):
            return psum.tile(shape, F32, name="bank%d" % bank)

        def gather(dst, window, lst, c0, c1):
            nc.vector.tensor_copy(dst[:, c0 * P : c1 * P], window.indirect(lst[:, c0 * LIST_COLS : c1 * LIST_COLS]))

        def bank_view(bank, b):
            if b == TURNED:
                return bank[:].rearrange("p (m u e) -> p u m e", u=2, e=2)
            return bank[:].rearrange("p (t j) -> p j t", t=4)

        def flat_view(ap, b):
            if b == TURNED:
                return ap.rearrange("p (u m e) -> p u m e", u=2, e=2)
            return ap.rearrange("p (j t) -> p j t", t=4)

        def first_product(b, bank, cols_w, cols_s, w_words, w_scales):
            acc = bank_tile(bank, [P, PASS])
            if b == TURNED:
                nc.tensor.matmul_mx(out=acc[:], lhsT=cols_w, lhsT_scale=cols_s, rhs=w_words(0, PASS), rhs_scale=w_scales[:, 0:PASS], start=True, stop=True)
            else:
                for t in range(4):
                    nc.tensor.matmul_mx(out=acc[:, t * P : (t + 1) * P], lhsT=w_words(t * P, (t + 1) * P), lhsT_scale=w_scales[:, t * P : (t + 1) * P], rhs=cols_w, rhs_scale=cols_s, start=True, stop=True)
            return acc

        def make_gate(c, b, bank):
            cols = slice(c * P, (c + 1) * P)
            words = wb_w[:].bitcast(U8) if b == TURNED else wb_dw[:]
            scales = wb_s.bitcast(U8) if b == TURNED else wb_ds
            hb = first_product(b, bank, v2_w[:, cols].bitcast(FP8X4), v2_s[:, cols], lambda lo, hi: words[:, 2 * lo : 2 * hi].bitcast(FP4X4), scales)
            nc.scalar.activation(out=flat_view(gate[c, b][:], b), in_=bank_view(hb, b), func=SIGMOID)

        def project(c, b, bank):
            cols = slice(c * P, (c + 1) * P)
            words = wa_w0[:] if b == TURNED else wa_dw[:]
            scales = wa_s.bitcast(U8) if b == TURNED else wa_ds
            ha[c, b] = first_product(b, bank, v_w[:, cols].bitcast(FP8X4), v_s[TAB_ROW:P, cols], lambda lo, hi: words[:, lo:hi].bitcast(FP8X4), scales)

        def multiply(c, b):
            dst = unturned[c][:] if b == TURNED else ready_part(c, b)
            nc.vector.tensor_tensor(out=flat_view(dst, b), in0=flat_view(gate[c, b][:], b), in1=bank_view(ha[c, b], b), op=MULT)

        def multiply_on_gpsimd(c):
            ha_sb = sb([P, PASS], F32, "ha_sb")
            nc.scalar.copy(out=flat_view(ha_sb[:], TURNED), in_=bank_view(ha[c, TURNED], TURNED))
            nc.gpsimd.tensor_tensor(out=unturned[c][:], in0=ha_sb[:], in1=gate[c, TURNED][:], op=MULT)

        def turn(c, bank):
            xt = bank_tile(bank, [P, 2, P])
            pairs = unturned[c][:].bitcast(F32)
            for u in range(2):
                nc.tensor.transpose(xt[:, u, :], pairs[:, u * P : (u + 1) * P], ident[:])
            nc.scalar.copy(out=ready_part(c, TURNED).bitcast(F32).rearrange("p (j u) -> p j u", u=2), in_=xt[:].rearrange("p u j -> p j u"))

        def quantise(b, c0):
            width = ready[b, c0].shape[1] // 4
            words, plane = sb([P, width], U32, "hq_w%d%d" % (b, c0)), sb([P, width], U8, "hq_s%d%d" % (b, c0))
            nc.vector.quantize_mx(out=words[:].bitcast(FP8X4), scales=plane[:], in_=ready[b, c0][:])
            quantised[b, c0] = (words, plane)

        def score(dst, nt, b, c0, start, stop):
            if b == TURNED:
                en_words = en8_w[:, nt * P : (nt + 1) * P].bitcast(FP8X4)
                en_scales = en8_s[EN8_ROW:P, :].bitcast(U8)[:, nt * P : (nt + 1) * P]
            else:
                en_words = en4_w[:].bitcast(U8)[:, 2 * nt * P : 2 * (nt + 1) * P].bitcast(FP4X4)
                en_scales = en4_s[:].bitcast(U8)[:, nt * P : (nt + 1) * P]
            words, plane = quantised[b, c0]
            nc.tensor.matmul_mx(out=dst, lhsT=en_words, lhsT_scale=en_scales, rhs=words[:].bitcast(FP8X4), rhs_scale=plane[:], start=start, stop=stop)

        def finish(c0, c1, banks, halves, copies, queues):
            y = [bank_tile(bank, [P, (c1 - c0) * P]) for bank in banks]
            for b in halves:
                for nt in range(N_TILES):
                    score(y[nt][:], nt, b, c0, b == halves[0], b == halves[1])
            for nt in range(N_TILES):
                y_sb = sb([P, (c1 - c0) * P], F32, "y%d%d" % (c0, nt))
                copies[nt](out=y_sb[:], in_=y[nt][:])
                queues[nt].dma_start(out=out[nt * P : (nt + 1) * P, c0 * P : c1 * P], in_=y_sb[:])

        gather(v2_s, tab2_s[:].bitcast(U8), list2, 0, CHUNKS)
        gather(v2_w, tab2_w[:].bitcast(U32), list2, 0, 1)
        gather(v2_w, tab2_w[:].bitcast(U32), list2, 1, 2)
        gather(v2_w, tab2_w[:].bitcast(U32), list2, 2, CHUNKS)
        gather(v_s, tab_s[:].bitcast(U8), list1, 0, CHUNKS)
        gather(v_w, tab_w[:].bitcast(U32), list1, 0, 1)
        gather(v_w, tab_w[:].bitcast(U32), list1, POOL_CHUNK, CHUNKS)
        gather(v_w, tab_w[:].bitcast(U32), list1, 1, POOL_CHUNK)

        for c in range(CHUNKS):
            make_gate(c, TURNED, c)
        for c, bank in ((0, 4), (POOL_CHUNK, 5), (1, 6)):
            project(c, TURNED, bank)
        multiply_on_gpsimd(POOL_CHUNK)
        make_gate(0, DEALT, 0)
        project(2, TURNED, 7)
        make_gate(1, DEALT, 1)
        for c in range(POOL_CHUNK):
            multiply(c, TURNED)
        project(0, DEALT, 2)
        project(1, DEALT, 3)
        turn(0, 4)
        turn(1, 6)
        multiply(0, DEALT)
        multiply(1, DEALT)
        make_gate(2, DEALT, 0)
        make_gate(3, DEALT, 1)
        project(2, DEALT, 5)
        project(3, DEALT, 7)
        quantise(TURNED, 0)
        quantise(DEALT, 0)
        turn(2, 2)
        turn(3, 3)
        multiply(2, DEALT)
        multiply(3, DEALT)
        finish(0, 2, (4, 6), (TURNED, DEALT), (nc.scalar.copy, nc.scalar.copy), (nc.sync, nc.sync))
        quantise(DEALT, 2)
        quantise(TURNED, 2)
        quantise(TURNED, 3)
        quantise(DEALT, 3)
        both = (nc.vector.tensor_copy, nc.scalar.copy)
        finish(2, 3, (0, 5), (DEALT, TURNED), both, (nc.sync, nc.sync))
        finish(3, 4, (1, 2), (TURNED, DEALT), both, (nc.sync, nc.scalar))
